import numpy as np, ml_dtypes
CORES = [51,54,179,182]
N = 4
BF = ml_dtypes.bfloat16
def gentries(a):
    return np.ascontiguousarray(a.reshape(8, 16, -1).transpose(0, 2, 1)).reshape(8, -1)
def gtable(e):
    e = np.asarray(e); return np.ascontiguousarray(e.reshape(8, -1, 16).transpose(0, 2, 1)).reshape(128, -1).astype(np.int32)
S, B, D, T, J, L = 4096, 1024, 9, 4, 101, 2048
REC = np.array([0, 256, 128, 85, 64, 51, 42, 36, 32, 28], np.int64)
def sums(rng, tot, lo, hi, n):
    x = rng.integers(lo, hi + 1, n); e = int(tot - np.sum(x))
    room = np.repeat(np.arange(n), hi - x if e > 0 else x - lo)
    np.add.at(x, rng.permutation(room)[:abs(e)], 1 if e > 0 else -1)
    return x
def durs(rng):
    x = rng.integers(1, D + 1, (N, 8, B))
    for q in range(N):
        for g in range(8): x[q, g, :B - 1] = sums(rng, int(rng.integers(S // 8 * 7, S // 2 * 3 + 1)), 1, D, B - 1)
    return x
def gains(rng, e):
    return (1.0 + rng.random((N, 128, T))) * np.exp2(rng.integers(-e, 1, (N, 128, T))) * rng.choice(np.array([-1.0, 1.0]), (N, 128, T))
def pack(A, v, x, m, u):
    return {"am": np.ascontiguousarray(A.reshape(N, 128, B)).astype(np.float32).astype(BF), "ve": np.ascontiguousarray(v.reshape(N, 128, B)).astype(np.float32).astype(BF),
            "du": np.stack([gtable(a) for a in x]), "mp": np.stack([gtable(a) for a in m]), "gain": u.astype(np.float32)}
def setup_inputs(rng):
    return pack(rng.integers(-256, 257, (N, 8, 16, B)), rng.integers(-64, 65, (N, 8, 16, B)), durs(rng), rng.integers(0, B, (N, 8, B)), gains(rng, 1))
def setup_inputs_spread(rng):
    A = rng.integers(-256, 257, (N, 8, 16, B)) >> rng.integers(0, 2, (N, 8, 1, B)); v = rng.integers(-64, 65, (N, 8, 16, B)) >> rng.integers(0, 5, (N, 8, 1, B))
    x = durs(rng); x[:, 1::4] = np.sort(x[:, 1::4], axis=2); x[:, 2::4] = np.sort(x[:, 2::4], axis=2)[..., ::-1]
    m = np.minimum((B * rng.random((N, 8, B)) ** 3).astype(np.int64), B - 1)
    return pack(A, v, x, m, gains(rng, 0) * np.exp2(rng.integers(-1, 1, (N, 1, T))))
def setup_inputs_ends(rng):
    A = 256 * rng.choice(np.array([-1, 1]), (N, 8, 16, B)); one = 256 * rng.choice(np.array([-1, 1]), (N, 8, 1, B))
    for g in (0, 1, 4, 5): A[:, g] = one[:, g]
    for q in range(N):
        for g in (1, 5):
            i = int(rng.integers(0, 16)); A[q, g, i] = -A[q, g, i]
    A[:, 7, :, B - 1] = 256; A[:, 6, :, B - 1] = -256
    v = 64 * rng.choice(np.array([-1, 1]), (N, 8, 16, B))
    x = np.where(rng.random((N, 8, B)) < rng.choice(np.array([0.3, 0.5, 0.7]), (N, 8, 1)), D, 1)
    for q in range(N): x[q, (q + 8 - N) % 8] = D; x[q, (q + 11 - N) % 8] = 1
    return pack(A, v, x, (B - 1) * rng.integers(0, 2, (N, 8, B)), gains(rng, 1))
def setup_inputs_corners(rng):
    A = rng.integers(-256, 257, (N, 8, 16, B)); v = rng.choice(np.array([-64, -63, -1, 0, 0, 1, 63, 64]), (N, 8, 16, B))
    c = rng.integers(64, 257, 16) * rng.choice(np.array([-1, 1]), 16)
    for i in (0, 15): A[:, :, i] = c[i]; v[:, :, i] = 0
    x = rng.choice(np.array([1, D]), (N, 8, B)); m = rng.integers(0, B, (N, 8, B)); last = (S - 1, S, S + 1, S - 2, B - 1, D * (B - 1), S, S - 1)
    for q in range(N):
        for g in range(8):
            x[q, g, :B - 1] = sums(rng, last[(q + g) % 8], 1, D, B - 1); w = (q + 3 * g) % 4
            if w == 0: m[q, g] = np.arange(B)
            elif w == 1: m[q, g] = 0
            elif w == 2: m[q, g] = B - 1
    return pack(A, v, x, m, gains(rng, 0))
def setup_inputs_crowd(rng):
    mid = rng.integers(24, 49, (N, 8, 16)) * rng.choice(np.array([-1, 1]), (N, 8, 16))
    A = np.repeat(mid[..., None], B, axis=3); v = rng.integers(-3, 4, (N, 8, 16, B)); x = rng.integers(1, 4, (N, 8, B)); m = rng.integers(0, B, (N, 8, B))
    for q in range(N):
        for g in range(8):
            if g % 2 == 0:
                n = int(rng.choice(np.array([0, 1, 7, 8, 9, 15, 16])))
                if q == 0: n = (8, 9, 16, 0)[g // 2]
                if q == 1: n = (15, 7, 9, 8)[g // 2]
                o = rng.permutation(16); A[q, g] = rng.integers(112, 257, (16, B)); A[q, g, o[:n]] = -rng.integers(112, 257, (n, B))
                if n < 16: A[q, g, o[n]] = mid[(q + 1) % N, g + 1, o[n]]
            if (q + g // 2) % 2 == 1: x[q, g] = rng.integers(D - 2, D + 1, B)
            w = (q + g) % 4; a = int(rng.integers(0, B))
            if w < 2: m[q, g] = a
            if w == 1: m[q, g, int(rng.integers(0, B))] = (a + 1) % B
            if w == 2: m[q, g] = rng.choice(np.array([0, a, B - 1]), B)
    return pack(A, v, x, m, gains(rng, 0))
def setup_inputs_calm(rng):
    A = rng.integers(14, 27, (N, 8, 16, B)) * rng.choice(np.array([-1, 1]), (N, 8, 16, B)); A[:, ::2] = -rng.integers(32, 65, (N, 4, 16, B))
    A[:, 1::2, 3::4] = rng.integers(6, 9, (N, 4, 4, B)) * rng.choice(np.array([-1, 1]), (N, 4, 4, B)); A[:, ::2, 3::4] = -rng.integers(10, 14, (N, 4, 4, B))
    A[:, ::2, 11::4] = 2 + ((np.arange(B) + rng.integers(0, 2, (N, 4, 2, 1))) & 1)
    A[:, 1::2, 11::4] = 4 + ((np.arange(B) + rng.integers(0, 2, (N, 4, 2, 1))) & 1)
    v = rng.integers(0, 4, (N, 8, 16, B)); v[:, :, 3::4] = 0
    g0 = 2 * int(rng.integers(0, 4)); g1 = 2 * int(rng.integers(0, 4))
    two = rng.permutation(np.array([1, 2, 4, 5, 6, 9, 10, 12, 13, 14])); i0 = int(two[0]); i1 = int(two[1])
    A[:, g0, i0] = -256; A[:, g0 + 1, i0] = 256
    A[:, g1, i1] = -rng.integers(240, 257, (N, B)); A[:, g1 + 1, i1] = rng.integers(240, 257, (N, B))
    x = rng.integers(1, 5, (N, 8, B))
    for q in range(N):
        for g in range(0, 8, 2): x[q, g] = rng.integers(1, D, B); x[q, g, :B - 1] = sums(rng, S - 1 - (B - 1) + (0, 1, 2, -1)[(q + g // 2) % 4], 1, D - 1, B - 1)
    m = rng.integers(0, B, (N, 8, B))
    u = gains(rng, 0); u = np.sign(u) * (0.875 + 0.125 * np.abs(u))
    row = np.arange(128); full = (row % 8 == 0) | (row % 4 == 3); least = (row % 16 == 11) | (row % 16 == 15)
    low = np.zeros(128, bool); low[[16 * ((g0 + 7) % 8) + i0, 16 * g0 + i0, 16 * (g0 + 1) + i0]] = True
    near = np.zeros(128, bool); near[[16 * ((g1 + 7) % 8) + i1, 16 * (g1 + 1) + i1]] = True
    big = row == 16 * g1 + i1
    rest = ~(full | low | near | big)
    u[:, full] = 2.0 * np.sign(u[:, full]); u[:, least] = 2.5 * np.sign(u[:, least])
    u[:, low] = rng.choice(np.array([-1.0, 1.0]), (N, 3, 1)) * (0.125 + (rng.integers(0, 256, (N, 3, T)) + 0.47) * 2.0 ** -17)
    u[:, near] = 0.125 * np.sign(u[:, near])
    u[:, big] = rng.choice(np.array([-2.5, 2.5]), (N, 1, 1)) * np.where(np.arange(T) == 0, 1.0, -1.0 / (T - 1))
    y = np.mean(reference(**pack(A, v, x, m, u))["yo"].astype(np.float64) ** 2, axis=2)
    aim = (2.0 * T * (S // L) / 72.0) ** 2
    have = np.sum(y[:, ~rest], axis=1) / 128.0; more = np.sum(y[:, rest], axis=1) / 128.0
    c = np.clip(np.sqrt(np.maximum(aim - have, 0.0) / more), 0.125, 2.2)
    u[:, rest] = u[:, rest] * c[:, None, None]
    return pack(A, v, x, m, u)
def check_ranges(d):
    bad = []
    for k, lo, hi in (("am", -256, 256), ("ve", -64, 64), ("du", 1, D), ("mp", 0, B - 1)):
        a = np.asarray(d[k]).astype(np.float64)
        if not (np.min(a) >= lo and np.max(a) <= hi) or np.any(a != np.floor(a)): bad.append("range of " + k)
    u = np.abs(np.asarray(d["gain"]).astype(np.float64))
    if not np.all((u >= 0.125) & (u <= 2.5)): bad.append("range of gain")
    return bad
def reference(am, ve, du, mp, gain):
    A = am.astype(np.float32).astype(np.int64).reshape(N, 8, 16, B); v = ve.astype(np.float32).astype(np.int64).reshape(N, 8, 16, B)
    d = np.stack([gentries(a) for a in du]).astype(np.int64); m = np.stack([gentries(a) for a in mp]).astype(np.int64)
    u = gain.astype(np.float64).reshape(N, 8, 16, T); out = np.zeros((N, 8, 16, L)); n = np.arange(S)
    for t in range(T):
        O = np.add.accumulate(d, axis=2) - d
        seg, ks, ys = [], [], []
        for q in range(N):
            b = np.stack([np.searchsorted(O[q, g], n, side="right") - 1 for g in range(8)])
            k = n - np.take_along_axis(O[q], b, 1)
            w = np.minimum(k * np.take_along_axis(REC[d[q]], b, 1), 256)
            dif = np.roll(A[q], -1, axis=2) - A[q]
            ys.append(256 * np.take_along_axis(A[q], b[:, None, :], 2) + np.take_along_axis(dif, b[:, None, :], 2) * w[:, None, :])
            seg.append(b); ks.append(k)
        A2, v2, d2 = [], [], []
        for r in range(N):
            q = (r + 1 + t % (N - 1)) % N
            X = np.roll(ys[q], -1, axis=0); P = np.roll(O[q], -1, axis=0)
            at = (np.take_along_axis(np.take_along_axis(P, m[r], 1), seg[r], 1) + J * ks[r]) & (S - 1)
            z = (ys[r] * np.take_along_axis(X, at[:, None, :], 2)) * 2.0 ** -30
            out[r] += u[r, :, :, t][:, :, None] * np.add.reduce(np.tanh(z).reshape(8, 16, S // L, L), axis=2)
            if t < T - 1:
                s = np.take_along_axis(X, np.minimum(O[r], S - 1)[:, None, :], 2)
                up = np.add.reduce((s > 256 * A[r]).astype(np.int64), axis=1) >= 9; live = O[r] < S
                nd = np.where(up, np.where(d[r] == D, D - 1, d[r] + 1), np.where(d[r] == 1, 2, d[r] - 1))
                nv = np.clip(v[r] + (s >> 12), -64, 64); na = A[r] + nv
                na = np.where(na > 256, 512 - na, na); na = np.where(na < -256, -512 - na, na)
                d2.append(np.where(live, nd, d[r])); v2.append(np.where(live[:, None, :], nv, v[r])); A2.append(np.where(live[:, None, :], na, A[r]))
        if t < T - 1: A, v, d = np.stack(A2), np.stack(v2), np.stack(d2)
    return {"yo": out.reshape(N, 128, L).astype(np.float32)}

def check_inputs(d):
    bad = list(check_ranges(d))
    if not bad:
        for name, y in reference(**d).items():
            for q in range(N):
                v = np.abs(np.asarray(y[q], np.float64)); s = np.sqrt(np.mean(v * v))
                if v.max() > 12 * s or s < 2.0 ** -3: bad.append('%s of rank %d is uneven or too small' % (name, q))
    return bad

@@ -1,0 +1,837 @@
+from concourse.bass import DstId, RemoteDMATransfer
+from concourse.mybir import AluOpType, ActivationFunctionType
+
+ALU = AluOpType
+ACT = ActivationFunctionType
+S, B, NB, L = 4096, 1024, 4, 2048
+WIN = 9232
+K = 1032
+EB, FB = 140, 150
+
+SCRATCH = {
+    "X0": ("sbuf", [128, 4104], "float32"), "X1": ("sbuf", [128, 4104], "float32"), "X2": ("sbuf", [128, 4104], "float32"),
+    "Y": ("sbuf", [128, 4096], "float32"), "Z0": ("sbuf", [128, 4096], "float32"), "Z1": ("sbuf", [128, 4096], "float32"),
+    "dlt": ("sbuf", [128, 3072], "float32"), "tab": ("sbuf", [128, 2064], "float32"),
+    "winF": ("sbuf", [128, WIN], "bfloat16"), "winE": ("sbuf", [128, WIN], "bfloat16"),
+    "Aa": ("sbuf", [128, 1040], "bfloat16"), "Ar": ("sbuf", [128, 1024], "bfloat16"), "uw": ("sbuf", [128, 1040], "bfloat16"),
+    "Fb": ("sbuf", [128, 1024], "bfloat16"), "vL": ("sbuf", [128, 1024], "bfloat16"), "gg": ("sbuf", [128, 1024], "bfloat16"),
+    "ov": ("sbuf", [128, 1024], "bfloat16"), "un": ("sbuf", [128, 1024], "bfloat16"), "cmpb": ("sbuf", [128, 1024], "bfloat16"),
+    "RE": ("sbuf", [128, 2048], "bfloat16"), "srcE": ("sbuf", [128, 1024], "bfloat16"), "Dg": ("sbuf", [128, 1024], "bfloat16"),
+    "srcF": ("sbuf", [128, 1040], "bfloat16"), "zb": ("sbuf", [128, 1024], "bfloat16"), "c101": ("sbuf", [128, 256], "bfloat16"),
+    "Pwin": ("sbuf", [128, 1024], "bfloat16"), "pd": ("sbuf", [128, 512], "bfloat16"), "pl": ("sbuf", [128, 512], "bfloat16"),
+    "dui": ("sbuf", [128, 64], "int32"), "mpi": ("sbuf", [128, 64], "int32"), "gn": ("sbuf", [128, 4], "float32"),
+    "ia": ("sbuf", [128, 256], "int32"), "ib": ("sbuf", [128, 256], "int32"),
+    "dh": ("sbuf", [128, 68], "float32"), "up": ("sbuf", [128, 68], "float32"), "dn": ("sbuf", [128, 68], "float32"),
+    "Dh": ("sbuf", [128, 68], "float32"), "thr": ("sbuf", [128, 64], "float32"),
+    "t1": ("sbuf", [128, 64], "float32"), "t2": ("sbuf", [128, 64], "float32"), "t3": ("sbuf", [128, 64], "float32"),
+    "od": ("sbuf", [128, 128], "float32"), "lv": ("sbuf", [128, 64], "float32"), "bi": ("sbuf", [128, 64], "float32"),
+    "of0": ("sbuf", [128, 66], "uint16"), "dls": ("sbuf", [128, 128], "uint16"), "eof": ("sbuf", [128, 64], "uint16"),
+    "sof": ("sbuf", [128, 64], "uint16"), "jl": ("sbuf", [128, 64], "uint16"), "idx": ("sbuf", [128, 256], "uint16"),
+    "el0": ("sbuf", [128, 256], "uint16"), "el1": ("sbuf", [128, 256], "uint16"), "ml": ("sbuf", [128, 256], "uint16"),
+    "H": ("sbuf", [128, 264], "bfloat16"), "HE": ("sbuf", [128, 260], "float32"),
+    "coef": ("sbuf", [128, 160], "float32"), "dtab": ("sbuf", [128, 16], "float32"), "sm": ("sbuf", [128, 64], "float32"),
+    "smi": ("sbuf", [128, 16], "int32"),
+    "two": ("sbuf", [128, 128], "float32"), "one": ("sbuf", [128, 128], "float32"), "B2": ("sbuf", [128, 128], "float32"),
+    "U1": ("sbuf", [128, 144], "float32"), "U2": ("sbuf", [128, 144], "float32"),
+    "Wf": ("sbuf", [128, 256], "float32"), "Wb": ("sbuf", [128, 256], "bfloat16"),
+    "nW": ("sbuf", [128, 256], "bfloat16"), "p2": ("sbuf", [128, 128], "bfloat16"), "n2": ("sbuf", [128, 128], "bfloat16"),
+    "KI": ("sbuf", [128, 128], "bfloat16"), "M1": ("sbuf", [128, 128], "bfloat16"), "M2": ("sbuf", [128, 128], "bfloat16"),
+    "Tle": ("sbuf", [128, 128], "float32"), "Tgt": ("sbuf", [128, 128], "float32"), "M2f": ("sbuf", [128, 128], "float32"),
+    "Sw": ("sbuf", [128, 144], "bfloat16"), "SE": ("sbuf", [128, 144], "bfloat16"), "Vw": ("sbuf", [128, 144], "bfloat16"),
+    "Gm": ("sbuf", [128, 512], "float32"),
+    "acc0": ("psum", [128, 512], "float32"), "acc1": ("psum", [128, 512], "float32"),
+    "acc2": ("psum", [128, 512], "float32"), "acc3": ("psum", [128, 512], "float32"),
+    "P0": ("psum", [128, 512], "float32"), "P1": ("psum", [128, 512], "float32"),
+    "P2": ("psum", [128, 512], "float32"), "P3": ("psum", [128, 512], "float32"),
+}
+NQ = 90
+SEMAPHORES = (["cV", "cS", "cP", "cG"] + ["q%d" % i for i in range(NQ)]
+              + ["xa%d" % t for t in range(NB)] + ["pa%d" % t for t in range(NB)]
+              + ["xl%d" % t for t in range(NB)] + ["pl%d" % t for t in range(NB)]
+              + ["h%d" % i for i in range(3 * NB)] + ["hl"])
+SIM_CORES = 256
+STOP = ["X0", "X1", "X2", "Y"]
+
+
+def bits(m):
+    return bin(m).count("1")
+
+
+def route(T, topo, r, t):
+    n = len(T.cores)
+    src = T.cores[r]
+    dst = T.cores[(r - 1 - t % (n - 1)) % n]
+    if dst in topo.cores_of(src):
+        return src, dst, None, None
+    near = [c for c in topo.cores_of(src) if T.rank_of(c) is None and topo.die(c) == topo.die(dst) and topo.may_write(c, dst)][0]
+    far = None
+    if topo.die(near) == topo.die(src):
+        far = [c for c in range(SIM_CORES) if topo.mates(c, dst) and topo.die(c) == topo.die(src)
+               and topo.may_write(src, c) and topo.may_write(c, dst)][0]
+    return src, dst, near, far
+
+
+def pieces(T, topo, r, t):
+    src, dst, near, far = route(T, topo, r, t)
+    m = topo.mask(src, dst)
+    if near is None:
+        return [[(0, 128, None, m, 0)]] + [[(1024 * c, 1024 * c + 1024, None, m, 0)] for c in range(4)]
+    nm = topo.mask(src, near) & ~m
+    fm = m if far is None else topo.mask(src, far)
+    return [[(0, 64, near, nm, 0), (64, 128, far, fm, 0)], [(0, 1024, far, fm, 1)], [(1024, 2048, near, nm, 1)],
+            [(2048, 2560, near, nm, 2), (2560, 3072, None, m, 0)], [(3072, 4096, None, m, 0)]]
+
+
+def arrivals(T, topo, r, t, first, last):
+    src, dst, near, far = route(T, topo, r, t)
+    return sum(bits(m if h is None else topo.mask(h, dst)) for call in pieces(T, topo, r, t)[first:last] for a, b, h, m, k in call)
+
+
+def helper_program(g, core, T, topo):
+    sent = 0
+    for t in range(NB):
+        for r in range(len(T.cores)):
+            src, dst, near, far = route(T, topo, r, t)
+            if core not in (near, far):
+                continue
+            out = topo.mask(core, dst)
+            rid, pid = topo.addr(dst, core)
+            for j, call in enumerate(pieces(T, topo, r, t)):
+                for a, b, h, m, k in call:
+                    if h != core:
+                        continue
+                    g.wait_ge(T.sem["h%d" % (3 * t + k)], bits(m))
+                    if j == 0:
+                        ap = T.pl[:, 128 * t + a:128 * t + b]
+                        g.remote_dma(ap, ap, T.sem["pa%d" % t], T.sem.hl, pid, rid, out)
+                    else:
+                        g.remote_dma(T["X%d" % (t % 3)][:, a:b], T[STOP[t]][:, a:b], T.sem["xa%d" % t], T.sem.hl, pid, rid, out)
+                    sent += bits(out)
+    if sent:
+        g.wait_ge(T.sem.hl, sent)
+
+
+def rank_program(g, core, T, topo):
+    rank = T.rank_of(core)
+    if rank is None:
+        helper_program(g, core, T, topo)
+        return
+    n = len(T.cores)
+    eng = {"V": g.vector, "S": g.scalar, "P": g.tensor, "G": g, "Y": g.sync}
+    cnt = {"V": 0, "S": 0, "P": 0, "G": 0}
+    known = {q: {} for q in eng}
+    lastw, readers = {}, {}
+    nq = [0]
+    dcount = {}
+    banks = ("P0", "P1", "P2", "P3", "acc0", "acc1", "acc2", "acc3")
+
+    def wait(q, tok):
+        s, v = tok
+        if known[q].get(s, 0) < v:
+            eng[q].wait_ge(T.sem[s], v)
+            known[q][s] = v
+
+    def before(q, r, w, skip=None):
+        toks = []
+        for k in r:
+            if k in lastw:
+                toks.append(lastw[k])
+        for k in w:
+            if k in lastw:
+                toks.append(lastw[k])
+            toks.extend(readers.get(k, []))
+        best = {}
+        for s, v in toks:
+            if s != skip:
+                best[s] = max(best.get(s, 0), v)
+        for s in best:
+            wait(q, (s, best[s]))
+
+    def after(tok, r, w):
+        for k in r:
+            readers.setdefault(k, []).append(tok)
+        for k in w:
+            lastw[k] = tok
+            readers[k] = []
+
+    def op(q, fn, r, w):
+        for k in r:
+            if k in banks:
+                for tok in readers.get(k, []):
+                    if tok[0] != "c" + q:
+                        wait(q, tok)
+        before(q, r, w)
+        cnt[q] += 1
+        fn().then_inc(T.sem["c" + q], 1)
+        after(("c" + q, cnt[q]), r, w)
+
+    def mm(calls, r, w):
+        before("P", r, w, skip="cP")
+        ins = None
+        for o, a, b, st, sp in calls:
+            ins = g.tensor.matmul(o, a, b, st, sp)
+        cnt["P"] += 1
+        ins.then_inc(T.sem.cP, 1)
+        after(("cP", cnt["P"]), r, w)
+
+    def dma(q, pairs, r, w, **kw):
+        before(q, r, w)
+        s = "q%d" % nq[0]
+        nq[0] += 1
+        for o, i in pairs:
+            eng[q].dma_start(o, i, **kw).then_inc(T.sem[s], 16)
+        dcount[s] = 16 * len(pairs)
+        after((s, dcount[s]), r, w)
+
+    def ts(o, i, s1, s2, o0, o1, r, w):
+        if s2 is None:
+            op("V", lambda: g.vector.tensor_scalar(o, i, s1, None, o0), r, w)
+        else:
+            op("V", lambda: g.vector.tensor_scalar(o, i, s1, s2, o0, o1), r, w)
+
+    def tt(o, a, b, o0, r, w):
+        op("V", lambda: g.vector.tensor_tensor(o, a, b, o0), r, w)
+
+    def cp(o, i, r, w):
+        op("V", lambda: g.vector.tensor_copy(o, i), r, w)
+
+    def ms(o, c, w):
+        op("V", lambda: g.vector.memset(o, c), [], w)
+
+    def scan(o, a, b, init, r, w):
+        op("V", lambda: g.vector.tensor_tensor_scan(o, a, b, init, ALU.add, ALU.add), r, w)
+
+    def act(o, i, f, r, w, bias=0.0, scale=1.0):
+        op("S", lambda: g.scalar.activation(o, i, f, bias=bias, scale=scale), r, w)
+
+    def sel(o, i, pat, cmp, fill, base, cm, r, w):
+        op("G", lambda: g.affine_select(o, i, pat, cmp, fill, base, cm), r, w)
+
+    def iota(o, pat, base, cm, w, f=True):
+        if f:
+            op("G", lambda: g.iota(o, pat, base, cm, allow_small_or_imprecise_dtypes=True), [], w)
+        else:
+            op("G", lambda: g.iota(o, pat, base, cm), [], w)
+
+    Ib = T.Wb[:, 0:128]
+    rotb = T.Wb[:, 112:240]
+    rotf = T.Wf[:, 112:240]
+    hs = [(0, 512), (512, 1024)]
+    ab = [2, 0]
+    Zs = [T.Z0, T.Z1, T.Z0, T.X1]
+    zk = ["Z0_%d", "Z1_%d", "Z0_%d", "Z3_%d"]
+    Xs = [T.X0, T.X1, T.X2]
+    els = [T.el0, T.el1]
+    Pb = [T.P0, T.P1, T.P2, T.P3]
+
+    dma("Y", [(T.dui[:], T.du[:])], [], ["dui"])
+    dma("S", [(T.Aa[:, 0:1024], T.am[:])], [], ["Aa0", "Aa1"])
+    iota(T.dtab[:], [[1, 16]], 0, 0, ["dtab"])
+    iota(T.smi[:, 0:1], [[1, 1]], 0, 1, ["smi0"], f=False)
+    ms(T.two[:], 2.0, ["two"])
+    ms(T.winF[:, 0:B], 0.0, ["winFa"])
+    dma("Y", [(T.winF[:, B * j:B * j + B], T.winF[:, 0:B]) for j in range(1, 4)], ["winFa"], ["winF"])
+    dma("Y", [(T.mpi[:], T.mp[:]), (T.gn[:], T.gain[:]), (T.uw[16:128, 16:1040], T.ve[0:112, :]), (T.uw[0:16, 16:1040], T.ve[112:128, :])],
+        [], ["mpi", "gn", "uw0", "uw1"])
+    sel(T.B2[:], T.two[:], [[-16, 8], [0, 16]], ALU.is_ge, 0.0, 0, 1, ["two"], ["B2"])
+    sel(T.B2[:], T.B2[:], [[16, 8], [0, 16]], ALU.is_ge, 0.0, 15, -1, ["B2"], ["B2"])
+    sel(T.U1[:, 16:144], T.B2[:], [[1, 128]], ALU.is_gt, 0.0, 0, -1, ["B2"], ["U1"])
+    sel(T.U2[:, 16:144], T.B2[:], [[-1, 128]], ALU.is_ge, 0.0, 0, 1, ["B2"], ["U2"])
+    ms(T.up[:], 0.0, ["up", "upx"])
+    ms(T.Dh[:, 0:1], 0.0, ["Dh0"])
+    ms(T.dh[:, 64:65], 0.5, ["dhx"])
+    ms(T.one[:], 1.0, ["one"])
+    ms(T.coef[:], 0.0, ["coef"])
+    ms(T.srcF[:, 1024:1040], 0.0, ["srcF"])
+    ms(T.Sw[:], 0.0, ["Sw"])
+    ms(T.srcF[:, 1025:1026], 1.0, ["srcF"])
+    sel(T.Wf[:, 0:128], T.one[:], [[-1, 128]], ALU.is_equal, 0.0, 0, 1, ["one"], ["Wf0"])
+    sel(T.Sw[:, 16:144:16], T.Sw[:, 16:144:16], [[-16, 8]], ALU.not_equal, 1.0, 0, 1, ["Sw"], ["Sw"])
+    sel(T.Tle[:], T.B2[:], [[1, 128]], ALU.is_ge, 0.0, 0, -1, ["B2"], ["Tle"])
+    sel(T.Tgt[:], T.B2[:], [[-1, 128]], ALU.is_gt, 0.0, 0, 1, ["B2"], ["Tgt"])
+    sel(T.M2f[:], T.Tgt[:], [[-1, 128]], ALU.not_equal, -2.0 * K, 0, 1, ["Tgt"], ["M2f"])
+    act(T.srcF[:, 0:1024], T.Aa[:, 0:1024], ACT.Identity, ["Aa0", "Aa1"], ["srcFa"], bias=1.0, scale=0.0)
+    act(T.Wb[:, 0:128], T.Wf[:, 0:128], ACT.Copy, ["Wf0"], ["Wb0"])
+    act(T.nW[:, 0:128], T.Wf[:, 0:128], ACT.Copy, ["Wf0"], ["nI"], scale=-1.0)
+    act(T.U1[:, 0:16], T.U1[:, 128:144], ACT.Copy, ["U1"], ["U1r"])
+    act(T.U2[:, 0:16], T.U2[:, 128:144], ACT.Copy, ["U2"], ["U2r"])
+    act(T.Wf[:, 128:256], T.Wf[:, 0:128], ACT.Copy, ["Wf0"], ["Wf1"])
+    act(T.SE[:], T.Sw[:], ACT.Copy, ["Sw"], ["SE"])
+    iota(T.bi[:], [[16, 64]], 16, 0, ["bi"])
+    for r, w in ((1, 1.0), (2, -101.0), (3, -1.0), (4, -1.0)):
+        sel(T.SE[:, 16:144:16], T.SE[:, 16:144:16], [[-16, 8]], ALU.not_equal, w, -r, 1, ["SE"], ["SE"])
+
+    def more_constants():
+        act(T.KI[:], T.Wf[:, 0:128], ACT.Copy, ["Wf0"], ["KI"], scale=float(K))
+        act(T.M1[:], T.Tle[:], ACT.Copy, ["Tle"], ["M1"], scale=0.5)
+        act(T.M2[:], T.M2f[:], ACT.Copy, ["M2f"], ["M2"], scale=0.5)
+        act(T.zb[:], T.Aa[:, 0:1024], ACT.Copy, ["Aa0", "Aa1"], ["zb"], scale=0.0)
+        dma("Y", [(T.Pwin[:], T.zb[:])] + [(T.winE[:, 1024 * j:1024 * j + 1024], T.zb[:]) for j in range(4)], ["zb"], ["Pwin", "winE"])
+
+    def factors():
+        dd, a, b = T.dtab[:, 1:10], T.sm[:, 0:9], T.sm[:, 16:25]
+        op("V", lambda: g.vector.reciprocal(a, dd), ["dtab"], ["sma"])
+        ts(T.smi[:, 1:2], T.smi[:, 0:1], 15, None, ALU.bitwise_and, None, ["smi0"], ["smi1"])
+        ts(b, a, 256.0, -0.49, ALU.mult, ALU.add, ["sma"], ["smb"])
+        cp(T.sm[:, 32:33], T.smi[:, 1:2], ["smi1"], ["pm"])
+        cp(T.smi[:, 4:13], b, ["smb"], ["smi2"])
+        ts(T.sm[:, 33:34], T.sm[:, 32:33], 14.0, 10.0, ALU.max, ALU.mult, ["pm"], ["ecol"])
+        ts(T.coef[:, 1:10], T.smi[:, 4:13], 1.0 / 256, None, ALU.mult, None, ["smi2"], ["coef"])
+        tt(a, T.coef[:, 1:10], dd, ALU.mult, ["coef", "dtab"], ["sma"])
+        ts(T.coef[:, FB + 1:FB + 10], a, -1.0, 1.0, ALU.mult, ALU.add, ["sma"], ["coefF"])
+        tt(T.coef[:, EB + 1:EB + 10], T.coef[:, FB + 1:FB + 10], T.coef[:, 1:10], ALU.add, ["coefF", "coef"], ["coef"])
+
+    def late_a():
+        ts(T.ib[:, 128:192], T.mpi[:], 15, None, ALU.bitwise_and, None, ["mpi"], ["ib1"])
+        ts(T.ib[:, 0:64], T.mpi[:], 4, None, ALU.arith_shift_right, None, ["mpi"], ["ib0"])
+        ts(T.t1[:], T.ib[:, 128:192], 64.0, None, ALU.mult, None, ["ib1"], ["t1"])
+        cp(T.t2[:], T.ib[:, 0:64], ["ib0"], ["t2"])
+        tt(T.t3[:], T.t1[:], T.t2[:], ALU.add, ["t1", "t2"], ["t3"])
+
+    def late_b():
+        calls = []
+        for s in range(1, 5):
+            lh = T.Wf[:, 128 - 16 * s:256 - 16 * s]
+            calls.append((T.P0[:, 64 * (s - 1):64 * s], lh, T.t3[:], True, True))
+            calls.append((T.P0[:, 256 + 4 * (s - 1):256 + 4 * s], lh, T.gn[:], True, True))
+        mm(calls, ["Wf0", "Wf1", "t3", "gn"], ["P0"])
+
+    def late_b2():
+        cp(T.ml[:], T.P0[:, 0:256], ["P0"], ["ml"])
+        cp(T.sm[:, 40:56], T.P0[:, 256:272], ["P0"], ["grot"])
+
+    def late_c():
+        ms(T.uw[:, 0:16], 0.0, ["uwz"])
+        ts(T.bi[:], T.bi[:], T.sm[:, 32:33], None, ALU.add, None, ["bi", "pm"], ["bi"])
+
+    def weights():
+        act(T.Vw[:], T.Sw[:], ACT.Copy, ["Sw"], ["Vw"])
+        act(T.Vw[:, 16:144:16], T.B2[:, 0:128:16], ACT.Copy, ["B2"], ["Vw"], scale=0.5)
+
+    def late_d():
+        act(T.Wb[:, 128:256], T.Wf[:, 0:128], ACT.Copy, ["Wf0"], ["Wb1"])
+        act(T.nW[:, 128:256], T.Wf[:, 0:128], ACT.Copy, ["Wf0"], ["nW1"], scale=-1.0)
+        for t in range(NB):
+            s = t + 1
+            act(T.Gm[:, 128 * t:128 * t + 128], T.Wf[:, 16 * s:16 * s + 128], ACT.Copy, ["Wf0", "Wf1", "grot"], ["Gm%d" % t],
+                scale=T.sm[:, 40 + 5 * t:41 + 5 * t])
+        act(T.p2[:], T.Wf[:, 0:128], ACT.Copy, ["Wf0"], ["p2"], scale=2.0)
+        act(T.n2[:], T.Wf[:, 0:128], ACT.Copy, ["Wf0"], ["n2"], scale=-2.0)
+        act(T.Tle[:], T.Tle[:], ACT.Copy, ["Tle"], ["Tle"], scale=0.5)
+        act(T.Tgt[:], T.Tgt[:], ACT.Copy, ["Tgt"], ["Tgt"], scale=0.5)
+        ms(T.c101[:], 101.0, ["c101"])
+        ms(T.HE[:, 0:1], 0.0, ["HE0"])
+        ms(T.dn[:, 64:65], 0.5, ["dnx"])
+        for x in range(3):
+            ms(Xs[x][:, S:S + 8], 0.0, ["Xz%d" % x])
+
+    def arrived(t):
+        lastw["X%d" % (t % 3)] = ("xa%d" % t, arrivals(T, topo, (rank + 1 + t % (n - 1)) % n, t, 1, 5))
+        readers["X%d" % (t % 3)] = []
+
+    def send(t, j):
+        dst = route(T, topo, rank, t)[1]
+        loc = ("pl%d" if j == 0 else "xl%d") % t
+        trs = []
+        for a, b, h, m, k in pieces(T, topo, rank, t)[j]:
+            rid, pid = topo.addr(dst if h is None else h, core)
+            if j == 0:
+                o, i = T.pl[:, 128 * t + a:128 * t + b], T.pd[:, 128 * t + a:128 * t + b]
+            else:
+                o, i = T["X%d" % (t % 3) if h is None else STOP[t]][:, a:b], T.Y[:, a:b]
+            sem = T.sem[(("pa%d" if j == 0 else "xa%d") % t) if h is None else "h%d" % (3 * t + k)]
+            trs.append((o, i, sem, rid, pid, m))
+            dcount[loc] = dcount.get(loc, 0) + bits(m)
+        if len(trs) == 1:
+            o, i, sem, rid, pid, m = trs[0]
+            g.remote_dma(o, i, sem, T.sem[loc], pid, rid, m)
+        else:
+            g.remote_dma_fused([RemoteDMATransfer(dst_ids=[DstId(rid=rid, pnc=pid)], dma_engine_mask=m, remote_sem=sem, src=i, dst=o)
+                                for o, i, sem, rid, pid, m in trs], local_sem=T.sem[loc])
+
+    def z_chunk(t, c, w=1):
+        z = Zs[t][:, 512 * c:512 * (c + w)]
+        ks = [zk[t] % j for j in range(c, c + w)]
+        tt(z, Xs[t % 3][:, 0:S].indirect(els[t % 2][:, 32 * c:32 * (c + w)]), z, ALU.mult,
+           ["X%d" % (t % 3), "el%d_%d" % (t % 2, c // 4)] + ks, ks)
+
+    def tanh_chunk(t, c0, c1):
+        z = Zs[t][:, 512 * c0:512 * c1]
+        ks = [zk[t] % c for c in range(c0, c1)]
+        act(z, z, ACT.Tanh, ks, ks, scale=2.0 ** -14)
+
+    def fold(t, c0, c1):
+        z = Zs[t]
+        dma("G", [(z[:, 512 * c0:512 * c1], z[:, L + 512 * c0:L + 512 * c1])],
+            [zk[t] % (c + 4) for c in range(c0, c1)], [zk[t] % c for c in range(c0, c1)], accum_op=ALU.add)
+
+    def out_mm(t, c, col=None):
+        col = c if col is None else col
+        mm([(T["acc%d" % c][:], T.Gm[:, 128 * t:128 * t + 128], Zs[t][:, 512 * col:512 * col + 512], t == 0, t == NB - 1)],
+           ["Gm%d" % t, zk[t] % col], ["acc%d" % c])
+
+    def e_w(t, h):
+        mm([(Pb[h][:, 0:128], T.SE[:, 16 - i:144 - i], T.winE[:, L * h + i:L * h + L:16], i == 0, i == 15) for i in range(16)],
+           ["SE", "winE"], ["P%d" % h])
+        if h == 1 and t < NB - 1:
+            dma("Y", [(T.winE[r:128:16, 0:S], T.zb[:, 0:256]) for r in range(5)], ["zb"], ["winE"])
+
+    def e_s(t, h):
+        a = 128 * h
+        scan(T.HE[:, 1 + a:129 + a], Pb[h][:, 0:128], T.c101[:, 0:128], T.HE[:, a:a + 1], ["P%d" % h, "c101", "HE%d" % h], ["HE%d" % (h + 1)])
+
+    def e_c(t, h):
+        a = 128 * h
+        mm([(Pb[h][:, 128:256], T.Tle[:], T.HE[:, 1 + a:129 + a], True, False), (Pb[h][:, 128:256], T.Tgt[:], T.HE[:, a:128 + a], False, True)],
+           ["Tle", "Tgt", "HE%d" % h, "HE%d" % (h + 1)], ["P%d" % h])
+
+    def e_v(t, h, k):
+        a = 128 * h
+        if k == 0:
+            ts(T.ia[:, a:a + 128], Pb[h][:, 128:256], -101.0, None, ALU.add, None, ["P%d" % h], ["ia%d" % h])
+        elif k == 1:
+            ts(T.ib[:, a:a + 128], T.ia[:, a:a + 128], S - 1, None, ALU.bitwise_and, None, ["ia%d" % h], ["ib%d" % h])
+        else:
+            cp(els[t % 2][:, a:a + 128], T.ib[:, a:a + 128], ["ib%d" % h], ["el%d_%d" % (t % 2, h)])
+
+    for t in range(NB):
+        if t == 0:
+            ts(T.dh[:, 0:64], T.dui[:], 0.5, None, ALU.mult, None, ["dui"], ["dh"])
+            scan(T.Dh[:, 1:66], T.dh[:, 0:65], T.up[:, 0:65], 0.0, ["dh", "dhx", "up"], ["Dh"])
+        else:
+            arrived(t - 1)
+            xk = "X%d" % ((t - 1) % 3)
+            xw = Xs[(t - 1) % 3][:, 0:S + 8]
+            xr = [xk, "Xz%d" % ((t - 1) % 3), "sof"]
+            tt(T.cmpb[:], xw.indirect(T.sof[:]), T.Ar[:], ALU.is_gt, xr + ["Ar"], ["cmpb"])
+            for h, (a, b) in enumerate(hs):
+                act(T.Fb[:, a:b], xw.indirect(T.sof[:, 32 * h:32 * h + 32]), ACT.Identity, xr, ["Fb%d" % h],
+                    bias=191.5 + 2.0 ** -13, scale=2.0 ** -4)
+
+            def x1(h):
+                a, b = hs[h]
+                mm([(Pb[h][:], Ib, T.Fb[:, a:b], False, True)], ["Wb0", "Fb%d" % h], ["P%d" % h])
+
+            def ucut(h):
+                a, b = hs[h]
+                ts(T.gg[:, a:b], Pb[h][:], -64.0, 64.0, ALU.max, ALU.min, ["P%d" % h], ["gg%d" % h])
+
+            def xsum(h):
+                a, b = hs[h]
+                mm([(Pb[h][:], Ib, T.Ar[:, a:b], True, False), (Pb[h][:], Ib, T.gg[:, a:b], False, True)],
+                   ["Wb0", "Ar", "gg%d" % h], ["P%d" % h])
+
+            def mirror(h):
+                a, b = hs[h]
+                act(T.ov[:, a:b], Pb[h][:], ACT.Relu, ["P%d" % h], ["ov%d" % h], bias=-256.0)
+                act(T.un[:, a:b], Pb[h][:], ACT.Relu, ["P%d" % h], ["un%d" % h], bias=-256.0, scale=-1.0)
+                k = ab[h]
+                mm([(Pb[k][:], T.n2[:], T.ov[:, a:b], False, False), (Pb[k][:], T.p2[:], T.un[:, a:b], False, True)],
+                   ["n2", "p2", "ov%d" % h, "un%d" % h], ["P%d" % k])
+
+            def xopen(h):
+                a, b = hs[h]
+                k = ab[h]
+                mm([(Pb[k][:], Ib, T.Ar[:, a:b], True, False), (Pb[k][:], Ib, T.gg[:, a:b], False, False)],
+                   ["Wb0", "Ar", "gg%d" % h], ["P%d" % k])
+
+            x1(0)
+            x1(1)
+            mm([(T.P3[:, 0:64], T.Vw[:, 16 - i:144 - i], T.cmpb[:, i:B:16], i == 0, i == 15) for i in range(16)],
+               ["Vw", "cmpb"], ["P3"])
+            ucut(0)
+            ucut(1)
+            xsum(0)
+            tt(T.up[:, 0:64], T.P3[:, 0:64], T.thr[:], ALU.is_ge, ["P3", "thr"], ["up"])
+            scan(T.Dh[:, 1:66], T.up[:, 0:65], T.dn[:, 0:65], 0.0, ["up", "upx", "dn", "dnx"], ["Dh"])
+        mm([(T.P3[:, 0:65], T.U1[:, 16:144], T.Dh[:, 1:66], True, False), (T.P3[:, 0:65], T.U2[:, 16:144], T.Dh[:, 0:65], False, True)],
+           ["U1", "U2", "Dh", "Dh0"], ["P3"])
+        if t == 0:
+            factors()
+        else:
+            xsum(1)
+            xopen(0)
+            tt(T.dh[:, 0:64], T.up[:, 0:64], T.dn[:, 0:64], ALU.add, ["up", "dn"], ["dh"])
+        ts(T.dls[:, 0:64], T.dh[:, 0:64], 2.0, None, ALU.mult, None, ["dh"], ["dlsa"])
+        cp(T.of0[:, 0:65], T.P3[:, 0:65], ["P3"], ["of0"])
+
+
+        def jump_lists():
+            ts(T.dls[:, 64:127], T.dh[:, 0:63], 2.0, float(EB), ALU.mult, ALU.add, ["dh"], ["dlsb"])
+            ts(T.dls[:, 127:128], T.dh[:, 63:64], 2.0, T.sm[:, 33:34], ALU.mult, ALU.add, ["dh", "ecol"], ["dlsc"])
+
+        if t == 0:
+            jump_lists()
+        cp(T.winF[:, 0:WIN].indirect(T.of0[:, 0:65]), T.srcF[:], ["of0", "srcF", "srcFa"], ["winF", "winFa"])
+        if t > 0:
+            jump_lists()
+            mirror(0)
+            xopen(1)
+            mirror(1)
+        mm([(T.P3[:, 128:192], T.U1[:, 0:128], T.Dh[:, 1:65], True, False), (T.P3[:, 128:192], T.U2[:, 0:128], T.Dh[:, 0:64], False, True),
+            (T.P3[:, 192:256], rotf, T.dh[:, 0:64], True, True)],
+           ["U1", "U2", "U1r", "U2r", "Dh", "Dh0", "Wf0", "Wf1", "dh"], ["P3"])
+        cw = T.coef[:, 0:160]
+
+        def rea(h):
+            a, b = hs[h]
+            act(T.RE[:, a:b], cw.indirect(T.dls[:, 32 * h:32 * h + 32]), ACT.Identity, ["coef", "coefF", "dlsa"], ["REa%d" % h])
+
+        def reb(h, q="S"):
+            a, b = hs[h]
+            o, i, r = T.RE[:, 1024 + a:1024 + b], cw.indirect(T.dls[:, 64 + 32 * h:96 + 32 * h]), ["coef", "coefF", "dlsb", "dlsc"]
+            if q == "S":
+                act(o, i, ACT.Identity, r, ["REb%d" % h])
+            else:
+                cp(o, i, r, ["REb%d" % h])
+
+        def ends():
+            act(T.Aa[:, 1024:1025], T.Aa[:, 0:1], ACT.Copy, ["Aa0"], ["Aaw"])
+            act(T.tab[:, K + 1:K + 2], T.Aa[:, 0:1], ACT.Copy, ["Aa0"], ["tab0"])
+
+        if t == 0:
+            ends()
+            rea(0)
+            rea(1)
+            more_constants()
+            act(T.H[:, 0:8], T.Aa[:, 0:8], ACT.Copy, ["Aa0"], ["Hz"], scale=0.0)
+            reb(0)
+            reb(1)
+            for a, b, k in ((0, 1, "tabz0"), (1025, 1033, "tabz1"), (2058, 2064, "tabz2")):
+                act(T.tab[:, a:b], T.Aa[:, 0:b - a], ACT.Copy, ["Aa0"], [k], scale=0.0)
+            weights()
+        else:
+            act(T.Aa[:, 0:512], Pb[ab[0]][:], ACT.Copy, ["P%d" % ab[0]], ["Aa0"])
+            act(T.Aa[:, 512:1024], Pb[ab[1]][:], ACT.Copy, ["P%d" % ab[1]], ["Aa1"])
+            rea(0)
+            ends()
+            reb(0)
+            rea(1)
+        pa, pb = T.pd[:, 128 * t:128 * t + 64], T.pd[:, 128 * t + 64:128 * t + 128]
+        cp(pa, T.P3[:, 0:64], ["P3"], ["pda"])
+        tt(pb, T.P3[:, 0:64], pa, ALU.subtract, ["P3", "pda"], ["pdb"])
+        cp(T.od[:], T.P3[:, 128:256], ["P3"], ["od"])
+        before("G", ["pda", "pdb"], [])
+        send(t, 0)
+        lastw["pl%d" % t] = ("pa%d" % t, arrivals(T, topo, (rank + 1 + t % (n - 1)) % n, t, 0, 1))
+        part = [(0, 64), (64, 128), (128, 256)]
+
+        def w_mm(c):
+            a, b = part[c]
+            mm([(Pb[2 + c % 2][:, 0:b - a], T.Sw[:, 16 - i:144 - i], T.winF[:, 16 * a + i:16 * b:16], i == 0, i == 15)
+                for i in range(16)], ["Sw", "winF"], ["P%d" % (2 + c % 2)])
+
+        def h_scan(c):
+            a, b = part[c]
+            scan(T.H[:, 8 + a:8 + b], Pb[2 + c % 2][:, 0:b - a], T.zb[:, 0:b - a], T.H[:, 7 + a:8 + a],
+                 ["P%d" % (2 + c % 2), "zb", "H%d" % (c - 1) if c else "Hz"], ["H%d" % c])
+
+        def i_mm(c):
+            a, b = part[c]
+            o = Pb[2 + c % 2][:, 256:256 + b - a]
+            h1, h0 = T.H[:, 8 + a:8 + b], T.H[:, 7 + a:7 + b]
+            mm([(o, T.M1[:], h1, True, False), (o, T.KI[:], h1, False, False), (o, T.M2[:], h0, False, True)],
+               ["M1", "KI", "M2", "H%d" % c, "H%d" % (c - 1) if c else "Hz"], ["P%d" % (2 + c % 2)])
+
+        def i_cp(c):
+            a, b = part[c]
+            cp(T.idx[:, a:b], Pb[2 + c % 2][:, 256:256 + b - a], ["P%d" % (2 + c % 2)], ["idx%d" % c])
+
+        def da(h):
+            a, b = hs[h]
+            k = 1 - h
+            mm([(Pb[k][:], Ib, T.Aa[:, a + 1:b + 1], True, False), (Pb[k][:], T.nW[:, 0:128], T.Aa[:, a:b], False, True)],
+               ["Wb0", "nI", "Aa0", "Aa1"] + (["Aaw"] if h else []), ["P%d" % k])
+
+        def slope(h):
+            a, b = hs[h]
+            tt(T.tab[:, 1 + a:1 + b], Pb[1 - h][:], T.RE[:, a:b], ALU.mult, ["P%d" % (1 - h), "REa%d" % h], ["tabs%d" % h])
+
+        def jump(h):
+            a, b = hs[h]
+            tt(T.tab[:, K + 2 + a:K + 2 + b], Pb[1 - h][:], T.RE[:, 1024 + a:1024 + b], ALU.mult, ["P%d" % (1 - h), "REb%d" % h],
+               ["tabj%d" % h])
+
+        if t == 0:
+            da(0)
+            da(1)
+            w_mm(0)
+            w_mm(1)
+            slope(0)
+            h_scan(0)
+            i_mm(0)
+            slope(1)
+            jump(0)
+            i_cp(0)
+            h_scan(1)
+            i_mm(1)
+            w_mm(2)
+            jump(1)
+        else:
+            da(0)
+            w_mm(0)
+            da(1)
+            reb(1)
+            slope(0)
+            h_scan(0)
+            i_mm(0)
+            w_mm(1)
+            jump(0)
+            i_cp(0)
+            w_mm(2)
+            slope(1)
+            h_scan(1)
+            i_mm(1)
+            jump(1)
+            h_scan(2)
+            i_mm(2)
+        i_cp(1)
+        if t < NB - 1:
+            dma("Y", [(T.Ar[16:128, :], T.Aa[0:112, 0:1024]), (T.Ar[0:16, :], T.Aa[112:128, 0:1024])], ["Aa0", "Aa1"], ["Ar"])
+
+        def p_window():
+            dma("Y", [(T.Pwin[0:128:16, :], T.pl[:, 128 * t:128 * t + 64]), (T.Pwin[1:128:16, :], T.pl[:, 128 * t + 64:128 * t + 128])],
+                ["pl%d" % t], ["Pwin"])
+
+        if t > 0:
+            p_window()
+        tabr = ["tabz0", "tabz1", "tabz2", "tab0", "tabs0", "tabs1", "tabj0", "tabj1"]
+
+        def delta(c, q="S"):
+            o = T.dlt[:, 1024 * (c % 3):1024 * (c % 3) + 1024]
+            i = T.tab[:, 0:2064].indirect(T.idx[:, 64 * c:64 * c + 64])
+            if q == "S":
+                act(o, i, ACT.Identity, tabr + ["idx%d" % min(c, 2)], ["dlt%d" % (c % 3)])
+            else:
+                cp(o, i, tabr + ["idx%d" % min(c, 2)], ["dlt%d" % (c % 3)])
+
+        def y_scan(c):
+            init = 0.0 if c == 0 else T.Y[:, 1024 * c - 1:1024 * c]
+            scan(T.Y[:, 1024 * c:1024 * c + 1024], T.dlt[:, 1024 * (c % 3):1024 * (c % 3) + 1024], T.zb[:], init,
+                 ["dlt%d" % (c % 3), "zb"] + (["Y%d" % (c - 1)] if c else []), ["Y%d" % c])
+            before("G", ["Y%d" % c], [])
+            send(t, c + 1)
+
+        def move_y(c0, c1):
+            z = Zs[t]
+            a, b = 1024 * c0, 1024 * c1
+            dma("Y", [(z[16:128, a:b], T.Y[0:112, a:b]), (z[0:16, a:b], T.Y[112:128, a:b])],
+                ["Y%d" % c for c in range(c0, c1)] + (["xsent"] if t < NB - 1 else []),
+                [zk[t] % c for c in range(2 * c0, 2 * c1)] + (["X1"] if t == NB - 1 and c0 == 0 else []))
+
+        o1, d1 = T.od[:, 0:64], T.od[:, 64:128]
+
+        def lists_a():
+            ts(T.lv[:], o1, float(S), None, ALU.is_lt, None, ["od"], ["lv"])
+            ts(T.t1[:], d1, 0.5, 0.5, ALU.is_equal, ALU.subtract, ["od"], ["t1"])
+            ts(T.sof[:], o1, float(S), None, ALU.min, None, ["od"], ["sof"])
+            tt(T.t2[:], T.t1[:], T.lv[:], ALU.mult, ["t1", "lv"], ["t2"])
+            tt(T.t3[:], T.lv[:], T.bi[:], ALU.mult, ["lv", "bi"], ["t3"])
+
+        def lists_b(k):
+            if k == 0:
+                ts(T.t1[:], d1, 4.4, 99.0, ALU.is_ge, ALU.mult, ["od"], ["t1"])
+                ts(T.lv[:], T.t2[:], 200.0, 108.5, ALU.mult, ALU.add, ["t2"], ["lv"])
+            else:
+                tt(T.dn[:, 0:64], d1, T.t2[:], ALU.add, ["od", "t2"], ["dn"])
+                cp(T.jl[:], T.t3[:], ["t3"], ["jl"])
+                tt(T.thr[:], T.t1[:], T.lv[:], ALU.max, ["t1", "lv"], ["thr"])
+
+        def durations(q, h):
+            a, b = hs[h]
+            i = T.dtab[:, 0:16].indirect(T.dls[:, 32 * h:32 * h + 32])
+            if q == "S":
+                act(T.Dg[:, a:b], i, ACT.Identity, ["dtab", "dlsa"], ["Dg%d" % h])
+            else:
+                cp(T.Dg[:, a:b], i, ["dtab", "dlsa"], ["Dg%d" % h])
+
+        def e_source():
+            act(T.srcE[:], T.Pwin[:, 0:1024].indirect(T.ml[:, 64 * t:64 * t + 64]), ACT.Identity, ["Pwin", "ml"], ["srcE"])
+            dma("Y", [(T.srcE[3:128:16, 1:1024], T.srcE[0:128:16, 0:1023]), (T.srcE[4:128:16, 1:1024], T.srcE[1:128:16, 0:1023]),
+                      (T.srcE[18:128:16, 1:1024], T.Dg[0:112:16, 0:1023]), (T.srcE[2:3, 1:1024], T.Dg[112:113, 0:1023])],
+                ["Dg0", "Dg1"], ["srcE"])
+
+        def e_scatter():
+            cp(T.winE[:, 0:WIN].indirect(T.eof[:]), T.srcE[:], ["eof", "srcE"], ["winE"])
+
+        def v_move(h):
+            a, b = hs[h]
+            mm([(Pb[h][:], rotb, T.gg[:, a:b], True, False), (Pb[h][:], rotb, T.uw[:, 16 + a:16 + b], False, False),
+                (Pb[h][:], T.nW[:, 112:240], T.vL[:, a:b], False, True)],
+               ["Wb0", "Wb1", "nI", "nW1", "gg%d" % h, "uw%d" % h, "vL"], ["P%d" % h])
+
+        def v_keep(h):
+            a, b = hs[h]
+            act(T.uw[:, 16 + a:16 + b], Pb[h][:], ACT.Identity, ["P%d" % h], ["uw%d" % h], bias=-192.0)
+
+        def v_live():
+            act(T.vL[:], T.uw[:, 0:1040].indirect(T.jl[:]), ACT.Identity, ["uw0", "uw1", "uwz", "jl"], ["vL"], bias=-192.0)
+            for h, (a, b) in enumerate(hs):
+                mm([(Pb[h][:], Ib, T.vL[:, a:b], True, False)], ["Wb0", "vL"], ["P%d" % h])
+
+        last = t == NB - 1
+        if t == 0:
+            delta(0)
+            late_a()
+            p_window()
+            delta(1)
+            h_scan(2)
+            i_mm(2)
+            late_b()
+            y_scan(0)
+            i_cp(2)
+            delta(2)
+            late_b2()
+            y_scan(1)
+            delta(3)
+            late_c()
+            y_scan(2)
+            lists_a()
+            y_scan(3)
+        else:
+            if last:
+                durations("S", 0)
+            delta(0)
+            e_w(t - 1, 0)
+            e_w(t - 1, 1)
+            cp(T.eof[:], o1, ["od"], ["eof"])
+            i_cp(2)
+            if last:
+                durations("V", 1)
+            else:
+                lists_a()
+            delta(1)
+            y_scan(0)
+            e_s(t - 1, 0)
+            e_c(t - 1, 0)
+            if not last:
+                lists_b(0)
+            delta(2)
+            y_scan(1)
+            delta(3)
+            e_s(t - 1, 1)
+            e_c(t - 1, 1)
+            e_v(t - 1, 0, 0)
+            if last:
+                move_y(0, 2)
+            else:
+                lists_b(1)
+            y_scan(2)
+            for h, k in ((0, 1), (1, 0), (0, 2), (1, 1)):
+                e_v(t - 1, h, k)
+            y_scan(3)
+            if not last:
+                v_move(0)
+                v_move(1)
+            if t >= 2:
+                for c in range(4):
+                    out_mm(t - 2, c)
+            if last:
+                move_y(2, 4)
+        if not last:
+            dma("Y", [(T.winF[0:128:16, 0:S], T.zb[:, 0:256])], ["zb"], ["winF", "winFa"])
+        for c in range(4):
+            readers["Y%d" % c].append(("xl%d" % t, dcount["xl%d" % t]))
+        lastw["xsent"] = ("xl%d" % t, dcount["xl%d" % t])
+        if t == 0:
+            cp(T.eof[:], o1, ["od"], ["eof"])
+            durations("V", 0)
+            durations("V", 1)
+            e_source()
+            lists_b(0)
+            lists_b(1)
+            late_d()
+            v_live()
+            e_scatter()
+        else:
+            if not last:
+                durations("S", 0)
+                durations("S", 1)
+            e_source()
+            z_chunk(t - 1, 0, 2)
+            e_v(t - 1, 1, 2)
+            if not last:
+                v_keep(0)
+                v_keep(1)
+            tanh_chunk(t - 1, 0, 2)
+            z_chunk(t - 1, 4, 2)
+            tanh_chunk(t - 1, 4, 6)
+            fold(t - 1, 0, 2)
+            if last:
+                e_scatter()
+                e_w(t, 0)
+                e_w(t, 1)
+            else:
+                v_live()
+            if last:
+                z_chunk(t - 1, 2)
+                tanh_chunk(t - 1, 2, 3)
+                z_chunk(t - 1, 6)
+                tanh_chunk(t - 1, 6, 7)
+                fold(t - 1, 2, 3)
+                e_s(t, 0)
+                e_c(t, 0)
+                z_chunk(t - 1, 3)
+                tanh_chunk(t - 1, 3, 4)
+                e_s(t, 1)
+                e_c(t, 1)
+                out_mm(t - 1, 0)
+                out_mm(t - 1, 1)
+                e_v(t, 0, 0)
+                z_chunk(t - 1, 7)
+                tanh_chunk(t - 1, 7, 8)
+                fold(t - 1, 3, 4)
+            else:
+                z_chunk(t - 1, 2, 2)
+                tanh_chunk(t - 1, 2, 4)
+                z_chunk(t - 1, 6, 2)
+                tanh_chunk(t - 1, 6, 8)
+                fold(t - 1, 2, 4)
+            if not last:
+                e_scatter()
+        if not last:
+            move_y(0, 4)
+
+    t = NB - 1
+    for h, k in ((1, 0), (0, 1), (1, 1), (0, 2), (1, 2)):
+        e_v(t, h, k)
+    out_mm(t - 1, 2)
+    out_mm(t - 1, 3)
+    arrived(t)
+    z = Zs[t]
+
+    def pair(p):
+        z_chunk(t, p)
+        act(Pb[p % 2][:], z[:, 512 * p:512 * p + 512], ACT.Tanh, [zk[t] % p], ["P%d" % (p % 2)], scale=2.0 ** -14)
+        z_chunk(t, p + 4)
+        tanh_chunk(t, p + 4, p + 5)
+
+    def finish(p):
+        zz = z[:, 512 * (p + 4):512 * (p + 5)]
+        tt(zz, Pb[p % 2][:], zz, ALU.add, ["P%d" % (p % 2), zk[t] % (p + 4)], [zk[t] % (p + 4)])
+        out_mm(t, p, p + 4)
+
+    def store(p):
+        act(T.Z0[:, 512 * p:512 * p + 512], T["acc%d" % p][:], ACT.Copy, ["acc%d" % p], ["Z0_%d" % p])
+        dma("Y", [(T.yo[:, 512 * p:512 * p + 512], T.Z0[:, 512 * p:512 * p + 512])], ["Z0_%d" % p], ["yo%d" % p])
+
+    z_chunk(t, 0)
+    tanh_chunk(t, 0, 1)
+    z_chunk(t, 4)
+    tanh_chunk(t, 4, 5)
+    fold(t, 0, 1)
+    pair(1)
+    pair(2)
+    finish(1)
+    out_mm(t, 0)
+    pair(3)
+    finish(2)
+    store(1)
+    store(0)
+    finish(3)
+    store(2)
+    store(3)
+    for s in dcount:
+        wait("G", (s, dcount[s]))
+    for q in cnt:
+        wait("G", ("c" + q, cnt[q]))

@@ -4,111 +4,184 @@ from concourse.mybir import AluOpType, ActivationFunctionType
 ALU = AluOpType
 ACT = ActivationFunctionType
 S, B, NB, L = 4096, 1024, 4, 2048
-WIN = 9232
+WIN = 9248
 K = 1032
-EB, FB = 140, 150
+MW, MS = 130, 136
 
 SCRATCH = {
-    "X0": ("sbuf", [128, 4104], "float32"), "X1": ("sbuf", [128, 4104], "float32"), "X2": ("sbuf", [128, 4104], "float32"),
-    "Y": ("sbuf", [128, 4096], "float32"), "Z0": ("sbuf", [128, 4096], "float32"), "Z1": ("sbuf", [128, 4096], "float32"),
+    "X0": ("sbuf", [128, 4096], "float32"), "X1": ("sbuf", [128, 4096], "float32"), "X2": ("sbuf", [128, 4096], "float32"),
+    "Y0": ("sbuf", [128, 4104], "float32"), "Y1": ("sbuf", [128, 4104], "float32"),
+    "Z0": ("sbuf", [128, 4096], "float32"), "Z1": ("sbuf", [128, 4096], "float32"), "Z2": ("sbuf", [128, 4096], "float32"),
     "dlt": ("sbuf", [128, 3072], "float32"), "tab": ("sbuf", [128, 2064], "float32"),
     "winF": ("sbuf", [128, WIN], "bfloat16"), "winE": ("sbuf", [128, WIN], "bfloat16"),
-    "Aa": ("sbuf", [128, 1040], "bfloat16"), "Ar": ("sbuf", [128, 1024], "bfloat16"), "uw": ("sbuf", [128, 1040], "bfloat16"),
-    "Fb": ("sbuf", [128, 1024], "bfloat16"), "vL": ("sbuf", [128, 1024], "bfloat16"), "gg": ("sbuf", [128, 1024], "bfloat16"),
-    "ov": ("sbuf", [128, 1024], "bfloat16"), "un": ("sbuf", [128, 1024], "bfloat16"), "cmpb": ("sbuf", [128, 1024], "bfloat16"),
-    "RE": ("sbuf", [128, 2048], "bfloat16"), "srcE": ("sbuf", [128, 1024], "bfloat16"), "Dg": ("sbuf", [128, 1024], "bfloat16"),
-    "srcF": ("sbuf", [128, 1040], "bfloat16"), "zb": ("sbuf", [128, 1024], "bfloat16"), "c101": ("sbuf", [128, 256], "bfloat16"),
-    "Pwin": ("sbuf", [128, 1024], "bfloat16"), "pd": ("sbuf", [128, 512], "bfloat16"), "pl": ("sbuf", [128, 512], "bfloat16"),
-    "dui": ("sbuf", [128, 64], "int32"), "mpi": ("sbuf", [128, 64], "int32"), "gn": ("sbuf", [128, 4], "float32"),
-    "ia": ("sbuf", [128, 256], "int32"), "ib": ("sbuf", [128, 256], "int32"),
-    "dh": ("sbuf", [128, 68], "float32"), "up": ("sbuf", [128, 68], "float32"), "dn": ("sbuf", [128, 68], "float32"),
-    "Dh": ("sbuf", [128, 68], "float32"), "thr": ("sbuf", [128, 64], "float32"),
-    "t1": ("sbuf", [128, 64], "float32"), "t2": ("sbuf", [128, 64], "float32"), "t3": ("sbuf", [128, 64], "float32"),
-    "od": ("sbuf", [128, 128], "float32"), "lv": ("sbuf", [128, 64], "float32"), "bi": ("sbuf", [128, 64], "float32"),
-    "of0": ("sbuf", [128, 66], "uint16"), "dls": ("sbuf", [128, 128], "uint16"), "eof": ("sbuf", [128, 64], "uint16"),
+    "Aa": ("sbuf", [128, 1040], "bfloat16"), "Al": ("sbuf", [128, 3072], "bfloat16"),
+    "uw": ("sbuf", [128, 1040], "bfloat16"), "Fb": ("sbuf", [128, 1024], "bfloat16"), "Fl": ("sbuf", [128, 1024], "bfloat16"),
+    "vD": ("sbuf", [128, 1024], "bfloat16"), "cmpb": ("sbuf", [128, 1024], "bfloat16"), "RE": ("sbuf", [128, 1024], "bfloat16"),
+    "srcE": ("sbuf", [128, 1024], "bfloat16"), "Dg": ("sbuf", [128, 1024], "bfloat16"),
+    "zb": ("sbuf", [128, 1040], "bfloat16"), "ob": ("sbuf", [128, 1024], "bfloat16"), "c101": ("sbuf", [128, 256], "bfloat16"),
+    "Pwin": ("sbuf", [128, 1024], "bfloat16"), "pd": ("sbuf", [128, 128], "bfloat16"), "qb": ("sbuf", [128, 256], "bfloat16"),
+    "dui": ("sbuf", [128, 64], "int32"), "mpi": ("sbuf", [128, 64], "int32"), "gn": ("sbuf", [128, 8], "float32"),
+    "ia": ("sbuf", [128, 128], "int32"),
+    "Mb": ("sbuf", [128, 14 * MS], "uint16"), "Mq": ("sbuf", [128, 64], "uint16"), "Mr": ("sbuf", [128, 64], "uint16"),
+    "up": ("sbuf", [128, 68], "float32"), "df": ("sbuf", [128, 68], "float32"), "lv": ("sbuf", [128, 68], "float32"),
+    "a2": ("sbuf", [128, 68], "float32"), "Dh": ("sbuf", [128, 68], "float32"), "four": ("sbuf", [128, 68], "float32"),
+    "dd": ("sbuf", [128, 64], "float32"), "sq": ("sbuf", [128, 64], "float32"), "bn": ("sbuf", [128, 64], "float32"),
+    "t1": ("sbuf", [128, 64], "float32"), "t2": ("sbuf", [128, 64], "float32"), "pf": ("sbuf", [128, 64], "float32"),
+    "bi": ("sbuf", [128, 64], "float32"),
     "sof": ("sbuf", [128, 64], "uint16"), "jl": ("sbuf", [128, 64], "uint16"), "idx": ("sbuf", [128, 256], "uint16"),
-    "el0": ("sbuf", [128, 256], "uint16"), "el1": ("sbuf", [128, 256], "uint16"), "ml": ("sbuf", [128, 256], "uint16"),
+    "el0": ("sbuf", [128, 256], "uint16"), "el1": ("sbuf", [128, 256], "uint16"), "ml": ("sbuf", [128, 64], "uint16"),
     "H": ("sbuf", [128, 264], "bfloat16"), "HE": ("sbuf", [128, 260], "float32"),
-    "coef": ("sbuf", [128, 160], "float32"), "dtab": ("sbuf", [128, 16], "float32"), "sm": ("sbuf", [128, 64], "float32"),
+    "coef": ("sbuf", [128, 16], "float32"), "dtab": ("sbuf", [128, 16], "float32"), "sm": ("sbuf", [128, 32], "float32"),
     "smi": ("sbuf", [128, 16], "int32"),
-    "two": ("sbuf", [128, 128], "float32"), "one": ("sbuf", [128, 128], "float32"), "B2": ("sbuf", [128, 128], "float32"),
-    "U1": ("sbuf", [128, 144], "float32"), "U2": ("sbuf", [128, 144], "float32"),
-    "Wf": ("sbuf", [128, 256], "float32"), "Wb": ("sbuf", [128, 256], "bfloat16"),
-    "nW": ("sbuf", [128, 256], "bfloat16"), "p2": ("sbuf", [128, 128], "bfloat16"), "n2": ("sbuf", [128, 128], "bfloat16"),
+    "one": ("sbuf", [128, 128], "float32"), "B1": ("sbuf", [128, 128], "float32"),
+    "U1": ("sbuf", [128, 128], "float32"), "U2": ("sbuf", [128, 128], "float32"),
+    "Wf": ("sbuf", [128, 144], "float32"), "Wb": ("sbuf", [128, 144], "bfloat16"), "nIf": ("sbuf", [128, 128], "float32"),
+    "nI": ("sbuf", [128, 144], "bfloat16"), "n192": ("sbuf", [128, 128], "bfloat16"), "n4096": ("sbuf", [128, 128], "bfloat16"),
     "KI": ("sbuf", [128, 128], "bfloat16"), "M1": ("sbuf", [128, 128], "bfloat16"), "M2": ("sbuf", [128, 128], "bfloat16"),
-    "Tle": ("sbuf", [128, 128], "float32"), "Tgt": ("sbuf", [128, 128], "float32"), "M2f": ("sbuf", [128, 128], "float32"),
-    "Sw": ("sbuf", [128, 144], "bfloat16"), "SE": ("sbuf", [128, 144], "bfloat16"), "Vw": ("sbuf", [128, 144], "bfloat16"),
+    "Tle": ("sbuf", [128, 128], "float32"), "Tgt": ("sbuf", [128, 128], "float32"),
+    "Sw": ("sbuf", [128, 144], "bfloat16"), "SE": ("sbuf", [128, 160], "bfloat16"), "Vw": ("sbuf", [128, 144], "bfloat16"),
     "Gm": ("sbuf", [128, 512], "float32"),
     "acc0": ("psum", [128, 512], "float32"), "acc1": ("psum", [128, 512], "float32"),
     "acc2": ("psum", [128, 512], "float32"), "acc3": ("psum", [128, 512], "float32"),
     "P0": ("psum", [128, 512], "float32"), "P1": ("psum", [128, 512], "float32"),
     "P2": ("psum", [128, 512], "float32"), "P3": ("psum", [128, 512], "float32"),
 }
-NQ = 90
-SEMAPHORES = (["cV", "cS", "cP", "cG"] + ["q%d" % i for i in range(NQ)]
-              + ["xa%d" % t for t in range(NB)] + ["pa%d" % t for t in range(NB)]
-              + ["xl%d" % t for t in range(NB)] + ["pl%d" % t for t in range(NB)]
-              + ["h%d" % i for i in range(3 * NB)] + ["hl"])
+NQ = 60
+SEMAPHORES = (["cV", "cS", "cP", "cG", "ml", "fl", "al", "hl", "oa"] + ["q%d" % i for i in range(NQ)]
+              + ["xa%d" % t for t in range(NB)] + ["xl%d" % t for t in range(NB)] + ["wa%d" % t for t in range(1, NB - 1)]
+              + ["ma%d" % i for i in range(4 * NB - 3)] + ["fa%d" % t for t in range(NB - 1)] + ["aa%d" % t for t in range(NB - 1)]
+              + ["ya%d" % c for c in range(4)] + ["h%d" % i for i in range(4 * NB)] + ["k%d" % i for i in range(4 * NB)])
 SIM_CORES = 256
-STOP = ["X0", "X1", "X2", "Y"]
+STOPS = ["X0", "X1", "X2", "Y0", "Y1", "Z0", "Z1", "Z2"]
+LAST = (NB - 1, 3)
+PLAN = {}
 
 
 def bits(m):
     return bin(m).count("1")
 
 
-def route(T, topo, r, t):
+def reader(n, r, t):
+    return (r - 1 - t % (n - 1)) % n
+
+
+def partner(n, r, t):
+    return (r + 1 + t % (n - 1)) % n
+
+
+def crosses(topo, c):
+    return any(topo.mates(c, x) and topo.may_write(c, x) for x in range(SIM_CORES))
+
+
+def ways(T, topo, r, t):
     n = len(T.cores)
-    src = T.cores[r]
-    dst = T.cores[(r - 1 - t % (n - 1)) % n]
+    src, dst = T.cores[r], T.cores[reader(n, r, t)]
+    free = [c for c in topo.cores_of(src) if T.rank_of(c) is None]
+    h0, h1 = [c for c in free if topo.die(c) == topo.die(src) and not crosses(topo, c)]
+    gate = [c for c in free if topo.die(c) == topo.die(src) and crosses(topo, c)][0]
     if dst in topo.cores_of(src):
-        return src, dst, None, None
-    near = [c for c in topo.cores_of(src) if T.rank_of(c) is None and topo.die(c) == topo.die(dst) and topo.may_write(c, dst)][0]
-    far = None
-    if topo.die(near) == topo.die(src):
-        far = [c for c in range(SIM_CORES) if topo.mates(c, dst) and topo.die(c) == topo.die(src)
-               and topo.may_write(src, c) and topo.may_write(c, dst)][0]
-    return src, dst, near, far
+        return [[h1, dst], [gate, dst], [h0, dst], [h0, dst]]
+    other = [c for c in free if topo.die(c) != topo.die(src) and not crosses(topo, c)][1]
+    far = [c for c in range(SIM_CORES) if topo.mates(c, dst) and topo.die(c) == topo.die(src) and topo.may_write(c, dst)][0]
+    peer = [T.rank_of(c) for c in topo.cores_of(src) if c != src and T.rank_of(c) is not None][0]
+    if T.cores[reader(n, peer, t)] not in topo.cores_of(src):
+        return [[gate, far, dst], [h0, dst], [h0, dst], [h0, dst]]
+    if t == NB - 1:
+        across = [c for c in free if topo.die(c) != topo.die(src) and crosses(topo, c)][0]
+        return [[across, dst], [h0, dst], [other, dst], [h0, dst]]
+    return [[h1, other, dst], [gate, other, dst], [h0, dst], [h0, dst]]
 
 
-def pieces(T, topo, r, t):
-    src, dst, near, far = route(T, topo, r, t)
-    m = topo.mask(src, dst)
-    if near is None:
-        return [[(0, 128, None, m, 0)]] + [[(1024 * c, 1024 * c + 1024, None, m, 0)] for c in range(4)]
-    nm = topo.mask(src, near) & ~m
-    fm = m if far is None else topo.mask(src, far)
-    return [[(0, 64, near, nm, 0), (64, 128, far, fm, 0)], [(0, 1024, far, fm, 1)], [(1024, 2048, near, nm, 1)],
-            [(2048, 2560, near, nm, 2), (2560, 3072, None, m, 0)], [(3072, 4096, None, m, 0)]]
+def plan(T, topo):
+    if not PLAN:
+        allways, first, jobs, used = {}, {}, {}, {}
+
+        def stop(c):
+            m = used.get(c, 0)
+            used[c] = m + 2
+            return STOPS[m // 4], B * (m % 4)
+
+        for t in range(NB):
+            for r in range(len(T.cores)):
+                allways[r, t] = ways(T, topo, r, t)
+                for c, way in enumerate(allways[r, t]):
+                    at = stop(way[0])
+                    first[r, t, c] = (way[0],) + at
+                    for j in range(len(way) - 1):
+                        last = j + 2 == len(way)
+                        to = ("X%d" % (t % 3), B * c) if last else stop(way[j + 1])
+                        jobs.setdefault(way[j], []).append((t, j, c, r, way[j - 1] if j else T.cores[r], at, way[j + 1], to, last))
+                        at = to
+        for c in jobs:
+            jobs[c].sort()
+        PLAN.update(ways=allways, first=first, jobs=jobs)
+    return PLAN
 
 
-def arrivals(T, topo, r, t, first, last):
-    src, dst, near, far = route(T, topo, r, t)
-    return sum(bits(m if h is None else topo.mask(h, dst)) for call in pieces(T, topo, r, t)[first:last] for a, b, h, m, k in call)
+def small_mask(T, topo, src):
+    return [topo.mask(src, c) for c in T.cores if c not in topo.cores_of(src)][0]
+
+
+def first_mask(T, topo, r, t, c):
+    m = topo.mask(T.cores[r], plan(T, topo)["first"][r, t, c][0])
+    return m & ~small_mask(T, topo, T.cores[r]) if c == 3 or c == 0 and t < NB - 1 else m
+
+
+def arrivals(T, topo, r, t):
+    w = plan(T, topo)["ways"][r, t]
+    return sum(bits(small_mask(T, topo, T.cores[r]) if (t, c) == LAST else topo.mask(w[c][-2], w[c][-1])) for c in range(4))
 
 
 def helper_program(g, core, T, topo):
-    sent = 0
-    for t in range(NB):
-        for r in range(len(T.cores)):
-            src, dst, near, far = route(T, topo, r, t)
-            if core not in (near, far):
+    jobs = plan(T, topo)["jobs"].get(core, [])
+    sent, held = [0], []
+
+    def write(dst, o, i, sem):
+        rid, pid = topo.addr(dst, core)
+        if dst not in topo.cores_of(core) and sent[0]:
+            g.wait_ge(T.sem.hl, sent[0])
+        g.remote_dma(o, i, T.sem[sem], T.sem.hl, pid, rid, topo.mask(core, dst))
+        sent[0] += bits(topo.mask(core, dst))
+
+    resets = [job for job in jobs if job[1] == 0 and job[2] == 2 and 0 < job[0] < NB - 1]
+    if resets:
+        g.sync.wait_ge(T.sem.oa, bits(small_mask(T, topo, resets[0][4])))
+        for j in (1, 2):
+            g.sync.dma_start(T.winF[:, B * j:B * j + B], T.winF[:, 0:B]).then_inc(T.sem.q0, 16)
+        g.wait_ge(T.sem.q0, 32)
+    for num, (t, j, c, r, src, at, nxt, to, last) in enumerate(jobs):
+        buf, col = T[at[0]], at[1]
+        sem = "xa%d" % t if last else "k%d" % (4 * t + c)
+        if j == 0:
+            came, count = T.sem["h%d" % (4 * t + c)], bits(first_mask(T, topo, r, t, c))
+            turned = T.sem["q%d" % (num + 1)]
+            g.sync.wait_ge(came, count)
+            cut = 112 if t < NB - 1 else 16
+            raw, col = col, col + B
+            g.sync.dma_start(buf[0:cut, col:col + B], buf[128 - cut:128, raw:raw + B]).then_inc(turned, 16)
+            g.sync.dma_start(buf[cut:128, col:col + B], buf[0:128 - cut, raw:raw + B]).then_inc(turned, 16)
+            if t == NB - 1:
+                if (t, c) != LAST:
+                    g.wait_ge(came, count)
+                    write(nxt, T[to[0]][:, to[1]:to[1] + B], buf[:, raw:raw + B], sem)
+                g.wait_ge(turned, 32)
+                write(src, T.Z2[:, B * c:B * c + B], buf[:, col:col + B], "ya%d" % c)
                 continue
-            out = topo.mask(core, dst)
-            rid, pid = topo.addr(dst, core)
-            for j, call in enumerate(pieces(T, topo, r, t)):
-                for a, b, h, m, k in call:
-                    if h != core:
-                        continue
-                    g.wait_ge(T.sem["h%d" % (3 * t + k)], bits(m))
-                    if j == 0:
-                        ap = T.pl[:, 128 * t + a:128 * t + b]
-                        g.remote_dma(ap, ap, T.sem["pa%d" % t], T.sem.hl, pid, rid, out)
-                    else:
-                        g.remote_dma(T["X%d" % (t % 3)][:, a:b], T[STOP[t]][:, a:b], T.sem["xa%d" % t], T.sem.hl, pid, rid, out)
-                    sent += bits(out)
-    if sent:
-        g.wait_ge(T.sem.hl, sent)
+            if c == 2 and t > 0:
+                g.wait_ge(came, count)
+                write(src, T.winF[:, 0:3 * B], T.winF[:, 0:3 * B], "wa%d" % t)
+            ready = (turned, 32)
+        else:
+            ready = (T.sem["k%d" % (4 * t + c)], bits(topo.mask(src, core)))
+        held.append((ready, nxt, T[to[0]][:, to[1]:to[1] + B], buf[:, col:col + B], sem))
+        if c < 3 and j == 0 and last and nxt not in topo.cores_of(core):
+            continue
+        g.wait_ge(*ready)
+        while held:
+            g.wait_ge(*held[0][0])
+            write(*held.pop(0)[1:])
+    if sent[0]:
+        g.wait_ge(T.sem.hl, sent[0])
 
 
 def rank_program(g, core, T, topo):
@@ -121,6 +194,7 @@ def rank_program(g, core, T, topo):
     cnt = {"V": 0, "S": 0, "P": 0, "G": 0}
     known = {q: {} for q in eng}
     lastw, readers = {}, {}
+    small = small_mask(T, topo, core)
     nq = [0]
     dcount = {}
     banks = ("P0", "P1", "P2", "P3", "acc0", "acc1", "acc2", "acc3")
@@ -132,13 +206,8 @@ def rank_program(g, core, T, topo):
             known[q][s] = v
 
     def before(q, r, w, skip=None):
-        toks = []
-        for k in r:
-            if k in lastw:
-                toks.append(lastw[k])
+        toks = [lastw[k] for k in r + w if k in lastw]
         for k in w:
-            if k in lastw:
-                toks.append(lastw[k])
             toks.extend(readers.get(k, []))
         best = {}
         for s, v in toks:
@@ -183,6 +252,17 @@ def rank_program(g, core, T, topo):
         dcount[s] = 16 * len(pairs)
         after((s, dcount[s]), r, w)
 
+    def remote(dst, o, i, sem, loc, r):
+        before("G", r, [])
+        rid, pid = topo.addr(dst, core)
+        g.remote_dma(o, i, T.sem[sem], T.sem[loc], pid, rid, small)
+        dcount[loc] = dcount.get(loc, 0) + bits(small)
+        after((loc, dcount[loc]), r, [])
+
+    def lands(key, sem):
+        lastw[key] = (sem, bits(small))
+        dcount[sem] = lastw[key][1]
+
     def ts(o, i, s1, s2, o0, o1, r, w):
         if s2 is None:
             op("V", lambda: g.vector.tensor_scalar(o, i, s1, None, o0), r, w)
@@ -198,8 +278,8 @@ def rank_program(g, core, T, topo):
     def ms(o, c, w):
         op("V", lambda: g.vector.memset(o, c), [], w)
 
-    def scan(o, a, b, init, r, w):
-        op("V", lambda: g.vector.tensor_tensor_scan(o, a, b, init, ALU.add, ALU.add), r, w)
+    def scan(o, a, b, init, r, w, o0=ALU.add):
+        op("V", lambda: g.vector.tensor_tensor_scan(o, a, b, init, o0, ALU.add), r, w)
 
     def act(o, i, f, r, w, bias=0.0, scale=1.0):
         op("S", lambda: g.scalar.activation(o, i, f, bias=bias, scale=scale), r, w)
@@ -213,624 +293,597 @@ def rank_program(g, core, T, topo):
         else:
             op("G", lambda: g.iota(o, pat, base, cm), [], w)
 
-    Ib = T.Wb[:, 0:128]
-    rotb = T.Wb[:, 112:240]
-    rotf = T.Wf[:, 112:240]
+    def up_one(o, i):
+        return [(o(16, 128), i(0, 112)), (o(0, 16), i(112, 128))]
+
+    If, Ib, downb = T.Wf[:, 0:128], T.Wb[:, 0:128], T.Wb[:, 16:144]
     hs = [(0, 512), (512, 1024)]
-    ab = [2, 0]
-    Zs = [T.Z0, T.Z1, T.Z0, T.X1]
-    zk = ["Z0_%d", "Z1_%d", "Z0_%d", "Z3_%d"]
-    Xs = [T.X0, T.X1, T.X2]
+    Ys, Zs, Xs = [T.Y0, T.Y1], [T.Z0, T.Z1, T.Z0, T.Z2], [T.X0, T.X1, T.X2]
+    zn = ["Z0", "Z1", "Z0", "Z2"]
     els = [T.el0, T.el1]
     Pb = [T.P0, T.P1, T.P2, T.P3]
+    xb = [2, 0]
+    db = [2, 1]
+    part = [(0, 128, 3), (128, 256, 0)]
+    wk = ["winF%d" % c for c in range(4)]
+
+    def yk(t, c):
+        return "Y%d_%d" % (t % 2, c)
+
+    def zk(t, c):
+        return "%s_%d" % (zn[t], c)
+
+    def msg(t, k, a=0, b=MW, p0=0, p1=128):
+        c = MS * (4 * t + k)
+        return T.Mb[p0:p1, c + a:c + b]
+
+    def mkey(t, k):
+        return ["M%d_%do" % (t, k), "M%d_%dd" % (t, k)]
+
+    def made(t):
+        return 0 if t == 0 else reader(n, 0, t - 1)
+
+    def needed(t):
+        ks = [0, partner(n, 0, t)] + ([reader(n, 0, t)] if t < NB - 1 else [])
+        return [k for j, k in enumerate(ks) if k not in ks[:j]]
+
+    def send_lists(t):
+        mine = (rank + made(t)) % n
+        for k in needed(t):
+            if t > 0 and k == needed(t)[1]:
+                send_y(t - 1, 3)
+            if k != made(t):
+                remote(T.cores[(mine - k) % n], msg(t, k), msg(t, made(t)), "ma%d" % (4 * t + k), "ml", mkey(t, made(t)))
+                for key in mkey(t, k):
+                    lands(key, "ma%d" % (4 * t + k))
+
+    def send_y(t, c):
+        before("G", [yk(t, c)], [])
+        h, buf, col = plan(T, topo)["first"][rank, t, c]
+        rid, pid = topo.addr(h, core)
+        m = first_mask(T, topo, rank, t, c)
+        y = Ys[t % 2][:, B * c:B * c + B]
+        if (t, c) == LAST:
+            rid2, pid2 = topo.addr(T.cores[reader(n, rank, t)], core)
+            g.remote_dma_fused([RemoteDMATransfer(dst_ids=[DstId(rid=rid2, pnc=pid2)], dma_engine_mask=small, remote_sem=T.sem["xa%d" % t],
+                                                  src=y, dst=Xs[t % 3][:, B * c:B * c + B]),
+                                RemoteDMATransfer(dst_ids=[DstId(rid=rid, pnc=pid)], dma_engine_mask=m, remote_sem=T.sem["h%d" % (4 * t + c)],
+                                                  src=y, dst=T[buf][:, col:col + B])], local_sem=T.sem["xl%d" % t])
+            m |= small
+        else:
+            g.remote_dma(T[buf][:, col:col + B], y, T.sem["h%d" % (4 * t + c)], T.sem["xl%d" % t], pid, rid, m)
+        dcount["xl%d" % t] = dcount.get("xl%d" % t, 0) + bits(m)
+        if t == NB - 1:
+            for j in (2 * c, 2 * c + 1):
+                lastw[zk(t, j)] = ("ya%d" % c, bits(topo.mask(h, core)))
+        elif c == 2 and t > 0:
+            dcount["wa%d" % t] = bits(topo.mask(h, core))
+            for k in wk[:3]:
+                lastw[k] = ("wa%d" % t, dcount["wa%d" % t])
+                readers[k] = []
+        if c == 3:
+            for j in range(4):
+                readers[yk(t, j)].append(("xl%d" % t, dcount["xl%d" % t]))
+            lastw["X%d" % (t % 3)] = ("xa%d" % t, arrivals(T, topo, partner(n, rank, t), t))
+            readers["X%d" % (t % 3)] = []
+
+    def onsets(t):
+        k = made(t)
+        calls = [(T.P3[:, 0:66], T.U1[:], T.Dh[:, 1:67], True, False), (T.P3[:, 0:66], T.U2[:], T.Dh[:, 0:66], False, True)]
+        if t == 0:
+            mm(calls, ["U1", "U2", "Dh", "Dh0"], ["P3"])
+            cp(msg(t, k, 0, 66), T.P3[:, 0:66], ["P3"], [mkey(t, k)[0]])
+        else:
+            calls += [(T.P3[:, 66:MW], If, T.Dh[:, 1:65], True, False), (T.P3[:, 66:MW], T.nIf[:], T.Dh[:, 0:64], False, True)]
+            mm(calls, ["U1", "U2", "Wf", "nIf", "Dh", "Dh0"], ["P3"])
+            cp(msg(t, k), T.P3[:, 0:MW], ["P3"], mkey(t, k))
+
+    def vote_lists(t, step):
+        k = reader(n, 0, t)
+        ko, kd = mkey(t, k)
+        if step == -1:
+            dma("Y", up_one(lambda a, b: T.Mq[a:b, :], lambda a, b: msg(t, k, 0, 64, a, b))
+                + up_one(lambda a, b: T.Mr[a:b, :], lambda a, b: msg(t, 0, 0, 64, a, b)), [ko, mkey(t, 0)[0]], ["Mq", "Mr"])
+        elif step == 0:
+            ts(T.lv[:, 0:64], msg(t, k, 0, 64), float(S), 4.0, ALU.is_lt, ALU.mult, [ko], ["lv"])
+            cp(T.df[:, 0:64], msg(t, k, 66, MW), [kd], ["df"])
+        elif step == 1:
+            tt(T.dd[:], T.df[:, 0:64], T.lv[:, 0:64], ALU.mult, ["df", "lv"], ["dd"])
+            act(T.sq[:], T.dd[:], ACT.Abs, ["dd"], ["sq"], bias=-5.0, scale=0.25)
+            act(T.a2[:, 0:64], T.dd[:], ACT.Relu, ["dd"], ["a2"], bias=5.0, scale=-0.75)
+            act(T.bn[:], T.sq[:], ACT.Sign, ["sq"], ["bn"], bias=3.5, scale=-1.0)
+        elif step == 2:
+            ts(T.sof[:], T.Mq[:], float(S), None, ALU.min, None, ["Mq"], ["sof"])
+        else:
+            o = T.P3[:, 64:130]
+            mm([(o, If, T.df[:, 0:66], True, False), (o, If, T.a2[:, 0:66], False, False), (o, If, T.lv[:, 0:66], False, False),
+                (o, T.nIf[:], T.four[:, 0:66], False, True),
+                (T.P3[:, 0:64], If, T.bn[:], True, False)], ["Wf", "nIf", "df", "a2", "lv", "bn", "x66"], ["P3"])
+
+    def votes(t):
+        yw = Ys[t % 2][:, 0:S + 8]
+        yr = [yk(t, c) for c in range(4)] + ["Yz", "sof"]
+        for h, (a, b) in enumerate(hs):
+            o = T.sof[:, 32 * h:32 * h + 32]
+            tt(T.cmpb[:, a:b], yw.indirect(o), T.Al[:, B * t + a:B * t + b], ALU.is_gt, yr + ["Al%d" % t], ["cmp%d" % h])
+            act(T.Fb[:, a:b], yw.indirect(o), ACT.Identity, yr, ["Fb%d" % h], bias=191.5 + 2.0 ** -13, scale=2.0 ** -4)
+            mm([(T.P3[:, 32 * h:32 * h + 32], T.Vw[:, 16 - i:144 - i], T.cmpb[:, a + i:b:16], False, h == 1 and i == 15) for i in range(16)],
+               ["Vw", "cmp%d" % h], ["P3"])
+        before("G", ["Al%d" % t], [])
+        remote(T.cores[reader(n, rank, t)], T.Fl[:], T.Fb[:], "fa%d" % t, "fl", ["Fb0", "Fb1"])
+        lands("Fl", "fa%d" % t)
+        dead_list(t, 1)
+        if t > 0:
+            e_v(t - 1, 2)
+        if t > 1:
+            e_scatter(t, 0, 1)
+        act(T.up[:, 0:64], T.P3[:, 0:64], ACT.Sign, ["P3"], ["up"], bias=-1.0 - 8.5 / 32)
+        scan(T.Dh[:, 1:67], T.up[:, 0:66], T.P3[:, 64:130], 0.0, ["up", "x66", "P3"], ["Dh"])
+        onsets(t + 1)
+        send_lists(t + 1)
+
+    def dead_list(t, step):
+        if step == 0:
+            ts(T.t1[:], T.Mr[:], float(S), -2048.0, ALU.is_lt, ALU.mult, ["Mr"], ["t1"])
+            o = T.P0[:, 0:64]
+            mm([(o, If, T.t1[:], True, False), (o, If, T.bi[:], False, True)], ["Wf", "t1", "bi"], ["P0"])
+        else:
+            cp(T.jl[:], T.P0[:, 0:64], ["P0"], ["jl"])
+
+    def dead_v():
+        act(T.vD[:], T.uw[:, 0:1040].indirect(T.jl[:]), ACT.Identity, ["uw0", "uw1", "uwz", "jl"], ["vD"])
+
+    def open_y(h):
+        a, b = hs[h]
+        mm([(Pb[h][:], Ib, T.uw[:, 16 + a:16 + b], True, False), (Pb[h][:], T.n192[:], T.ob[:, 0:512], False, False)],
+           ["Wb", "n192", "ob", "uw%d" % h], ["P%d" % h])
+
+    def open_x(h):
+        a, b = hs[h]
+        o = Pb[xb[h]][:]
+        mm([(o, Ib, T.Aa[:, a:b], True, False), (o, T.nI[:, 0:128], T.vD[:, a:b], False, False)],
+           ["Wb", "nI", "Aa%d" % h, "vD"], ["P%d" % xb[h]])
+
+    def close_y(h):
+        a, b = hs[h]
+        mm([(Pb[h][:], Ib, T.Fl[:, a:b], False, True)], ["Wb", "Fl"], ["P%d" % h])
+
+    def cut_v(h):
+        a, b = hs[h]
+        ts(T.uw[:, 16 + a:16 + b], Pb[h][:], -64.0, 64.0, ALU.max, ALU.min, ["P%d" % h], ["uw%d" % h])
+
+    def close_x(h):
+        a, b = hs[h]
+        mm([(Pb[xb[h]][:], Ib, T.uw[:, 16 + a:16 + b], False, True)], ["Wb", "uw%d" % h], ["P%d" % xb[h]])
+
+    def mirror(h):
+        a, b = hs[h]
+        w = T.dlt[:, 2048 + a:2048 + b]
+        act(w, Pb[xb[h]][:], ACT.Abs, ["P%d" % xb[h]], ["w%d" % h] + (["dlt2"] if h == 0 else []), bias=256.0)
+        act(w, w, ACT.Abs, ["w%d" % h], ["w%d" % h], bias=512.0, scale=-1.0)
+        act(T.Aa[:, a:b], w, ACT.Identity, ["w%d" % h], ["Aa%d" % h], bias=256.0, scale=-1.0)
+
+    def send_a(t):
+        remote(T.cores[partner(n, rank, t)], T.Al[:, B * t:B * t + B], T.Aa[:, 0:B], "aa%d" % t, "al", ["Aa0", "Aa1"])
+        lands("Al%d" % t, "aa%d" % t)
+
+    def ends():
+        act(T.Aa[:, 1024:1025], T.Aa[:, 0:1], ACT.Copy, ["Aa0"], ["Aaw"])
+
+    def down_a(h):
+        a, b = hs[h]
+        mm([(Pb[1 - h][:], downb, T.Aa[:, a:b], True, True)], ["Wb", "Aa%d" % h], ["P%d" % (1 - h)])
+
+    def levels(h):
+        a, b = hs[h]
+        act(T.tab[:, K + 1 + a:K + 1 + b], Pb[1 - h][:], ACT.Copy, ["P%d" % (1 - h), "w0", "w1"], ["tabA%d" % h] + (["dlt2"] if h else []))
+        if h == 0:
+            act(T.tab[:, K + 1025:K + 1026], T.P1[:, 0:1], ACT.Copy, ["P1"], ["tabA2"])
+
+    def rate(t, h):
+        a, b = hs[h]
+        act(T.RE[:, a:b], T.coef[:, 0:16].indirect(msg(t, 0, 66 + 32 * h, 98 + 32 * h)), ACT.Identity, ["coef", mkey(t, 0)[1]], ["RE%d" % h])
+
+    def da(h):
+        a, b = hs[h]
+        o = Pb[db[h]][:]
+        mm([(o, downb, T.Aa[:, a + 1:b + 1], True, False), (o, T.nI[:, 16:144], T.Aa[:, a:b], False, True)],
+           ["Wb", "nI", "Aa0", "Aa1"] + (["Aaw"] if h else []), ["P%d" % db[h]])
+
+    def slope(h):
+        a, b = hs[h]
+        tt(T.tab[:, 1 + a:1 + b], Pb[db[h]][:], T.RE[:, a:b], ALU.mult, ["P%d" % db[h], "RE%d" % h], ["tabs%d" % h])
+
+    def scatter_f(t):
+        cp(T.winF[:, 0:WIN].indirect(msg(t, 0, 0, 65)), T.zb[:, 0:1040], [mkey(t, 0)[0], "zb", "zbx"], wk)
+
+    def w_mm(c):
+        a, b, k = part[c]
+        mm([(Pb[k][:, 0:b - a], T.Sw[:, 16 - i:144 - i], T.winF[:, 16 * a + i:16 * b:16], i == 0, i == 15) for i in range(16)],
+           ["Sw"] + wk, ["P%d" % k])
+
+    def h_scan(c):
+        a, b, k = part[c]
+        scan(T.H[:, 8 + a:8 + b], Pb[k][:, 0:b - a], T.ob[:, 0:b - a], T.H[:, 7 + a:8 + a],
+             ["P%d" % k, "ob0", "H%d" % (c - 1) if c else "Hz"], ["H%d" % c])
+
+    def i_mm(c):
+        a, b, k = part[c]
+        o = Pb[k][:, b - a:2 * (b - a)]
+        h1, h0 = T.H[:, 8 + a:8 + b], T.H[:, 7 + a:7 + b]
+        mm([(o, T.M1[:], h1, True, False), (o, T.KI[:], h1, False, False), (o, T.M2[:], h0, False, True)],
+           ["M1", "KI", "M2", "H%d" % c, "H%d" % (c - 1) if c else "Hz"], ["P%d" % k])
+
+    def i_cp(c):
+        a, b, k = part[c]
+        cp(T.idx[:, a:b], Pb[k][:, b - a:2 * (b - a)], ["P%d" % k], ["idx%d" % c])
+
+    def delta(c):
+        act(T.dlt[:, B * (c % 3):B * (c % 3) + B], T.tab[:, 0:2064].indirect(T.idx[:, 64 * c:64 * c + 64]), ACT.Identity,
+            ["tabz", "tabA0", "tabA1", "tabA2", "tabs0", "tabs1", "idx%d" % (c // 2)], ["dlt%d" % (c % 3)])
+
+    def y_scan(t, c):
+        a, b = B * c, B * c + B
+        y = Ys[t % 2]
+        init = 0.0 if c == 0 else y[:, a - 1:a]
+        scan(y[:, a:b], T.winF[:, a:b], T.dlt[:, B * (c % 3):B * (c % 3) + B], init,
+             ["dlt%d" % (c % 3), wk[c]] + ([yk(t, c - 1)] if c else []), [yk(t, c)], ALU.mult)
+        if c < 3 or t == NB - 1:
+            send_y(t, c)
+        elif t > 0:
+            dma("Y", [(T.winF[:, a:b], T.ob[:])], ["ob"], [wk[c]])
+
+    def e_digits(t, step):
+        k = partner(n, 0, t)
+        if step == 0:
+            cp(T.pf[:], msg(t, k, 0, 64), [mkey(t, k)[0]], ["pf"])
+        elif step == 1:
+            cp(T.pd[:, 0:64], T.pf[:], ["pf"], ["pda"])
+        else:
+            tt(T.pd[:, 64:128], T.pf[:], T.pd[:, 0:64], ALU.subtract, ["pf", "pda"], ["pdb"])
+            dma("Y", [pair for r in range(2) for pair in ((T.Pwin[r:112:16, :], T.pd[16:128, 64 * r:64 * r + 64]),
+                                                          (T.Pwin[112 + r:113 + r, :], T.pd[0:16, 64 * r:64 * r + 64]))],
+                ["pda", "pdb"], ["Pwin"])
+
+    def durations(t):
+        act(T.Dg[:], T.dtab[:, 0:16].indirect(msg(t, 0, 66, MW)), ACT.Identity, ["dtab", mkey(t, 0)[1]], ["Dg"])
+
+    def e_source():
+        act(T.srcE[:], T.Pwin[:, 0:1024].indirect(T.ml[:]), ACT.Identity, ["Pwin", "ml"], ["srcE"])
+        dma("Y", [(T.srcE[3:128:16, 1:1024], T.srcE[0:128:16, 0:1023]), (T.srcE[4:128:16, 1:1024], T.srcE[1:128:16, 0:1023]),
+                  (T.srcE[2:128:16, 1:1024], T.Dg[0:128:16, 0:1023])], ["Dg"], ["srcE"])
+
+    def e_scatter(t, h0=0, h1=2):
+        cp(T.winE[:, 0:WIN].indirect(msg(t, 0, 32 * h0, 32 * h1)), T.srcE[:, 512 * h0:512 * h1], [mkey(t, 0)[0], "srcE"], ["winE"])
+
+    def e_w(t):
+        s = 32 if t < NB - 1 else 16
+        mm([(T.P3[:, 256:512], T.SE[:, s - i:s + 128 - i], T.winE[:, i:S:16], i == 0, i == 15) for i in range(16)], ["SE", "winE"], ["P3"])
+        if t < NB - 1:
+            dma("Y", [(T.winE[r:128:16, 0:S], T.winE[8 + r:128:16, 0:S]) for r in range(5)], [], ["winE"])
+
+    def e_s():
+        scan(T.HE[:, 1:257], T.P3[:, 256:512], T.c101[:], T.HE[:, 0:1], ["P3", "c101", "HE0"], ["HE"])
+
+    def e_c():
+        for k in (1, 2):
+            o = Pb[k][:, 0:256]
+            mm([(o, T.Tle[:], T.HE[:, 1:257], True, False), (o, T.Tgt[:], T.HE[:, 0:256], False, k == 1)], ["Tle", "Tgt", "HE", "HE0"],
+               ["P%d" % k])
+
+    def e_v(t, k):
+        if k == 0:
+            act(T.qb[:], T.P1[:, 0:256], ACT.Identity, ["P1"], ["qb"], bias=-0.5 + 2.0 ** -13, scale=2.0 ** -12)
+        elif k == 1:
+            mm([(T.P2[:, 0:256], T.n4096[:], T.qb[:], False, True)], ["n4096", "qb"], ["P2"])
+        else:
+            cp(els[t % 2][:], T.P2[:, 0:256], ["P2"], ["el%d" % (t % 2)])
+
+    def z(t, c, w=2):
+        y, key = (Ys[t % 2], yk(t, c // 2)) if t < NB - 1 else (Zs[t], zk(t, c))
+        tt(Zs[t][:, 512 * c:512 * (c + w)], Xs[t % 3][:, 0:S].indirect(els[t % 2][:, 32 * c:32 * (c + w)]), y[:, 512 * c:512 * (c + w)],
+           ALU.mult, ["X%d" % (t % 3), "el%d" % (t % 2), key], [zk(t, j) for j in range(c, c + w)])
+
+    def tanh(t, c, w=2):
+        o = Zs[t][:, 512 * c:512 * (c + w)]
+        ks = [zk(t, j) for j in range(c, c + w)]
+        act(o, o, ACT.Tanh, ks, ks, scale=2.0 ** -14)
+
+    summed = [0] * 4
+
+    def fold(t, c, w=2):
+        o = Zs[t]
+        a, b = 512 * c, 512 * (c + w)
+        dma("G", [(o[:, a:b], o[:, L + a:L + b])], [zk(t, j + 4) for j in range(c, c + w)], [zk(t, j) for j in range(c, c + w)],
+            accum_op=ALU.add)
+        for j in range(c, c + w):
+            summed[j] += 1
+
+    def out_mm(t, c, w=2):
+        for j in range(c, c + w):
+            summed[j % 4] += 1
+            k = "acc%d" % (j % 4)
+            mm([(T[k][:], T.Gm[:, 128 * t:128 * t + 128], Zs[t][:, 512 * j:512 * j + 512], k not in lastw, summed[j % 4] == 2 * NB)],
+               ["Gm%d" % t, zk(t, j)], [k])
+
+    def scale(t, c):
+        o = Zs[t][:, 512 * c:512 * c + 512]
+        act(o, o, ACT.Copy, [zk(t, c), "gn"], [zk(t, c)], scale=T.gn[:, t:t + 1])
+
+    def store(c, more):
+        o = T.Y0[:, 512 * c:512 * c + 512]
+        tt(o, T["acc%d" % c][:], Zs[more][:, 512 * c:512 * c + 512], ALU.add, ["acc%d" % c, zk(more, c)], ["out%d" % c, yk(0, c // 2)])
+        dma("Y", [(T.yo[:, 512 * c:512 * c + 512], o)], ["out%d" % c], ["yo%d" % c])
 
     dma("Y", [(T.dui[:], T.du[:])], [], ["dui"])
-    dma("S", [(T.Aa[:, 0:1024], T.am[:])], [], ["Aa0", "Aa1"])
-    iota(T.dtab[:], [[1, 16]], 0, 0, ["dtab"])
-    iota(T.smi[:, 0:1], [[1, 1]], 0, 1, ["smi0"], f=False)
-    ms(T.two[:], 2.0, ["two"])
-    ms(T.winF[:, 0:B], 0.0, ["winFa"])
-    dma("Y", [(T.winF[:, B * j:B * j + B], T.winF[:, 0:B]) for j in range(1, 4)], ["winFa"], ["winF"])
-    dma("Y", [(T.mpi[:], T.mp[:]), (T.gn[:], T.gain[:]), (T.uw[16:128, 16:1040], T.ve[0:112, :]), (T.uw[0:16, 16:1040], T.ve[112:128, :])],
-        [], ["mpi", "gn", "uw0", "uw1"])
-    sel(T.B2[:], T.two[:], [[-16, 8], [0, 16]], ALU.is_ge, 0.0, 0, 1, ["two"], ["B2"])
-    sel(T.B2[:], T.B2[:], [[16, 8], [0, 16]], ALU.is_ge, 0.0, 15, -1, ["B2"], ["B2"])
-    sel(T.U1[:, 16:144], T.B2[:], [[1, 128]], ALU.is_gt, 0.0, 0, -1, ["B2"], ["U1"])
-    sel(T.U2[:, 16:144], T.B2[:], [[-1, 128]], ALU.is_ge, 0.0, 0, 1, ["B2"], ["U2"])
-    ms(T.up[:], 0.0, ["up", "upx"])
-    ms(T.Dh[:, 0:1], 0.0, ["Dh0"])
-    ms(T.dh[:, 64:65], 0.5, ["dhx"])
+    dma("S", up_one(lambda a, b: T.Aa[a:b, 0:B], lambda a, b: T.am[a:b, :]), [], ["Aa0", "Aa1"])
+    dma("Y", [(T.mpi[:], T.mp[:]), (T.gn[:, 0:4], T.gain[:])] + up_one(lambda a, b: T.uw[a:b, 16:1040], lambda a, b: T.ve[a:b, :])
+        + up_one(lambda a, b: T.gn[a:b, 4:8], lambda a, b: T.gain[a:b, :]), [], ["mpi", "gn", "uw0", "uw1"])
     ms(T.one[:], 1.0, ["one"])
+    iota(T.dtab[:], [[1, 16]], 0, 0, ["dtab"])
+    ms(T.winF[:, 0:B], 1.0, wk[:1])
+    sel(T.B1[:], T.one[:], [[-16, 8], [0, 16]], ALU.is_ge, 0.0, 0, 1, ["one"], ["B1"])
+    sel(T.B1[:], T.B1[:], [[16, 8], [0, 16]], ALU.is_ge, 0.0, 15, -1, ["B1"], ["B1"])
+    sel(T.U1[:], T.B1[:], [[1, 128]], ALU.is_gt, 0.0, 0, -1, ["B1"], ["U1"])
+    sel(T.U2[:], T.B1[:], [[-1, 128]], ALU.is_ge, 0.0, 0, 1, ["B1"], ["U2"])
+    act(T.ob[:, 0:128], T.winF[:, 0:128], ACT.Tanh, wk[:1], ["ob0"], scale=16.0)
+    act(T.zb[:, 0:B], T.winF[:, 0:B], ACT.Copy, wk[:1], ["zb"], scale=0.0)
+    op("V", lambda: g.vector.reciprocal(T.sm[:, 0:9], T.dtab[:, 1:10]), ["dtab"], ["sma"])
+    ms(T.zb[:, 1024:1040], 1.0, ["zbx"])
     ms(T.coef[:], 0.0, ["coef"])
-    ms(T.srcF[:, 1024:1040], 0.0, ["srcF"])
+    ts(T.sm[:, 16:25], T.sm[:, 0:9], 256.0, -0.49, ALU.mult, ALU.add, ["sma"], ["smb"])
+    ms(T.up[:], 0.0, ["up", "x66"])
+    ms(T.zb[:, 1025:1026], 0.0, ["zbx"])
+    cp(T.smi[:, 4:13], T.sm[:, 16:25], ["smb"], ["smi2"])
+    ms(T.df[:, 64:66], 1.0, ["x66"])
+    ms(T.Dh[:, 0:1], 0.0, ["Dh0"])
+    ts(T.coef[:, 1:10], T.smi[:, 4:13], 1.0 / 256, None, ALU.mult, None, ["smi2"], ["coef"])
     ms(T.Sw[:], 0.0, ["Sw"])
-    ms(T.srcF[:, 1025:1026], 1.0, ["srcF"])
-    sel(T.Wf[:, 0:128], T.one[:], [[-1, 128]], ALU.is_equal, 0.0, 0, 1, ["one"], ["Wf0"])
-    sel(T.Sw[:, 16:144:16], T.Sw[:, 16:144:16], [[-16, 8]], ALU.not_equal, 1.0, 0, 1, ["Sw"], ["Sw"])
-    sel(T.Tle[:], T.B2[:], [[1, 128]], ALU.is_ge, 0.0, 0, -1, ["B2"], ["Tle"])
-    sel(T.Tgt[:], T.B2[:], [[-1, 128]], ALU.is_gt, 0.0, 0, 1, ["B2"], ["Tgt"])
-    sel(T.M2f[:], T.Tgt[:], [[-1, 128]], ALU.not_equal, -2.0 * K, 0, 1, ["Tgt"], ["M2f"])
-    act(T.srcF[:, 0:1024], T.Aa[:, 0:1024], ACT.Identity, ["Aa0", "Aa1"], ["srcFa"], bias=1.0, scale=0.0)
-    act(T.Wb[:, 0:128], T.Wf[:, 0:128], ACT.Copy, ["Wf0"], ["Wb0"])
-    act(T.nW[:, 0:128], T.Wf[:, 0:128], ACT.Copy, ["Wf0"], ["nI"], scale=-1.0)
-    act(T.U1[:, 0:16], T.U1[:, 128:144], ACT.Copy, ["U1"], ["U1r"])
-    act(T.U2[:, 0:16], T.U2[:, 128:144], ACT.Copy, ["U2"], ["U2r"])
-    act(T.Wf[:, 128:256], T.Wf[:, 0:128], ACT.Copy, ["Wf0"], ["Wf1"])
-    act(T.SE[:], T.Sw[:], ACT.Copy, ["Sw"], ["SE"])
+    ms(T.winF[:, B:2 * B], 1.0, wk[1:2])
+    cp(T.df[:, 0:64], T.dui[:], ["dui"], ["df"])
+    cp(msg(0, 0, 66, MW), T.dui[:], ["dui"], [mkey(0, 0)[1]])
+    scan(T.Dh[:, 1:67], T.up[:, 0:66], T.df[:, 0:66], 0.0, ["up", "x66", "df"], ["Dh"])
+    ms(T.winF[:, 2 * B:4 * B], 1.0, wk[2:])
+    sel(If, T.one[:], [[-1, 128]], ALU.is_equal, 0.0, 0, 1, ["one"], ["Wf"])
+    sel(T.Sw[:, 16:144:16], T.Sw[:, 16:144:16], [[-16, 8]], ALU.not_equal, -1.0, 0, 1, ["Sw"], ["Sw"])
+    sel(T.Tle[:], T.B1[:], [[1, 128]], ALU.is_ge, 0.0, 0, -1, ["B1"], ["Tle"])
+    sel(T.Tgt[:], T.B1[:], [[-1, 128]], ALU.is_gt, 0.0, 0, 1, ["B1"], ["Tgt"])
+    sel(T.one[:], T.Tgt[:], [[-1, 128]], ALU.not_equal, -1.0 * K, 0, 1, ["Tgt"], ["one"])
+    onsets(0)
+    scatter_f(0)
+    send_lists(0)
+    send_a(0)
+    ends()
+    rate(0, 0)
+    act(T.Wf[:, 128:144], T.Wf[:, 0:16], ACT.Copy, ["Wf"], ["Wf1"])
+    act(T.Wb[:], T.Wf[:], ACT.Copy, ["Wf", "Wf1"], ["Wb"])
+    act(T.nI[:], T.Wf[:], ACT.Copy, ["Wf", "Wf1"], ["nI"], scale=-1.0)
+    down_a(0)
+    down_a(1)
+    rate(0, 1)
+    levels(0)
+    levels(1)
+    act(T.KI[:], If, ACT.Copy, ["Wf"], ["KI"], scale=float(K))
+    act(T.M1[:], T.Tle[:], ACT.Copy, ["Tle"], ["M1"])
+    act(T.M2[:], T.one[:], ACT.Copy, ["one"], ["M2"])
+    act(T.H[:, 0:8], T.Aa[:, 0:8], ACT.Copy, ["Aa0"], ["Hz"], scale=0.0)
+    for a, b in ((0, 1), (1025, K + 1), (K + 1026, 2064)):
+        act(T.tab[:, a:b], T.Aa[:, 0:b - a], ACT.Copy, ["Aa0"], ["tabz"], scale=0.0)
+    dma("Y", [(T.Pwin[:], T.zb[:, 0:B])] + [(T.winE[:, B * j:B * j + B], T.zb[:, 0:B]) for j in range(4)], ["zb"], ["Pwin", "winE"])
+    iota(T.smi[:, 0:1], [[1, 1]], 0, 1, ["smi0"], f=False)
     iota(T.bi[:], [[16, 64]], 16, 0, ["bi"])
-    for r, w in ((1, 1.0), (2, -101.0), (3, -1.0), (4, -1.0)):
-        sel(T.SE[:, 16:144:16], T.SE[:, 16:144:16], [[-16, 8]], ALU.not_equal, w, -r, 1, ["SE"], ["SE"])
+    sel(T.SE[:], T.zb[:, 0:160], [[0, 160]], ALU.is_gt, 0.0, 0, 0, ["zb"], ["SE"])
+    for r, w in ((0, 1.0), (1, 1.0), (2, -101.0), (3, -1.0), (4, -1.0)):
+        sel(T.SE[:, 32:160:16], T.SE[:, 32:160:16], [[-16, 8]], ALU.not_equal, w, -r, 1, ["SE"], ["SE"])
 
-    def more_constants():
-        act(T.KI[:], T.Wf[:, 0:128], ACT.Copy, ["Wf0"], ["KI"], scale=float(K))
-        act(T.M1[:], T.Tle[:], ACT.Copy, ["Tle"], ["M1"], scale=0.5)
-        act(T.M2[:], T.M2f[:], ACT.Copy, ["M2f"], ["M2"], scale=0.5)
-        act(T.zb[:], T.Aa[:, 0:1024], ACT.Copy, ["Aa0", "Aa1"], ["zb"], scale=0.0)
-        dma("Y", [(T.Pwin[:], T.zb[:])] + [(T.winE[:, 1024 * j:1024 * j + 1024], T.zb[:]) for j in range(4)], ["zb"], ["Pwin", "winE"])
+    def late_s():
+        act(T.nIf[:], If, ACT.Copy, ["Wf"], ["nIf"], scale=-1.0)
+        act(T.n192[:], If, ACT.Copy, ["Wf"], ["n192"], scale=-192.0)
+        act(T.Vw[:], T.Sw[:], ACT.Copy, ["Sw"], ["Vw"], scale=0.0)
+        act(T.Vw[:, 16:128:16], T.B1[:, 16:128:16], ACT.Copy, ["B1"], ["Vw"], scale=1.0 / 32)
+        act(T.Vw[:, 128:129], T.B1[:, 0:1], ACT.Copy, ["B1"], ["Vw"], scale=1.0 / 32)
 
-    def factors():
-        dd, a, b = T.dtab[:, 1:10], T.sm[:, 0:9], T.sm[:, 16:25]
-        op("V", lambda: g.vector.reciprocal(a, dd), ["dtab"], ["sma"])
-        ts(T.smi[:, 1:2], T.smi[:, 0:1], 15, None, ALU.bitwise_and, None, ["smi0"], ["smi1"])
-        ts(b, a, 256.0, -0.49, ALU.mult, ALU.add, ["sma"], ["smb"])
-        cp(T.sm[:, 32:33], T.smi[:, 1:2], ["smi1"], ["pm"])
-        cp(T.smi[:, 4:13], b, ["smb"], ["smi2"])
-        ts(T.sm[:, 33:34], T.sm[:, 32:33], 14.0, 10.0, ALU.max, ALU.mult, ["pm"], ["ecol"])
-        ts(T.coef[:, 1:10], T.smi[:, 4:13], 1.0 / 256, None, ALU.mult, None, ["smi2"], ["coef"])
-        tt(a, T.coef[:, 1:10], dd, ALU.mult, ["coef", "dtab"], ["sma"])
-        ts(T.coef[:, FB + 1:FB + 10], a, -1.0, 1.0, ALU.mult, ALU.add, ["sma"], ["coefF"])
-        tt(T.coef[:, EB + 1:EB + 10], T.coef[:, FB + 1:FB + 10], T.coef[:, 1:10], ALU.add, ["coefF", "coef"], ["coef"])
-
-    def late_a():
-        ts(T.ib[:, 128:192], T.mpi[:], 15, None, ALU.bitwise_and, None, ["mpi"], ["ib1"])
-        ts(T.ib[:, 0:64], T.mpi[:], 4, None, ALU.arith_shift_right, None, ["mpi"], ["ib0"])
-        ts(T.t1[:], T.ib[:, 128:192], 64.0, None, ALU.mult, None, ["ib1"], ["t1"])
-        cp(T.t2[:], T.ib[:, 0:64], ["ib0"], ["t2"])
-        tt(T.t3[:], T.t1[:], T.t2[:], ALU.add, ["t1", "t2"], ["t3"])
-
-    def late_b():
-        calls = []
-        for s in range(1, 5):
-            lh = T.Wf[:, 128 - 16 * s:256 - 16 * s]
-            calls.append((T.P0[:, 64 * (s - 1):64 * s], lh, T.t3[:], True, True))
-            calls.append((T.P0[:, 256 + 4 * (s - 1):256 + 4 * s], lh, T.gn[:], True, True))
-        mm(calls, ["Wf0", "Wf1", "t3", "gn"], ["P0"])
-
-    def late_b2():
-        cp(T.ml[:], T.P0[:, 0:256], ["P0"], ["ml"])
-        cp(T.sm[:, 40:56], T.P0[:, 256:272], ["P0"], ["grot"])
-
-    def late_c():
-        ms(T.uw[:, 0:16], 0.0, ["uwz"])
-        ts(T.bi[:], T.bi[:], T.sm[:, 32:33], None, ALU.add, None, ["bi", "pm"], ["bi"])
-
-    def weights():
-        act(T.Vw[:], T.Sw[:], ACT.Copy, ["Sw"], ["Vw"])
-        act(T.Vw[:, 16:144:16], T.B2[:, 0:128:16], ACT.Copy, ["B2"], ["Vw"], scale=0.5)
-
-    def late_d():
-        act(T.Wb[:, 128:256], T.Wf[:, 0:128], ACT.Copy, ["Wf0"], ["Wb1"])
-        act(T.nW[:, 128:256], T.Wf[:, 0:128], ACT.Copy, ["Wf0"], ["nW1"], scale=-1.0)
+    def gains():
+        act(T.n4096[:], If, ACT.Copy, ["Wf"], ["n4096"], scale=-float(S))
+        act(T.SE[:, 16:17], T.SE[:, 144:145], ACT.Copy, ["SE"], ["SE"])
         for t in range(NB):
-            s = t + 1
-            act(T.Gm[:, 128 * t:128 * t + 128], T.Wf[:, 16 * s:16 * s + 128], ACT.Copy, ["Wf0", "Wf1", "grot"], ["Gm%d" % t],
-                scale=T.sm[:, 40 + 5 * t:41 + 5 * t])
-        act(T.p2[:], T.Wf[:, 0:128], ACT.Copy, ["Wf0"], ["p2"], scale=2.0)
-        act(T.n2[:], T.Wf[:, 0:128], ACT.Copy, ["Wf0"], ["n2"], scale=-2.0)
-        act(T.Tle[:], T.Tle[:], ACT.Copy, ["Tle"], ["Tle"], scale=0.5)
-        act(T.Tgt[:], T.Tgt[:], ACT.Copy, ["Tgt"], ["Tgt"], scale=0.5)
-        ms(T.c101[:], 101.0, ["c101"])
-        ms(T.HE[:, 0:1], 0.0, ["HE0"])
-        ms(T.dn[:, 64:65], 0.5, ["dnx"])
-        for x in range(3):
-            ms(Xs[x][:, S:S + 8], 0.0, ["Xz%d" % x])
+            s = 16 * (t == NB - 1)
+            act(T.Gm[:, 128 * t:128 * t + 128], T.Wf[:, s:s + 128], ACT.Copy, ["Wf", "Wf1", "gn"], ["Gm%d" % t],
+                scale=T.gn[:, t + s // 4:t + s // 4 + 1])
 
-    def arrived(t):
-        lastw["X%d" % (t % 3)] = ("xa%d" % t, arrivals(T, topo, (rank + 1 + t % (n - 1)) % n, t, 1, 5))
-        readers["X%d" % (t % 3)] = []
-
-    def send(t, j):
-        dst = route(T, topo, rank, t)[1]
-        loc = ("pl%d" if j == 0 else "xl%d") % t
-        trs = []
-        for a, b, h, m, k in pieces(T, topo, rank, t)[j]:
-            rid, pid = topo.addr(dst if h is None else h, core)
-            if j == 0:
-                o, i = T.pl[:, 128 * t + a:128 * t + b], T.pd[:, 128 * t + a:128 * t + b]
-            else:
-                o, i = T["X%d" % (t % 3) if h is None else STOP[t]][:, a:b], T.Y[:, a:b]
-            sem = T.sem[(("pa%d" if j == 0 else "xa%d") % t) if h is None else "h%d" % (3 * t + k)]
-            trs.append((o, i, sem, rid, pid, m))
-            dcount[loc] = dcount.get(loc, 0) + bits(m)
-        if len(trs) == 1:
-            o, i, sem, rid, pid, m = trs[0]
-            g.remote_dma(o, i, sem, T.sem[loc], pid, rid, m)
+    def late_v(step):
+        if step == 0:
+            ms(T.lv[:, 64:66], 4.0, ["x66"])
+            ms(T.four[:], 4.0, ["x66"])
+            ms(T.a2[:, 64:66], 0.0, ["x66"])
+            ms(T.Y0[:, S:S + 8], 0.0, ["Yz"])
+            ms(T.Y1[:, S:S + 8], 0.0, ["Yz"])
+            ms(T.uw[:, 0:16], 0.0, ["uwz"])
+            ts(T.smi[:, 1:2], T.smi[:, 0:1], 15, None, ALU.bitwise_and, None, ["smi0"], ["smi1"])
+            ts(T.ia[:, 64:128], T.mpi[:], 15, None, ALU.bitwise_and, None, ["mpi"], ["ia1"])
+            ts(T.ia[:, 0:64], T.mpi[:], 4, None, ALU.arith_shift_right, None, ["mpi"], ["ia0"])
+            cp(T.sm[:, 30:31], T.smi[:, 1:2], ["smi1"], ["pm"])
         else:
-            g.remote_dma_fused([RemoteDMATransfer(dst_ids=[DstId(rid=rid, pnc=pid)], dma_engine_mask=m, remote_sem=sem, src=i, dst=o)
-                                for o, i, sem, rid, pid, m in trs], local_sem=T.sem[loc])
-
-    def z_chunk(t, c, w=1):
-        z = Zs[t][:, 512 * c:512 * (c + w)]
-        ks = [zk[t] % j for j in range(c, c + w)]
-        tt(z, Xs[t % 3][:, 0:S].indirect(els[t % 2][:, 32 * c:32 * (c + w)]), z, ALU.mult,
-           ["X%d" % (t % 3), "el%d_%d" % (t % 2, c // 4)] + ks, ks)
-
-    def tanh_chunk(t, c0, c1):
-        z = Zs[t][:, 512 * c0:512 * c1]
-        ks = [zk[t] % c for c in range(c0, c1)]
-        act(z, z, ACT.Tanh, ks, ks, scale=2.0 ** -14)
-
-    def fold(t, c0, c1):
-        z = Zs[t]
-        dma("G", [(z[:, 512 * c0:512 * c1], z[:, L + 512 * c0:L + 512 * c1])],
-            [zk[t] % (c + 4) for c in range(c0, c1)], [zk[t] % c for c in range(c0, c1)], accum_op=ALU.add)
-
-    def out_mm(t, c, col=None):
-        col = c if col is None else col
-        mm([(T["acc%d" % c][:], T.Gm[:, 128 * t:128 * t + 128], Zs[t][:, 512 * col:512 * col + 512], t == 0, t == NB - 1)],
-           ["Gm%d" % t, zk[t] % col], ["acc%d" % c])
-
-    def e_w(t, h):
-        mm([(Pb[h][:, 0:128], T.SE[:, 16 - i:144 - i], T.winE[:, L * h + i:L * h + L:16], i == 0, i == 15) for i in range(16)],
-           ["SE", "winE"], ["P%d" % h])
-        if h == 1 and t < NB - 1:
-            dma("Y", [(T.winE[r:128:16, 0:S], T.zb[:, 0:256]) for r in range(5)], ["zb"], ["winE"])
-
-    def e_s(t, h):
-        a = 128 * h
-        scan(T.HE[:, 1 + a:129 + a], Pb[h][:, 0:128], T.c101[:, 0:128], T.HE[:, a:a + 1], ["P%d" % h, "c101", "HE%d" % h], ["HE%d" % (h + 1)])
-
-    def e_c(t, h):
-        a = 128 * h
-        mm([(Pb[h][:, 128:256], T.Tle[:], T.HE[:, 1 + a:129 + a], True, False), (Pb[h][:, 128:256], T.Tgt[:], T.HE[:, a:128 + a], False, True)],
-           ["Tle", "Tgt", "HE%d" % h, "HE%d" % (h + 1)], ["P%d" % h])
-
-    def e_v(t, h, k):
-        a = 128 * h
-        if k == 0:
-            ts(T.ia[:, a:a + 128], Pb[h][:, 128:256], -101.0, None, ALU.add, None, ["P%d" % h], ["ia%d" % h])
-        elif k == 1:
-            ts(T.ib[:, a:a + 128], T.ia[:, a:a + 128], S - 1, None, ALU.bitwise_and, None, ["ia%d" % h], ["ib%d" % h])
-        else:
-            cp(els[t % 2][:, a:a + 128], T.ib[:, a:a + 128], ["ib%d" % h], ["el%d_%d" % (t % 2, h)])
+            ts(T.t1[:], T.ia[:, 64:128], 64.0, None, ALU.mult, None, ["ia1"], ["t1"])
+            ts(T.bi[:], T.bi[:], T.sm[:, 30:31], None, ALU.add, None, ["bi", "pm"], ["bi"])
+            tt(T.t2[:], T.t1[:], T.ia[:, 0:64], ALU.add, ["t1", "ia0"], ["t2"])
+            ms(T.c101[:], 101.0, ["c101"])
+            cp(T.ml[:], T.t2[:], ["t2"], ["ml"])
+            ts(T.HE[:, 0:1], T.sm[:, 30:31], 0.0, 136.0 * S - 101.0, ALU.is_equal, ALU.mult, ["pm"], ["HE0"])
 
     for t in range(NB):
-        if t == 0:
-            ts(T.dh[:, 0:64], T.dui[:], 0.5, None, ALU.mult, None, ["dui"], ["dh"])
-            scan(T.Dh[:, 1:66], T.dh[:, 0:65], T.up[:, 0:65], 0.0, ["dh", "dhx", "up"], ["Dh"])
-        else:
-            arrived(t - 1)
-            xk = "X%d" % ((t - 1) % 3)
-            xw = Xs[(t - 1) % 3][:, 0:S + 8]
-            xr = [xk, "Xz%d" % ((t - 1) % 3), "sof"]
-            tt(T.cmpb[:], xw.indirect(T.sof[:]), T.Ar[:], ALU.is_gt, xr + ["Ar"], ["cmpb"])
-            for h, (a, b) in enumerate(hs):
-                act(T.Fb[:, a:b], xw.indirect(T.sof[:, 32 * h:32 * h + 32]), ACT.Identity, xr, ["Fb%d" % h],
-                    bias=191.5 + 2.0 ** -13, scale=2.0 ** -4)
-
-            def x1(h):
-                a, b = hs[h]
-                mm([(Pb[h][:], Ib, T.Fb[:, a:b], False, True)], ["Wb0", "Fb%d" % h], ["P%d" % h])
-
-            def ucut(h):
-                a, b = hs[h]
-                ts(T.gg[:, a:b], Pb[h][:], -64.0, 64.0, ALU.max, ALU.min, ["P%d" % h], ["gg%d" % h])
-
-            def xsum(h):
-                a, b = hs[h]
-                mm([(Pb[h][:], Ib, T.Ar[:, a:b], True, False), (Pb[h][:], Ib, T.gg[:, a:b], False, True)],
-                   ["Wb0", "Ar", "gg%d" % h], ["P%d" % h])
-
-            def mirror(h):
-                a, b = hs[h]
-                act(T.ov[:, a:b], Pb[h][:], ACT.Relu, ["P%d" % h], ["ov%d" % h], bias=-256.0)
-                act(T.un[:, a:b], Pb[h][:], ACT.Relu, ["P%d" % h], ["un%d" % h], bias=-256.0, scale=-1.0)
-                k = ab[h]
-                mm([(Pb[k][:], T.n2[:], T.ov[:, a:b], False, False), (Pb[k][:], T.p2[:], T.un[:, a:b], False, True)],
-                   ["n2", "p2", "ov%d" % h, "un%d" % h], ["P%d" % k])
-
-            def xopen(h):
-                a, b = hs[h]
-                k = ab[h]
-                mm([(Pb[k][:], Ib, T.Ar[:, a:b], True, False), (Pb[k][:], Ib, T.gg[:, a:b], False, False)],
-                   ["Wb0", "Ar", "gg%d" % h], ["P%d" % k])
-
-            x1(0)
-            x1(1)
-            mm([(T.P3[:, 0:64], T.Vw[:, 16 - i:144 - i], T.cmpb[:, i:B:16], i == 0, i == 15) for i in range(16)],
-               ["Vw", "cmpb"], ["P3"])
-            ucut(0)
-            ucut(1)
-            xsum(0)
-            tt(T.up[:, 0:64], T.P3[:, 0:64], T.thr[:], ALU.is_ge, ["P3", "thr"], ["up"])
-            scan(T.Dh[:, 1:66], T.up[:, 0:65], T.dn[:, 0:65], 0.0, ["up", "upx", "dn", "dnx"], ["Dh"])
-        mm([(T.P3[:, 0:65], T.U1[:, 16:144], T.Dh[:, 1:66], True, False), (T.P3[:, 0:65], T.U2[:, 16:144], T.Dh[:, 0:65], False, True)],
-           ["U1", "U2", "Dh", "Dh0"], ["P3"])
-        if t == 0:
-            factors()
-        else:
-            xsum(1)
-            xopen(0)
-            tt(T.dh[:, 0:64], T.up[:, 0:64], T.dn[:, 0:64], ALU.add, ["up", "dn"], ["dh"])
-        ts(T.dls[:, 0:64], T.dh[:, 0:64], 2.0, None, ALU.mult, None, ["dh"], ["dlsa"])
-        cp(T.of0[:, 0:65], T.P3[:, 0:65], ["P3"], ["of0"])
-
-
-        def jump_lists():
-            ts(T.dls[:, 64:127], T.dh[:, 0:63], 2.0, float(EB), ALU.mult, ALU.add, ["dh"], ["dlsb"])
-            ts(T.dls[:, 127:128], T.dh[:, 63:64], 2.0, T.sm[:, 33:34], ALU.mult, ALU.add, ["dh", "ecol"], ["dlsc"])
-
-        if t == 0:
-            jump_lists()
-        cp(T.winF[:, 0:WIN].indirect(T.of0[:, 0:65]), T.srcF[:], ["of0", "srcF", "srcFa"], ["winF", "winFa"])
-        if t > 0:
-            jump_lists()
-            mirror(0)
-            xopen(1)
-            mirror(1)
-        mm([(T.P3[:, 128:192], T.U1[:, 0:128], T.Dh[:, 1:65], True, False), (T.P3[:, 128:192], T.U2[:, 0:128], T.Dh[:, 0:64], False, True),
-            (T.P3[:, 192:256], rotf, T.dh[:, 0:64], True, True)],
-           ["U1", "U2", "U1r", "U2r", "Dh", "Dh0", "Wf0", "Wf1", "dh"], ["P3"])
-        cw = T.coef[:, 0:160]
-
-        def rea(h):
-            a, b = hs[h]
-            act(T.RE[:, a:b], cw.indirect(T.dls[:, 32 * h:32 * h + 32]), ACT.Identity, ["coef", "coefF", "dlsa"], ["REa%d" % h])
-
-        def reb(h, q="S"):
-            a, b = hs[h]
-            o, i, r = T.RE[:, 1024 + a:1024 + b], cw.indirect(T.dls[:, 64 + 32 * h:96 + 32 * h]), ["coef", "coefF", "dlsb", "dlsc"]
-            if q == "S":
-                act(o, i, ACT.Identity, r, ["REb%d" % h])
-            else:
-                cp(o, i, r, ["REb%d" % h])
-
-        def ends():
-            act(T.Aa[:, 1024:1025], T.Aa[:, 0:1], ACT.Copy, ["Aa0"], ["Aaw"])
-            act(T.tab[:, K + 1:K + 2], T.Aa[:, 0:1], ACT.Copy, ["Aa0"], ["tab0"])
-
-        if t == 0:
-            ends()
-            rea(0)
-            rea(1)
-            more_constants()
-            act(T.H[:, 0:8], T.Aa[:, 0:8], ACT.Copy, ["Aa0"], ["Hz"], scale=0.0)
-            reb(0)
-            reb(1)
-            for a, b, k in ((0, 1, "tabz0"), (1025, 1033, "tabz1"), (2058, 2064, "tabz2")):
-                act(T.tab[:, a:b], T.Aa[:, 0:b - a], ACT.Copy, ["Aa0"], [k], scale=0.0)
-            weights()
-        else:
-            act(T.Aa[:, 0:512], Pb[ab[0]][:], ACT.Copy, ["P%d" % ab[0]], ["Aa0"])
-            act(T.Aa[:, 512:1024], Pb[ab[1]][:], ACT.Copy, ["P%d" % ab[1]], ["Aa1"])
-            rea(0)
-            ends()
-            reb(0)
-            rea(1)
-        pa, pb = T.pd[:, 128 * t:128 * t + 64], T.pd[:, 128 * t + 64:128 * t + 128]
-        cp(pa, T.P3[:, 0:64], ["P3"], ["pda"])
-        tt(pb, T.P3[:, 0:64], pa, ALU.subtract, ["P3", "pda"], ["pdb"])
-        cp(T.od[:], T.P3[:, 128:256], ["P3"], ["od"])
-        before("G", ["pda", "pdb"], [])
-        send(t, 0)
-        lastw["pl%d" % t] = ("pa%d" % t, arrivals(T, topo, (rank + 1 + t % (n - 1)) % n, t, 0, 1))
-        part = [(0, 64), (64, 128), (128, 256)]
-
-        def w_mm(c):
-            a, b = part[c]
-            mm([(Pb[2 + c % 2][:, 0:b - a], T.Sw[:, 16 - i:144 - i], T.winF[:, 16 * a + i:16 * b:16], i == 0, i == 15)
-                for i in range(16)], ["Sw", "winF"], ["P%d" % (2 + c % 2)])
-
-        def h_scan(c):
-            a, b = part[c]
-            scan(T.H[:, 8 + a:8 + b], Pb[2 + c % 2][:, 0:b - a], T.zb[:, 0:b - a], T.H[:, 7 + a:8 + a],
-                 ["P%d" % (2 + c % 2), "zb", "H%d" % (c - 1) if c else "Hz"], ["H%d" % c])
-
-        def i_mm(c):
-            a, b = part[c]
-            o = Pb[2 + c % 2][:, 256:256 + b - a]
-            h1, h0 = T.H[:, 8 + a:8 + b], T.H[:, 7 + a:7 + b]
-            mm([(o, T.M1[:], h1, True, False), (o, T.KI[:], h1, False, False), (o, T.M2[:], h0, False, True)],
-               ["M1", "KI", "M2", "H%d" % c, "H%d" % (c - 1) if c else "Hz"], ["P%d" % (2 + c % 2)])
-
-        def i_cp(c):
-            a, b = part[c]
-            cp(T.idx[:, a:b], Pb[2 + c % 2][:, 256:256 + b - a], ["P%d" % (2 + c % 2)], ["idx%d" % c])
-
-        def da(h):
-            a, b = hs[h]
-            k = 1 - h
-            mm([(Pb[k][:], Ib, T.Aa[:, a + 1:b + 1], True, False), (Pb[k][:], T.nW[:, 0:128], T.Aa[:, a:b], False, True)],
-               ["Wb0", "nI", "Aa0", "Aa1"] + (["Aaw"] if h else []), ["P%d" % k])
-
-        def slope(h):
-            a, b = hs[h]
-            tt(T.tab[:, 1 + a:1 + b], Pb[1 - h][:], T.RE[:, a:b], ALU.mult, ["P%d" % (1 - h), "REa%d" % h], ["tabs%d" % h])
-
-        def jump(h):
-            a, b = hs[h]
-            tt(T.tab[:, K + 2 + a:K + 2 + b], Pb[1 - h][:], T.RE[:, 1024 + a:1024 + b], ALU.mult, ["P%d" % (1 - h), "REb%d" % h],
-               ["tabj%d" % h])
-
-        if t == 0:
-            da(0)
-            da(1)
-            w_mm(0)
-            w_mm(1)
-            slope(0)
-            h_scan(0)
-            i_mm(0)
-            slope(1)
-            jump(0)
-            i_cp(0)
-            h_scan(1)
-            i_mm(1)
-            w_mm(2)
-            jump(1)
-        else:
-            da(0)
-            w_mm(0)
-            da(1)
-            reb(1)
-            slope(0)
-            h_scan(0)
-            i_mm(0)
-            w_mm(1)
-            jump(0)
-            i_cp(0)
-            w_mm(2)
-            slope(1)
-            h_scan(1)
-            i_mm(1)
-            jump(1)
-            h_scan(2)
-            i_mm(2)
-        i_cp(1)
-        if t < NB - 1:
-            dma("Y", [(T.Ar[16:128, :], T.Aa[0:112, 0:1024]), (T.Ar[0:16, :], T.Aa[112:128, 0:1024])], ["Aa0", "Aa1"], ["Ar"])
-
-        def p_window():
-            dma("Y", [(T.Pwin[0:128:16, :], T.pl[:, 128 * t:128 * t + 64]), (T.Pwin[1:128:16, :], T.pl[:, 128 * t + 64:128 * t + 128])],
-                ["pl%d" % t], ["Pwin"])
-
-        if t > 0:
-            p_window()
-        tabr = ["tabz0", "tabz1", "tabz2", "tab0", "tabs0", "tabs1", "tabj0", "tabj1"]
-
-        def delta(c, q="S"):
-            o = T.dlt[:, 1024 * (c % 3):1024 * (c % 3) + 1024]
-            i = T.tab[:, 0:2064].indirect(T.idx[:, 64 * c:64 * c + 64])
-            if q == "S":
-                act(o, i, ACT.Identity, tabr + ["idx%d" % min(c, 2)], ["dlt%d" % (c % 3)])
-            else:
-                cp(o, i, tabr + ["idx%d" % min(c, 2)], ["dlt%d" % (c % 3)])
-
-        def y_scan(c):
-            init = 0.0 if c == 0 else T.Y[:, 1024 * c - 1:1024 * c]
-            scan(T.Y[:, 1024 * c:1024 * c + 1024], T.dlt[:, 1024 * (c % 3):1024 * (c % 3) + 1024], T.zb[:], init,
-                 ["dlt%d" % (c % 3), "zb"] + (["Y%d" % (c - 1)] if c else []), ["Y%d" % c])
-            before("G", ["Y%d" % c], [])
-            send(t, c + 1)
-
-        def move_y(c0, c1):
-            z = Zs[t]
-            a, b = 1024 * c0, 1024 * c1
-            dma("Y", [(z[16:128, a:b], T.Y[0:112, a:b]), (z[0:16, a:b], T.Y[112:128, a:b])],
-                ["Y%d" % c for c in range(c0, c1)] + (["xsent"] if t < NB - 1 else []),
-                [zk[t] % c for c in range(2 * c0, 2 * c1)] + (["X1"] if t == NB - 1 and c0 == 0 else []))
-
-        o1, d1 = T.od[:, 0:64], T.od[:, 64:128]
-
-        def lists_a():
-            ts(T.lv[:], o1, float(S), None, ALU.is_lt, None, ["od"], ["lv"])
-            ts(T.t1[:], d1, 0.5, 0.5, ALU.is_equal, ALU.subtract, ["od"], ["t1"])
-            ts(T.sof[:], o1, float(S), None, ALU.min, None, ["od"], ["sof"])
-            tt(T.t2[:], T.t1[:], T.lv[:], ALU.mult, ["t1", "lv"], ["t2"])
-            tt(T.t3[:], T.lv[:], T.bi[:], ALU.mult, ["lv", "bi"], ["t3"])
-
-        def lists_b(k):
-            if k == 0:
-                ts(T.t1[:], d1, 4.4, 99.0, ALU.is_ge, ALU.mult, ["od"], ["t1"])
-                ts(T.lv[:], T.t2[:], 200.0, 108.5, ALU.mult, ALU.add, ["t2"], ["lv"])
-            else:
-                tt(T.dn[:, 0:64], d1, T.t2[:], ALU.add, ["od", "t2"], ["dn"])
-                cp(T.jl[:], T.t3[:], ["t3"], ["jl"])
-                tt(T.thr[:], T.t1[:], T.lv[:], ALU.max, ["t1", "lv"], ["thr"])
-
-        def durations(q, h):
-            a, b = hs[h]
-            i = T.dtab[:, 0:16].indirect(T.dls[:, 32 * h:32 * h + 32])
-            if q == "S":
-                act(T.Dg[:, a:b], i, ACT.Identity, ["dtab", "dlsa"], ["Dg%d" % h])
-            else:
-                cp(T.Dg[:, a:b], i, ["dtab", "dlsa"], ["Dg%d" % h])
-
-        def e_source():
-            act(T.srcE[:], T.Pwin[:, 0:1024].indirect(T.ml[:, 64 * t:64 * t + 64]), ACT.Identity, ["Pwin", "ml"], ["srcE"])
-            dma("Y", [(T.srcE[3:128:16, 1:1024], T.srcE[0:128:16, 0:1023]), (T.srcE[4:128:16, 1:1024], T.srcE[1:128:16, 0:1023]),
-                      (T.srcE[18:128:16, 1:1024], T.Dg[0:112:16, 0:1023]), (T.srcE[2:3, 1:1024], T.Dg[112:113, 0:1023])],
-                ["Dg0", "Dg1"], ["srcE"])
-
-        def e_scatter():
-            cp(T.winE[:, 0:WIN].indirect(T.eof[:]), T.srcE[:], ["eof", "srcE"], ["winE"])
-
-        def v_move(h):
-            a, b = hs[h]
-            mm([(Pb[h][:], rotb, T.gg[:, a:b], True, False), (Pb[h][:], rotb, T.uw[:, 16 + a:16 + b], False, False),
-                (Pb[h][:], T.nW[:, 112:240], T.vL[:, a:b], False, True)],
-               ["Wb0", "Wb1", "nI", "nW1", "gg%d" % h, "uw%d" % h, "vL"], ["P%d" % h])
-
-        def v_keep(h):
-            a, b = hs[h]
-            act(T.uw[:, 16 + a:16 + b], Pb[h][:], ACT.Identity, ["P%d" % h], ["uw%d" % h], bias=-192.0)
-
-        def v_live():
-            act(T.vL[:], T.uw[:, 0:1040].indirect(T.jl[:]), ACT.Identity, ["uw0", "uw1", "uwz", "jl"], ["vL"], bias=-192.0)
-            for h, (a, b) in enumerate(hs):
-                mm([(Pb[h][:], Ib, T.vL[:, a:b], True, False)], ["Wb0", "vL"], ["P%d" % h])
-
         last = t == NB - 1
-        if t == 0:
+        p, o = t - 1, t - 2
+        if t > 0:
+            close_y(0)
+            close_y(1)
+            cut_v(0)
+            close_x(0)
+            open_x(1)
+            cut_v(1)
+            close_x(1)
+            scatter_f(t)
+            if t > 1:
+                e_w(p)
+            else:
+                e_scatter(p)
+            rate(t, 0)
+            rate(t, 1)
+            mirror(0)
+            down_a(0)
+            mirror(1)
+            if not last:
+                send_a(t)
+                vote_lists(t, -1)
+            ends()
+            levels(0)
+            w_mm(0)
+            if t > 1:
+                z(o, 0, 1)
+            e_digits(t, 0)
+            if t > 1:
+                e_s()
+            e_digits(t, 1)
+            h_scan(0)
+            e_digits(t, 2)
+            down_a(1)
+            da(0)
+            levels(1)
+            da(1)
+            i_mm(0)
+            if t > 1:
+                z(o, 1, 1)
+            i_cp(0)
+            w_mm(1)
+            slope(0)
+            slope(1)
+            durations(t)
             delta(0)
-            late_a()
-            p_window()
-            delta(1)
-            h_scan(2)
-            i_mm(2)
-            late_b()
-            y_scan(0)
-            i_cp(2)
-            delta(2)
-            late_b2()
-            y_scan(1)
-            delta(3)
-            late_c()
-            y_scan(2)
-            lists_a()
-            y_scan(3)
+            if t > 1:
+                z(o, 2, 1)
+            h_scan(1)
+            i_mm(1)
+            if t > 1:
+                e_c()
+            else:
+                e_w(p)
         else:
-            if last:
-                durations("S", 0)
+            da(0)
+            da(1)
+            w_mm(0)
+            slope(0)
+            h_scan(0)
+            i_mm(0)
+            w_mm(1)
+            slope(1)
+            i_cp(0)
+            late_s()
             delta(0)
-            e_w(t - 1, 0)
-            e_w(t - 1, 1)
-            cp(T.eof[:], o1, ["od"], ["eof"])
-            i_cp(2)
-            if last:
-                durations("V", 1)
-            else:
-                lists_a()
-            delta(1)
-            y_scan(0)
-            e_s(t - 1, 0)
-            e_c(t - 1, 0)
-            if not last:
-                lists_b(0)
-            delta(2)
-            y_scan(1)
-            delta(3)
-            e_s(t - 1, 1)
-            e_c(t - 1, 1)
-            e_v(t - 1, 0, 0)
-            if last:
-                move_y(0, 2)
-            else:
-                lists_b(1)
-            y_scan(2)
-            for h, k in ((0, 1), (1, 0), (0, 2), (1, 1)):
-                e_v(t - 1, h, k)
-            y_scan(3)
-            if not last:
-                v_move(0)
-                v_move(1)
-            if t >= 2:
-                for c in range(4):
-                    out_mm(t - 2, c)
-            if last:
-                move_y(2, 4)
-        if not last:
-            dma("Y", [(T.winF[0:128:16, 0:S], T.zb[:, 0:256])], ["zb"], ["winF", "winFa"])
-        for c in range(4):
-            readers["Y%d" % c].append(("xl%d" % t, dcount["xl%d" % t]))
-        lastw["xsent"] = ("xl%d" % t, dcount["xl%d" % t])
+            vote_lists(t, -1)
+            late_v(0)
+            h_scan(1)
+            i_mm(1)
+            late_v(1)
+        if 0 < t < NB - 1:
+            vote_lists(t, 0)
+        i_cp(1)
+        delta(1)
+        if t > 2:
+            out_mm(t - 3, 0, 4)
+        y_scan(t, 0)
+        delta(2)
         if t == 0:
-            cp(T.eof[:], o1, ["od"], ["eof"])
-            durations("V", 0)
-            durations("V", 1)
-            e_source()
-            lists_b(0)
-            lists_b(1)
-            late_d()
-            v_live()
-            e_scatter()
+            for step in range(3):
+                e_digits(t, step)
+            vote_lists(t, 0)
+        elif t == 1:
+            e_s()
+            e_c()
         else:
-            if not last:
-                durations("S", 0)
-                durations("S", 1)
-            e_source()
-            z_chunk(t - 1, 0, 2)
-            e_v(t - 1, 1, 2)
-            if not last:
-                v_keep(0)
-                v_keep(1)
-            tanh_chunk(t - 1, 0, 2)
-            z_chunk(t - 1, 4, 2)
-            tanh_chunk(t - 1, 4, 6)
-            fold(t - 1, 0, 2)
-            if last:
-                e_scatter()
-                e_w(t, 0)
-                e_w(t, 1)
-            else:
-                v_live()
-            if last:
-                z_chunk(t - 1, 2)
-                tanh_chunk(t - 1, 2, 3)
-                z_chunk(t - 1, 6)
-                tanh_chunk(t - 1, 6, 7)
-                fold(t - 1, 2, 3)
-                e_s(t, 0)
-                e_c(t, 0)
-                z_chunk(t - 1, 3)
-                tanh_chunk(t - 1, 3, 4)
-                e_s(t, 1)
-                e_c(t, 1)
-                out_mm(t - 1, 0)
-                out_mm(t - 1, 1)
-                e_v(t, 0, 0)
-                z_chunk(t - 1, 7)
-                tanh_chunk(t - 1, 7, 8)
-                fold(t - 1, 3, 4)
-            else:
-                z_chunk(t - 1, 2, 2)
-                tanh_chunk(t - 1, 2, 4)
-                z_chunk(t - 1, 6, 2)
-                tanh_chunk(t - 1, 6, 8)
-                fold(t - 1, 2, 4)
-            if not last:
-                e_scatter()
+            z(o, 3, 1)
+        if 0 < t < NB - 1:
+            vote_lists(t, 1)
+        y_scan(t, 1)
+        delta(3)
+        if t > 0:
+            e_v(p, 0)
+            e_v(p, 1)
         if not last:
-            move_y(0, 4)
-
-    t = NB - 1
-    for h, k in ((1, 0), (0, 1), (1, 1), (0, 2), (1, 2)):
-        e_v(t, h, k)
-    out_mm(t - 1, 2)
-    out_mm(t - 1, 3)
-    arrived(t)
-    z = Zs[t]
-
-    def pair(p):
-        z_chunk(t, p)
-        act(Pb[p % 2][:], z[:, 512 * p:512 * p + 512], ACT.Tanh, [zk[t] % p], ["P%d" % (p % 2)], scale=2.0 ** -14)
-        z_chunk(t, p + 4)
-        tanh_chunk(t, p + 4, p + 5)
-
-    def finish(p):
-        zz = z[:, 512 * (p + 4):512 * (p + 5)]
-        tt(zz, Pb[p % 2][:], zz, ALU.add, ["P%d" % (p % 2), zk[t] % (p + 4)], [zk[t] % (p + 4)])
-        out_mm(t, p, p + 4)
-
-    def store(p):
-        act(T.Z0[:, 512 * p:512 * p + 512], T["acc%d" % p][:], ACT.Copy, ["acc%d" % p], ["Z0_%d" % p])
-        dma("Y", [(T.yo[:, 512 * p:512 * p + 512], T.Z0[:, 512 * p:512 * p + 512])], ["Z0_%d" % p], ["yo%d" % p])
-
-    z_chunk(t, 0)
-    tanh_chunk(t, 0, 1)
-    z_chunk(t, 4)
-    tanh_chunk(t, 4, 5)
-    fold(t, 0, 1)
-    pair(1)
-    pair(2)
-    finish(1)
-    out_mm(t, 0)
-    pair(3)
-    finish(2)
-    store(1)
-    store(0)
-    finish(3)
-    store(2)
-    store(3)
+            if t == 0:
+                vote_lists(t, 1)
+            vote_lists(t, 2)
+            dead_list(t, 0)
+        if t > 1:
+            z(o, 4)
+        if t == 0:
+            durations(t)
+        else:
+            e_source()
+        y_scan(t, 2)
+        if not last:
+            vote_lists(t, 3)
+        if t > 1:
+            z(o, 6)
+            tanh(o, 0)
+            tanh(o, 4)
+            tanh(o, 2)
+        y_scan(t, 3)
+        if not last:
+            votes(t)
+            if t == 0:
+                ms(T.winF[:, 0:S], 1.0, wk)
+                act(T.ob[:, 128:B], T.zb[:, 128:B], ACT.Identity, ["zb", "ob0"], ["ob"], bias=1.0)
+                remote(plan(T, topo)["first"][rank, 1, 2][0], T.winF[:, 0:B], T.ob[:], "oa", "ml", ["ob"])
+            dead_v()
+            open_y(0)
+            open_y(1)
+            open_x(0)
+            if t == 0:
+                e_source()
+                gains()
+            if t > 1:
+                tanh(o, 6)
+                fold(o, 0)
+                fold(o, 2)
+            if t > 0:
+                e_scatter(t, min(t - 1, 1), 2)
+    e_v(p, 2)
+    fold(o, 0)
+    tanh(o, 6)
+    out_mm(o, 2)
+    out_mm(o, 6)
+    z(p, 0)
+    z(p, 4)
+    e_scatter(t)
+    e_w(t)
+    tanh(p, 0)
+    tanh(p, 4)
+    fold(p, 0)
+    z(p, 2)
+    e_s()
+    e_c()
+    tanh(p, 2)
+    e_v(t, 0)
+    e_v(t, 1)
+    out_mm(o, 0)
+    z(p, 6)
+    e_v(t, 2)
+    tanh(p, 6)
+    fold(p, 2)
+    scale(p, 0)
+    scale(p, 1)
+    for c in range(4):
+        summed[c] += 1
+    for c in range(4):
+        for j in (c, c + 4):
+            z(t, j, 1)
+            tanh(t, j, 1)
+            out_mm(t, j, 1)
+        if c == 2:
+            scale(p, 2)
+    scale(p, 3)
+    for c in range(4):
+        store(c, p)
     for s in dcount:
         wait("G", (s, dcount[s]))
     for q in cnt:

from concourse.bass import DstId, RemoteDMATransfer
from concourse.mybir import AluOpType, ActivationFunctionType

ALU = AluOpType
ACT = ActivationFunctionType
S, B, NB, L = 4096, 1024, 4, 2048
WIN = 9248
K = 1032
MW, MS = 130, 136

SCRATCH = {
    "X0": ("sbuf", [128, 4096], "float32"), "X1": ("sbuf", [128, 4096], "float32"), "X2": ("sbuf", [128, 4096], "float32"),
    "Y0": ("sbuf", [128, 4104], "float32"), "Y1": ("sbuf", [128, 4104], "float32"),
    "Z0": ("sbuf", [128, 4096], "float32"), "Z1": ("sbuf", [128, 4096], "float32"), "Z2": ("sbuf", [128, 4096], "float32"),
    "dlt": ("sbuf", [128, 3072], "float32"), "tab": ("sbuf", [128, 2064], "float32"),
    "winF": ("sbuf", [128, WIN], "bfloat16"), "winE": ("sbuf", [128, WIN], "bfloat16"),
    "Aa": ("sbuf", [128, 1040], "bfloat16"), "Al": ("sbuf", [128, 3072], "bfloat16"),
    "uw": ("sbuf", [128, 1040], "bfloat16"), "Fb": ("sbuf", [128, 1024], "bfloat16"), "Fl": ("sbuf", [128, 1024], "bfloat16"),
    "vD": ("sbuf", [128, 1024], "bfloat16"), "cmpb": ("sbuf", [128, 1024], "bfloat16"), "RE": ("sbuf", [128, 1024], "bfloat16"),
    "srcE": ("sbuf", [128, 1024], "bfloat16"), "Dg": ("sbuf", [128, 1024], "bfloat16"),
    "zb": ("sbuf", [128, 1040], "bfloat16"), "ob": ("sbuf", [128, 1024], "bfloat16"), "c101": ("sbuf", [128, 256], "bfloat16"),
    "Pwin": ("sbuf", [128, 1024], "bfloat16"), "pd": ("sbuf", [128, 128], "bfloat16"), "qb": ("sbuf", [128, 256], "bfloat16"),
    "dui": ("sbuf", [128, 64], "int32"), "mpi": ("sbuf", [128, 64], "int32"), "gn": ("sbuf", [128, 8], "float32"),
    "ia": ("sbuf", [128, 128], "int32"),
    "Mb": ("sbuf", [128, 14 * MS], "uint16"), "Mq": ("sbuf", [128, 64], "uint16"), "Mr": ("sbuf", [128, 64], "uint16"),
    "up": ("sbuf", [128, 68], "float32"), "df": ("sbuf", [128, 68], "float32"), "lv": ("sbuf", [128, 68], "float32"),
    "a2": ("sbuf", [128, 68], "float32"), "Dh": ("sbuf", [128, 68], "float32"), "four": ("sbuf", [128, 68], "float32"),
    "dd": ("sbuf", [128, 64], "float32"), "sq": ("sbuf", [128, 64], "float32"), "bn": ("sbuf", [128, 64], "float32"),
    "t1": ("sbuf", [128, 64], "float32"), "t2": ("sbuf", [128, 64], "float32"), "pf": ("sbuf", [128, 64], "float32"),
    "bi": ("sbuf", [128, 64], "float32"),
    "sof": ("sbuf", [128, 64], "uint16"), "jl": ("sbuf", [128, 64], "uint16"), "idx": ("sbuf", [128, 256], "uint16"),
    "el0": ("sbuf", [128, 256], "uint16"), "el1": ("sbuf", [128, 256], "uint16"), "ml": ("sbuf", [128, 64], "uint16"),
    "H": ("sbuf", [128, 264], "bfloat16"), "HE": ("sbuf", [128, 260], "float32"),
    "coef": ("sbuf", [128, 16], "float32"), "dtab": ("sbuf", [128, 16], "float32"), "sm": ("sbuf", [128, 32], "float32"),
    "smi": ("sbuf", [128, 16], "int32"),
    "one": ("sbuf", [128, 128], "float32"), "B1": ("sbuf", [128, 128], "float32"),
    "U1": ("sbuf", [128, 128], "float32"), "U2": ("sbuf", [128, 128], "float32"),
    "Wf": ("sbuf", [128, 144], "float32"), "Wb": ("sbuf", [128, 144], "bfloat16"), "nIf": ("sbuf", [128, 128], "float32"),
    "nI": ("sbuf", [128, 144], "bfloat16"), "n192": ("sbuf", [128, 128], "bfloat16"), "n4096": ("sbuf", [128, 128], "bfloat16"),
    "KI": ("sbuf", [128, 128], "bfloat16"), "M1": ("sbuf", [128, 128], "bfloat16"), "M2": ("sbuf", [128, 128], "bfloat16"),
    "Tle": ("sbuf", [128, 128], "float32"), "Tgt": ("sbuf", [128, 128], "float32"),
    "Sw": ("sbuf", [128, 144], "bfloat16"), "SE": ("sbuf", [128, 160], "bfloat16"), "Vw": ("sbuf", [128, 144], "bfloat16"),
    "Gm": ("sbuf", [128, 512], "float32"),
    "acc0": ("psum", [128, 512], "float32"), "acc1": ("psum", [128, 512], "float32"),
    "acc2": ("psum", [128, 512], "float32"), "acc3": ("psum", [128, 512], "float32"),
    "P0": ("psum", [128, 512], "float32"), "P1": ("psum", [128, 512], "float32"),
    "P2": ("psum", [128, 512], "float32"), "P3": ("psum", [128, 512], "float32"),
}
NQ = 60
SEMAPHORES = (["cV", "cS", "cP", "cG", "ml", "fl", "al", "hl", "oa"] + ["q%d" % i for i in range(NQ)]
              + ["xa%d" % t for t in range(NB)] + ["xl%d" % t for t in range(NB)] + ["wa%d" % t for t in range(1, NB - 1)]
              + ["ma%d" % i for i in range(4 * NB - 3)] + ["fa%d" % t for t in range(NB - 1)] + ["aa%d" % t for t in range(NB - 1)]
              + ["ya%d" % c for c in range(4)] + ["h%d" % i for i in range(4 * NB)] + ["k%d" % i for i in range(4 * NB)])
SIM_CORES = 256
STOPS = ["X0", "X1", "X2", "Y0", "Y1", "Z0", "Z1", "Z2"]
LAST = (NB - 1, 3)
PLAN = {}


def bits(m):
    return bin(m).count("1")


def reader(n, r, t):
    return (r - 1 - t % (n - 1)) % n


def partner(n, r, t):
    return (r + 1 + t % (n - 1)) % n


def crosses(topo, c):
    return any(topo.mates(c, x) and topo.may_write(c, x) for x in range(SIM_CORES))


def ways(T, topo, r, t):
    n = len(T.cores)
    src, dst = T.cores[r], T.cores[reader(n, r, t)]
    free = [c for c in topo.cores_of(src) if T.rank_of(c) is None]
    h0, h1 = [c for c in free if topo.die(c) == topo.die(src) and not crosses(topo, c)]
    gate = [c for c in free if topo.die(c) == topo.die(src) and crosses(topo, c)][0]
    if dst in topo.cores_of(src):
        return [[h1, dst], [gate, dst], [h0, dst], [h0, dst]]
    other = [c for c in free if topo.die(c) != topo.die(src) and not crosses(topo, c)][1]
    far = [c for c in range(SIM_CORES) if topo.mates(c, dst) and topo.die(c) == topo.die(src) and topo.may_write(c, dst)][0]
    peer = [T.rank_of(c) for c in topo.cores_of(src) if c != src and T.rank_of(c) is not None][0]
    if T.cores[reader(n, peer, t)] not in topo.cores_of(src):
        return [[gate, far, dst], [h0, dst], [h0, dst], [h0, dst]]
    if t == NB - 1:
        across = [c for c in free if topo.die(c) != topo.die(src) and crosses(topo, c)][0]
        return [[across, dst], [h0, dst], [other, dst], [h0, dst]]
    return [[h1, other, dst], [gate, other, dst], [h0, dst], [h0, dst]]


def plan(T, topo):
    if not PLAN:
        allways, first, jobs, used = {}, {}, {}, {}

        def stop(c):
            m = used.get(c, 0)
            used[c] = m + 2
            return STOPS[m // 4], B * (m % 4)

        for t in range(NB):
            for r in range(len(T.cores)):
                allways[r, t] = ways(T, topo, r, t)
                for c, way in enumerate(allways[r, t]):
                    at = stop(way[0])
                    first[r, t, c] = (way[0],) + at
                    for j in range(len(way) - 1):
                        last = j + 2 == len(way)
                        to = ("X%d" % (t % 3), B * c) if last else stop(way[j + 1])
                        jobs.setdefault(way[j], []).append((t, j, c, r, way[j - 1] if j else T.cores[r], at, way[j + 1], to, last))
                        at = to
        for c in jobs:
            jobs[c].sort()
        PLAN.update(ways=allways, first=first, jobs=jobs)
    return PLAN


def small_mask(T, topo, src):
    return [topo.mask(src, c) for c in T.cores if c not in topo.cores_of(src)][0]


def first_mask(T, topo, r, t, c):
    m = topo.mask(T.cores[r], plan(T, topo)["first"][r, t, c][0])
    return m & ~small_mask(T, topo, T.cores[r]) if c == 3 or c == 0 and t < NB - 1 else m


def arrivals(T, topo, r, t):
    w = plan(T, topo)["ways"][r, t]
    return sum(bits(small_mask(T, topo, T.cores[r]) if (t, c) == LAST else topo.mask(w[c][-2], w[c][-1])) for c in range(4))


def helper_program(g, core, T, topo):
    jobs = plan(T, topo)["jobs"].get(core, [])
    sent, held = [0], []

    def write(dst, o, i, sem):
        rid, pid = topo.addr(dst, core)
        if dst not in topo.cores_of(core) and sent[0]:
            g.wait_ge(T.sem.hl, sent[0])
        g.remote_dma(o, i, T.sem[sem], T.sem.hl, pid, rid, topo.mask(core, dst))
        sent[0] += bits(topo.mask(core, dst))

    resets = [job for job in jobs if job[1] == 0 and job[2] == 2 and 0 < job[0] < NB - 1]
    if resets:
        g.sync.wait_ge(T.sem.oa, bits(small_mask(T, topo, resets[0][4])))
        for j in (1, 2):
            g.sync.dma_start(T.winF[:, B * j:B * j + B], T.winF[:, 0:B]).then_inc(T.sem.q0, 16)
        g.wait_ge(T.sem.q0, 32)
    for num, (t, j, c, r, src, at, nxt, to, last) in enumerate(jobs):
        buf, col = T[at[0]], at[1]
        sem = "xa%d" % t if last else "k%d" % (4 * t + c)
        if j == 0:
            came, count = T.sem["h%d" % (4 * t + c)], bits(first_mask(T, topo, r, t, c))
            turned = T.sem["q%d" % (num + 1)]
            g.sync.wait_ge(came, count)
            cut = 112 if t < NB - 1 else 16
            raw, col = col, col + B
            g.sync.dma_start(buf[0:cut, col:col + B], buf[128 - cut:128, raw:raw + B]).then_inc(turned, 16)
            g.sync.dma_start(buf[cut:128, col:col + B], buf[0:128 - cut, raw:raw + B]).then_inc(turned, 16)
            if t == NB - 1:
                if (t, c) != LAST:
                    g.wait_ge(came, count)
                    write(nxt, T[to[0]][:, to[1]:to[1] + B], buf[:, raw:raw + B], sem)
                g.wait_ge(turned, 32)
                write(src, T.Z2[:, B * c:B * c + B], buf[:, col:col + B], "ya%d" % c)
                continue
            if c == 2 and t > 0:
                g.wait_ge(came, count)
                write(src, T.winF[:, 0:3 * B], T.winF[:, 0:3 * B], "wa%d" % t)
            ready = (turned, 32)
        else:
            ready = (T.sem["k%d" % (4 * t + c)], bits(topo.mask(src, core)))
        held.append((ready, nxt, T[to[0]][:, to[1]:to[1] + B], buf[:, col:col + B], sem))
        if c < 3 and j == 0 and last and nxt not in topo.cores_of(core):
            continue
        g.wait_ge(*ready)
        while held:
            g.wait_ge(*held[0][0])
            write(*held.pop(0)[1:])
    if sent[0]:
        g.wait_ge(T.sem.hl, sent[0])


def rank_program(g, core, T, topo):
    rank = T.rank_of(core)
    if rank is None:
        helper_program(g, core, T, topo)
        return
    n = len(T.cores)
    eng = {"V": g.vector, "S": g.scalar, "P": g.tensor, "G": g, "Y": g.sync}
    cnt = {"V": 0, "S": 0, "P": 0, "G": 0}
    known = {q: {} for q in eng}
    lastw, readers = {}, {}
    small = small_mask(T, topo, core)
    nq = [0]
    dcount = {}
    banks = ("P0", "P1", "P2", "P3", "acc0", "acc1", "acc2", "acc3")

    def wait(q, tok):
        s, v = tok
        if known[q].get(s, 0) < v:
            eng[q].wait_ge(T.sem[s], v)
            known[q][s] = v

    def before(q, r, w, skip=None):
        toks = [lastw[k] for k in r + w if k in lastw]
        for k in w:
            toks.extend(readers.get(k, []))
        best = {}
        for s, v in toks:
            if s != skip:
                best[s] = max(best.get(s, 0), v)
        for s in best:
            wait(q, (s, best[s]))

    def after(tok, r, w):
        for k in r:
            readers.setdefault(k, []).append(tok)
        for k in w:
            lastw[k] = tok
            readers[k] = []

    def op(q, fn, r, w):
        for k in r:
            if k in banks:
                for tok in readers.get(k, []):
                    if tok[0] != "c" + q:
                        wait(q, tok)
        before(q, r, w)
        cnt[q] += 1
        fn().then_inc(T.sem["c" + q], 1)
        after(("c" + q, cnt[q]), r, w)

    def mm(calls, r, w):
        before("P", r, w, skip="cP")
        ins = None
        for o, a, b, st, sp in calls:
            ins = g.tensor.matmul(o, a, b, st, sp)
        cnt["P"] += 1
        ins.then_inc(T.sem.cP, 1)
        after(("cP", cnt["P"]), r, w)

    def dma(q, pairs, r, w, **kw):
        before(q, r, w)
        s = "q%d" % nq[0]
        nq[0] += 1
        for o, i in pairs:
            eng[q].dma_start(o, i, **kw).then_inc(T.sem[s], 16)
        dcount[s] = 16 * len(pairs)
        after((s, dcount[s]), r, w)

    def remote(dst, o, i, sem, loc, r):
        before("G", r, [])
        rid, pid = topo.addr(dst, core)
        g.remote_dma(o, i, T.sem[sem], T.sem[loc], pid, rid, small)
        dcount[loc] = dcount.get(loc, 0) + bits(small)
        after((loc, dcount[loc]), r, [])

    def lands(key, sem):
        lastw[key] = (sem, bits(small))
        dcount[sem] = lastw[key][1]

    def ts(o, i, s1, s2, o0, o1, r, w):
        if s2 is None:
            op("V", lambda: g.vector.tensor_scalar(o, i, s1, None, o0), r, w)
        else:
            op("V", lambda: g.vector.tensor_scalar(o, i, s1, s2, o0, o1), r, w)

    def tt(o, a, b, o0, r, w):
        op("V", lambda: g.vector.tensor_tensor(o, a, b, o0), r, w)

    def cp(o, i, r, w):
        op("V", lambda: g.vector.tensor_copy(o, i), r, w)

    def ms(o, c, w):
        op("V", lambda: g.vector.memset(o, c), [], w)

    def scan(o, a, b, init, r, w, o0=ALU.add):
        op("V", lambda: g.vector.tensor_tensor_scan(o, a, b, init, o0, ALU.add), r, w)

    def act(o, i, f, r, w, bias=0.0, scale=1.0):
        op("S", lambda: g.scalar.activation(o, i, f, bias=bias, scale=scale), r, w)

    def sel(o, i, pat, cmp, fill, base, cm, r, w):
        op("G", lambda: g.affine_select(o, i, pat, cmp, fill, base, cm), r, w)

    def iota(o, pat, base, cm, w, f=True):
        if f:
            op("G", lambda: g.iota(o, pat, base, cm, allow_small_or_imprecise_dtypes=True), [], w)
        else:
            op("G", lambda: g.iota(o, pat, base, cm), [], w)

    def up_one(o, i):
        return [(o(16, 128), i(0, 112)), (o(0, 16), i(112, 128))]

    If, Ib, downb = T.Wf[:, 0:128], T.Wb[:, 0:128], T.Wb[:, 16:144]
    hs = [(0, 512), (512, 1024)]
    Ys, Zs, Xs = [T.Y0, T.Y1], [T.Z0, T.Z1, T.Z0, T.Z2], [T.X0, T.X1, T.X2]
    zn = ["Z0", "Z1", "Z0", "Z2"]
    els = [T.el0, T.el1]
    Pb = [T.P0, T.P1, T.P2, T.P3]
    xb = [2, 0]
    db = [2, 1]
    part = [(0, 128, 3), (128, 256, 0)]
    wk = ["winF%d" % c for c in range(4)]

    def yk(t, c):
        return "Y%d_%d" % (t % 2, c)

    def zk(t, c):
        return "%s_%d" % (zn[t], c)

    def msg(t, k, a=0, b=MW, p0=0, p1=128):
        c = MS * (4 * t + k)
        return T.Mb[p0:p1, c + a:c + b]

    def mkey(t, k):
        return ["M%d_%do" % (t, k), "M%d_%dd" % (t, k)]

    def made(t):
        return 0 if t == 0 else reader(n, 0, t - 1)

    def needed(t):
        ks = [0, partner(n, 0, t)] + ([reader(n, 0, t)] if t < NB - 1 else [])
        return [k for j, k in enumerate(ks) if k not in ks[:j]]

    def send_lists(t):
        mine = (rank + made(t)) % n
        for k in needed(t):
            if t > 0 and k == needed(t)[1]:
                send_y(t - 1, 3)
            if k != made(t):
                remote(T.cores[(mine - k) % n], msg(t, k), msg(t, made(t)), "ma%d" % (4 * t + k), "ml", mkey(t, made(t)))
                for key in mkey(t, k):
                    lands(key, "ma%d" % (4 * t + k))

    def send_y(t, c):
        before("G", [yk(t, c)], [])
        h, buf, col = plan(T, topo)["first"][rank, t, c]
        rid, pid = topo.addr(h, core)
        m = first_mask(T, topo, rank, t, c)
        y = Ys[t % 2][:, B * c:B * c + B]
        if (t, c) == LAST:
            rid2, pid2 = topo.addr(T.cores[reader(n, rank, t)], core)
            g.remote_dma_fused([RemoteDMATransfer(dst_ids=[DstId(rid=rid2, pnc=pid2)], dma_engine_mask=small, remote_sem=T.sem["xa%d" % t],
                                                  src=y, dst=Xs[t % 3][:, B * c:B * c + B]),
                                RemoteDMATransfer(dst_ids=[DstId(rid=rid, pnc=pid)], dma_engine_mask=m, remote_sem=T.sem["h%d" % (4 * t + c)],
                                                  src=y, dst=T[buf][:, col:col + B])], local_sem=T.sem["xl%d" % t])
            m |= small
        else:
            g.remote_dma(T[buf][:, col:col + B], y, T.sem["h%d" % (4 * t + c)], T.sem["xl%d" % t], pid, rid, m)
        dcount["xl%d" % t] = dcount.get("xl%d" % t, 0) + bits(m)
        if t == NB - 1:
            for j in (2 * c, 2 * c + 1):
                lastw[zk(t, j)] = ("ya%d" % c, bits(topo.mask(h, core)))
        elif c == 2 and t > 0:
            dcount["wa%d" % t] = bits(topo.mask(h, core))
            for k in wk[:3]:
                lastw[k] = ("wa%d" % t, dcount["wa%d" % t])
                readers[k] = []
        if c == 3:
            for j in range(4):
                readers[yk(t, j)].append(("xl%d" % t, dcount["xl%d" % t]))
            lastw["X%d" % (t % 3)] = ("xa%d" % t, arrivals(T, topo, partner(n, rank, t), t))
            readers["X%d" % (t % 3)] = []

    def onsets(t):
        k = made(t)
        calls = [(T.P3[:, 0:66], T.U1[:], T.Dh[:, 1:67], True, False), (T.P3[:, 0:66], T.U2[:], T.Dh[:, 0:66], False, True)]
        if t == 0:
            mm(calls, ["U1", "U2", "Dh", "Dh0"], ["P3"])
            cp(msg(t, k, 0, 66), T.P3[:, 0:66], ["P3"], [mkey(t, k)[0]])
        else:
            calls += [(T.P3[:, 66:MW], If, T.Dh[:, 1:65], True, False), (T.P3[:, 66:MW], T.nIf[:], T.Dh[:, 0:64], False, True)]
            mm(calls, ["U1", "U2", "Wf", "nIf", "Dh", "Dh0"], ["P3"])
            cp(msg(t, k), T.P3[:, 0:MW], ["P3"], mkey(t, k))

    def vote_lists(t, step):
        k = reader(n, 0, t)
        ko, kd = mkey(t, k)
        if step == -1:
            dma("Y", up_one(lambda a, b: T.Mq[a:b, :], lambda a, b: msg(t, k, 0, 64, a, b))
                + up_one(lambda a, b: T.Mr[a:b, :], lambda a, b: msg(t, 0, 0, 64, a, b)), [ko, mkey(t, 0)[0]], ["Mq", "Mr"])
        elif step == 0:
            ts(T.lv[:, 0:64], msg(t, k, 0, 64), float(S), 4.0, ALU.is_lt, ALU.mult, [ko], ["lv"])
            cp(T.df[:, 0:64], msg(t, k, 66, MW), [kd], ["df"])
        elif step == 1:
            tt(T.dd[:], T.df[:, 0:64], T.lv[:, 0:64], ALU.mult, ["df", "lv"], ["dd"])
            act(T.sq[:], T.dd[:], ACT.Abs, ["dd"], ["sq"], bias=-5.0, scale=0.25)
            act(T.a2[:, 0:64], T.dd[:], ACT.Relu, ["dd"], ["a2"], bias=5.0, scale=-0.75)
            act(T.bn[:], T.sq[:], ACT.Sign, ["sq"], ["bn"], bias=3.5, scale=-1.0)
        elif step == 2:
            ts(T.sof[:], T.Mq[:], float(S), None, ALU.min, None, ["Mq"], ["sof"])
        else:
            o = T.P3[:, 64:130]
            mm([(o, If, T.df[:, 0:66], True, False), (o, If, T.a2[:, 0:66], False, False), (o, If, T.lv[:, 0:66], False, False),
                (o, T.nIf[:], T.four[:, 0:66], False, True),
                (T.P3[:, 0:64], If, T.bn[:], True, False)], ["Wf", "nIf", "df", "a2", "lv", "bn", "x66"], ["P3"])

    def votes(t):
        yw = Ys[t % 2][:, 0:S + 8]
        yr = [yk(t, c) for c in range(4)] + ["Yz", "sof"]
        for h, (a, b) in enumerate(hs):
            o = T.sof[:, 32 * h:32 * h + 32]
            tt(T.cmpb[:, a:b], yw.indirect(o), T.Al[:, B * t + a:B * t + b], ALU.is_gt, yr + ["Al%d" % t], ["cmp%d" % h])
            act(T.Fb[:, a:b], yw.indirect(o), ACT.Identity, yr, ["Fb%d" % h], bias=191.5 + 2.0 ** -13, scale=2.0 ** -4)
            mm([(T.P3[:, 32 * h:32 * h + 32], T.Vw[:, 16 - i:144 - i], T.cmpb[:, a + i:b:16], False, h == 1 and i == 15) for i in range(16)],
               ["Vw", "cmp%d" % h], ["P3"])
        before("G", ["Al%d" % t], [])
        remote(T.cores[reader(n, rank, t)], T.Fl[:], T.Fb[:], "fa%d" % t, "fl", ["Fb0", "Fb1"])
        lands("Fl", "fa%d" % t)
        dead_list(t, 1)
        if t > 0:
            e_v(t - 1, 2)
        if t > 1:
            e_scatter(t, 0, 1)
        act(T.up[:, 0:64], T.P3[:, 0:64], ACT.Sign, ["P3"], ["up"], bias=-1.0 - 8.5 / 32)
        scan(T.Dh[:, 1:67], T.up[:, 0:66], T.P3[:, 64:130], 0.0, ["up", "x66", "P3"], ["Dh"])
        onsets(t + 1)
        send_lists(t + 1)

    def dead_list(t, step):
        if step == 0:
            ts(T.t1[:], T.Mr[:], float(S), -2048.0, ALU.is_lt, ALU.mult, ["Mr"], ["t1"])
            o = T.P0[:, 0:64]
            mm([(o, If, T.t1[:], True, False), (o, If, T.bi[:], False, True)], ["Wf", "t1", "bi"], ["P0"])
        else:
            cp(T.jl[:], T.P0[:, 0:64], ["P0"], ["jl"])

    def dead_v():
        act(T.vD[:], T.uw[:, 0:1040].indirect(T.jl[:]), ACT.Identity, ["uw0", "uw1", "uwz", "jl"], ["vD"])

    def open_y(h):
        a, b = hs[h]
        mm([(Pb[h][:], Ib, T.uw[:, 16 + a:16 + b], True, False), (Pb[h][:], T.n192[:], T.ob[:, 0:512], False, False)],
           ["Wb", "n192", "ob", "uw%d" % h], ["P%d" % h])

    def open_x(h):
        a, b = hs[h]
        o = Pb[xb[h]][:]
        mm([(o, Ib, T.Aa[:, a:b], True, False), (o, T.nI[:, 0:128], T.vD[:, a:b], False, False)],
           ["Wb", "nI", "Aa%d" % h, "vD"], ["P%d" % xb[h]])

    def close_y(h):
        a, b = hs[h]
        mm([(Pb[h][:], Ib, T.Fl[:, a:b], False, True)], ["Wb", "Fl"], ["P%d" % h])

    def cut_v(h):
        a, b = hs[h]
        ts(T.uw[:, 16 + a:16 + b], Pb[h][:], -64.0, 64.0, ALU.max, ALU.min, ["P%d" % h], ["uw%d" % h])

    def close_x(h):
        a, b = hs[h]
        mm([(Pb[xb[h]][:], Ib, T.uw[:, 16 + a:16 + b], False, True)], ["Wb", "uw%d" % h], ["P%d" % xb[h]])

    def mirror(h):
        a, b = hs[h]
        w = T.dlt[:, 2048 + a:2048 + b]
        act(w, Pb[xb[h]][:], ACT.Abs, ["P%d" % xb[h]], ["w%d" % h] + (["dlt2"] if h == 0 else []), bias=256.0)
        act(w, w, ACT.Abs, ["w%d" % h], ["w%d" % h], bias=512.0, scale=-1.0)
        act(T.Aa[:, a:b], w, ACT.Identity, ["w%d" % h], ["Aa%d" % h], bias=256.0, scale=-1.0)

    def send_a(t):
        remote(T.cores[partner(n, rank, t)], T.Al[:, B * t:B * t + B], T.Aa[:, 0:B], "aa%d" % t, "al", ["Aa0", "Aa1"])
        lands("Al%d" % t, "aa%d" % t)

    def ends():
        act(T.Aa[:, 1024:1025], T.Aa[:, 0:1], ACT.Copy, ["Aa0"], ["Aaw"])

    def down_a(h):
        a, b = hs[h]
        mm([(Pb[1 - h][:], downb, T.Aa[:, a:b], True, True)], ["Wb", "Aa%d" % h], ["P%d" % (1 - h)])

    def levels(h):
        a, b = hs[h]
        act(T.tab[:, K + 1 + a:K + 1 + b], Pb[1 - h][:], ACT.Copy, ["P%d" % (1 - h), "w0", "w1"], ["tabA%d" % h] + (["dlt2"] if h else []))
        if h == 0:
            act(T.tab[:, K + 1025:K + 1026], T.P1[:, 0:1], ACT.Copy, ["P1"], ["tabA2"])

    def rate(t, h):
        a, b = hs[h]
        act(T.RE[:, a:b], T.coef[:, 0:16].indirect(msg(t, 0, 66 + 32 * h, 98 + 32 * h)), ACT.Identity, ["coef", mkey(t, 0)[1]], ["RE%d" % h])

    def da(h):
        a, b = hs[h]
        o = Pb[db[h]][:]
        mm([(o, downb, T.Aa[:, a + 1:b + 1], True, False), (o, T.nI[:, 16:144], T.Aa[:, a:b], False, True)],
           ["Wb", "nI", "Aa0", "Aa1"] + (["Aaw"] if h else []), ["P%d" % db[h]])

    def slope(h):
        a, b = hs[h]
        tt(T.tab[:, 1 + a:1 + b], Pb[db[h]][:], T.RE[:, a:b], ALU.mult, ["P%d" % db[h], "RE%d" % h], ["tabs%d" % h])

    def scatter_f(t):
        cp(T.winF[:, 0:WIN].indirect(msg(t, 0, 0, 65)), T.zb[:, 0:1040], [mkey(t, 0)[0], "zb", "zbx"], wk)

    def w_mm(c):
        a, b, k = part[c]
        mm([(Pb[k][:, 0:b - a], T.Sw[:, 16 - i:144 - i], T.winF[:, 16 * a + i:16 * b:16], i == 0, i == 15) for i in range(16)],
           ["Sw"] + wk, ["P%d" % k])

    def h_scan(c):
        a, b, k = part[c]
        scan(T.H[:, 8 + a:8 + b], Pb[k][:, 0:b - a], T.ob[:, 0:b - a], T.H[:, 7 + a:8 + a],
             ["P%d" % k, "ob0", "H%d" % (c - 1) if c else "Hz"], ["H%d" % c])

    def i_mm(c):
        a, b, k = part[c]
        o = Pb[k][:, b - a:2 * (b - a)]
        h1, h0 = T.H[:, 8 + a:8 + b], T.H[:, 7 + a:7 + b]
        mm([(o, T.M1[:], h1, True, False), (o, T.KI[:], h1, False, False), (o, T.M2[:], h0, False, True)],
           ["M1", "KI", "M2", "H%d" % c, "H%d" % (c - 1) if c else "Hz"], ["P%d" % k])

    def i_cp(c):
        a, b, k = part[c]
        cp(T.idx[:, a:b], Pb[k][:, b - a:2 * (b - a)], ["P%d" % k], ["idx%d" % c])

    def delta(c):
        act(T.dlt[:, B * (c % 3):B * (c % 3) + B], T.tab[:, 0:2064].indirect(T.idx[:, 64 * c:64 * c + 64]), ACT.Identity,
            ["tabz", "tabA0", "tabA1", "tabA2", "tabs0", "tabs1", "idx%d" % (c // 2)], ["dlt%d" % (c % 3)])

    def y_scan(t, c):
        a, b = B * c, B * c + B
        y = Ys[t % 2]
        init = 0.0 if c == 0 else y[:, a - 1:a]
        scan(y[:, a:b], T.winF[:, a:b], T.dlt[:, B * (c % 3):B * (c % 3) + B], init,
             ["dlt%d" % (c % 3), wk[c]] + ([yk(t, c - 1)] if c else []), [yk(t, c)], ALU.mult)
        if c < 3 or t == NB - 1:
            send_y(t, c)
        elif t > 0:
            dma("Y", [(T.winF[:, a:b], T.ob[:])], ["ob"], [wk[c]])

    def e_digits(t, step):
        k = partner(n, 0, t)
        if step == 0:
            cp(T.pf[:], msg(t, k, 0, 64), [mkey(t, k)[0]], ["pf"])
        elif step == 1:
            cp(T.pd[:, 0:64], T.pf[:], ["pf"], ["pda"])
        else:
            tt(T.pd[:, 64:128], T.pf[:], T.pd[:, 0:64], ALU.subtract, ["pf", "pda"], ["pdb"])
            dma("Y", [pair for r in range(2) for pair in ((T.Pwin[r:112:16, :], T.pd[16:128, 64 * r:64 * r + 64]),
                                                          (T.Pwin[112 + r:113 + r, :], T.pd[0:16, 64 * r:64 * r + 64]))],
                ["pda", "pdb"], ["Pwin"])

    def durations(t):
        act(T.Dg[:], T.dtab[:, 0:16].indirect(msg(t, 0, 66, MW)), ACT.Identity, ["dtab", mkey(t, 0)[1]], ["Dg"])

    def e_source():
        act(T.srcE[:], T.Pwin[:, 0:1024].indirect(T.ml[:]), ACT.Identity, ["Pwin", "ml"], ["srcE"])
        dma("Y", [(T.srcE[3:128:16, 1:1024], T.srcE[0:128:16, 0:1023]), (T.srcE[4:128:16, 1:1024], T.srcE[1:128:16, 0:1023]),
                  (T.srcE[2:128:16, 1:1024], T.Dg[0:128:16, 0:1023])], ["Dg"], ["srcE"])

    def e_scatter(t, h0=0, h1=2):
        cp(T.winE[:, 0:WIN].indirect(msg(t, 0, 32 * h0, 32 * h1)), T.srcE[:, 512 * h0:512 * h1], [mkey(t, 0)[0], "srcE"], ["winE"])

    def e_w(t):
        s = 32 if t < NB - 1 else 16
        mm([(T.P3[:, 256:512], T.SE[:, s - i:s + 128 - i], T.winE[:, i:S:16], i == 0, i == 15) for i in range(16)], ["SE", "winE"], ["P3"])
        if t < NB - 1:
            dma("Y", [(T.winE[r:128:16, 0:S], T.winE[8 + r:128:16, 0:S]) for r in range(5)], [], ["winE"])

    def e_s():
        scan(T.HE[:, 1:257], T.P3[:, 256:512], T.c101[:], T.HE[:, 0:1], ["P3", "c101", "HE0"], ["HE"])

    def e_c():
        for k in (1, 2):
            o = Pb[k][:, 0:256]
            mm([(o, T.Tle[:], T.HE[:, 1:257], True, False), (o, T.Tgt[:], T.HE[:, 0:256], False, k == 1)], ["Tle", "Tgt", "HE", "HE0"],
               ["P%d" % k])

    def e_v(t, k):
        if k == 0:
            act(T.qb[:], T.P1[:, 0:256], ACT.Identity, ["P1"], ["qb"], bias=-0.5 + 2.0 ** -13, scale=2.0 ** -12)
        elif k == 1:
            mm([(T.P2[:, 0:256], T.n4096[:], T.qb[:], False, True)], ["n4096", "qb"], ["P2"])
        else:
            cp(els[t % 2][:], T.P2[:, 0:256], ["P2"], ["el%d" % (t % 2)])

    def z(t, c, w=2):
        y, key = (Ys[t % 2], yk(t, c // 2)) if t < NB - 1 else (Zs[t], zk(t, c))
        tt(Zs[t][:, 512 * c:512 * (c + w)], Xs[t % 3][:, 0:S].indirect(els[t % 2][:, 32 * c:32 * (c + w)]), y[:, 512 * c:512 * (c + w)],
           ALU.mult, ["X%d" % (t % 3), "el%d" % (t % 2), key], [zk(t, j) for j in range(c, c + w)])

    def tanh(t, c, w=2):
        o = Zs[t][:, 512 * c:512 * (c + w)]
        ks = [zk(t, j) for j in range(c, c + w)]
        act(o, o, ACT.Tanh, ks, ks, scale=2.0 ** -14)

    summed = [0] * 4

    def fold(t, c, w=2):
        o = Zs[t]
        a, b = 512 * c, 512 * (c + w)
        dma("G", [(o[:, a:b], o[:, L + a:L + b])], [zk(t, j + 4) for j in range(c, c + w)], [zk(t, j) for j in range(c, c + w)],
            accum_op=ALU.add)
        for j in range(c, c + w):
            summed[j] += 1

    def out_mm(t, c, w=2):
        for j in range(c, c + w):
            summed[j % 4] += 1
            k = "acc%d" % (j % 4)
            mm([(T[k][:], T.Gm[:, 128 * t:128 * t + 128], Zs[t][:, 512 * j:512 * j + 512], k not in lastw, summed[j % 4] == 2 * NB)],
               ["Gm%d" % t, zk(t, j)], [k])

    def scale(t, c):
        o = Zs[t][:, 512 * c:512 * c + 512]
        act(o, o, ACT.Copy, [zk(t, c), "gn"], [zk(t, c)], scale=T.gn[:, t:t + 1])

    def store(c, more):
        o = T.Y0[:, 512 * c:512 * c + 512]
        tt(o, T["acc%d" % c][:], Zs[more][:, 512 * c:512 * c + 512], ALU.add, ["acc%d" % c, zk(more, c)], ["out%d" % c, yk(0, c // 2)])
        dma("Y", [(T.yo[:, 512 * c:512 * c + 512], o)], ["out%d" % c], ["yo%d" % c])

    dma("Y", [(T.dui[:], T.du[:])], [], ["dui"])
    dma("S", up_one(lambda a, b: T.Aa[a:b, 0:B], lambda a, b: T.am[a:b, :]), [], ["Aa0", "Aa1"])
    dma("Y", [(T.mpi[:], T.mp[:]), (T.gn[:, 0:4], T.gain[:])] + up_one(lambda a, b: T.uw[a:b, 16:1040], lambda a, b: T.ve[a:b, :])
        + up_one(lambda a, b: T.gn[a:b, 4:8], lambda a, b: T.gain[a:b, :]), [], ["mpi", "gn", "uw0", "uw1"])
    ms(T.one[:], 1.0, ["one"])
    iota(T.dtab[:], [[1, 16]], 0, 0, ["dtab"])
    ms(T.winF[:, 0:B], 1.0, wk[:1])
    sel(T.B1[:], T.one[:], [[-16, 8], [0, 16]], ALU.is_ge, 0.0, 0, 1, ["one"], ["B1"])
    sel(T.B1[:], T.B1[:], [[16, 8], [0, 16]], ALU.is_ge, 0.0, 15, -1, ["B1"], ["B1"])
    sel(T.U1[:], T.B1[:], [[1, 128]], ALU.is_gt, 0.0, 0, -1, ["B1"], ["U1"])
    sel(T.U2[:], T.B1[:], [[-1, 128]], ALU.is_ge, 0.0, 0, 1, ["B1"], ["U2"])
    act(T.ob[:, 0:128], T.winF[:, 0:128], ACT.Tanh, wk[:1], ["ob0"], scale=16.0)
    act(T.zb[:, 0:B], T.winF[:, 0:B], ACT.Copy, wk[:1], ["zb"], scale=0.0)
    op("V", lambda: g.vector.reciprocal(T.sm[:, 0:9], T.dtab[:, 1:10]), ["dtab"], ["sma"])
    ms(T.zb[:, 1024:1040], 1.0, ["zbx"])
    ms(T.coef[:], 0.0, ["coef"])
    ts(T.sm[:, 16:25], T.sm[:, 0:9], 256.0, -0.49, ALU.mult, ALU.add, ["sma"], ["smb"])
    ms(T.up[:], 0.0, ["up", "x66"])
    ms(T.zb[:, 1025:1026], 0.0, ["zbx"])
    cp(T.smi[:, 4:13], T.sm[:, 16:25], ["smb"], ["smi2"])
    ms(T.df[:, 64:66], 1.0, ["x66"])
    ms(T.Dh[:, 0:1], 0.0, ["Dh0"])
    ts(T.coef[:, 1:10], T.smi[:, 4:13], 1.0 / 256, None, ALU.mult, None, ["smi2"], ["coef"])
    ms(T.Sw[:], 0.0, ["Sw"])
    ms(T.winF[:, B:2 * B], 1.0, wk[1:2])
    cp(T.df[:, 0:64], T.dui[:], ["dui"], ["df"])
    cp(msg(0, 0, 66, MW), T.dui[:], ["dui"], [mkey(0, 0)[1]])
    scan(T.Dh[:, 1:67], T.up[:, 0:66], T.df[:, 0:66], 0.0, ["up", "x66", "df"], ["Dh"])
    ms(T.winF[:, 2 * B:4 * B], 1.0, wk[2:])
    sel(If, T.one[:], [[-1, 128]], ALU.is_equal, 0.0, 0, 1, ["one"], ["Wf"])
    sel(T.Sw[:, 16:144:16], T.Sw[:, 16:144:16], [[-16, 8]], ALU.not_equal, -1.0, 0, 1, ["Sw"], ["Sw"])
    sel(T.Tle[:], T.B1[:], [[1, 128]], ALU.is_ge, 0.0, 0, -1, ["B1"], ["Tle"])
    sel(T.Tgt[:], T.B1[:], [[-1, 128]], ALU.is_gt, 0.0, 0, 1, ["B1"], ["Tgt"])
    sel(T.one[:], T.Tgt[:], [[-1, 128]], ALU.not_equal, -1.0 * K, 0, 1, ["Tgt"], ["one"])
    onsets(0)
    scatter_f(0)
    send_lists(0)
    send_a(0)
    ends()
    rate(0, 0)
    act(T.Wf[:, 128:144], T.Wf[:, 0:16], ACT.Copy, ["Wf"], ["Wf1"])
    act(T.Wb[:], T.Wf[:], ACT.Copy, ["Wf", "Wf1"], ["Wb"])
    act(T.nI[:], T.Wf[:], ACT.Copy, ["Wf", "Wf1"], ["nI"], scale=-1.0)
    down_a(0)
    down_a(1)
    rate(0, 1)
    levels(0)
    levels(1)
    act(T.KI[:], If, ACT.Copy, ["Wf"], ["KI"], scale=float(K))
    act(T.M1[:], T.Tle[:], ACT.Copy, ["Tle"], ["M1"])
    act(T.M2[:], T.one[:], ACT.Copy, ["one"], ["M2"])
    act(T.H[:, 0:8], T.Aa[:, 0:8], ACT.Copy, ["Aa0"], ["Hz"], scale=0.0)
    for a, b in ((0, 1), (1025, K + 1), (K + 1026, 2064)):
        act(T.tab[:, a:b], T.Aa[:, 0:b - a], ACT.Copy, ["Aa0"], ["tabz"], scale=0.0)
    dma("Y", [(T.Pwin[:], T.zb[:, 0:B])] + [(T.winE[:, B * j:B * j + B], T.zb[:, 0:B]) for j in range(4)], ["zb"], ["Pwin", "winE"])
    iota(T.smi[:, 0:1], [[1, 1]], 0, 1, ["smi0"], f=False)
    iota(T.bi[:], [[16, 64]], 16, 0, ["bi"])
    sel(T.SE[:], T.zb[:, 0:160], [[0, 160]], ALU.is_gt, 0.0, 0, 0, ["zb"], ["SE"])
    for r, w in ((0, 1.0), (1, 1.0), (2, -101.0), (3, -1.0), (4, -1.0)):
        sel(T.SE[:, 32:160:16], T.SE[:, 32:160:16], [[-16, 8]], ALU.not_equal, w, -r, 1, ["SE"], ["SE"])

    def late_s():
        act(T.nIf[:], If, ACT.Copy, ["Wf"], ["nIf"], scale=-1.0)
        act(T.n192[:], If, ACT.Copy, ["Wf"], ["n192"], scale=-192.0)
        act(T.Vw[:], T.Sw[:], ACT.Copy, ["Sw"], ["Vw"], scale=0.0)
        act(T.Vw[:, 16:128:16], T.B1[:, 16:128:16], ACT.Copy, ["B1"], ["Vw"], scale=1.0 / 32)
        act(T.Vw[:, 128:129], T.B1[:, 0:1], ACT.Copy, ["B1"], ["Vw"], scale=1.0 / 32)

    def gains():
        act(T.n4096[:], If, ACT.Copy, ["Wf"], ["n4096"], scale=-float(S))
        act(T.SE[:, 16:17], T.SE[:, 144:145], ACT.Copy, ["SE"], ["SE"])
        for t in range(NB):
            s = 16 * (t == NB - 1)
            act(T.Gm[:, 128 * t:128 * t + 128], T.Wf[:, s:s + 128], ACT.Copy, ["Wf", "Wf1", "gn"], ["Gm%d" % t],
                scale=T.gn[:, t + s // 4:t + s // 4 + 1])

    def late_v(step):
        if step == 0:
            ms(T.lv[:, 64:66], 4.0, ["x66"])
            ms(T.four[:], 4.0, ["x66"])
            ms(T.a2[:, 64:66], 0.0, ["x66"])
            ms(T.Y0[:, S:S + 8], 0.0, ["Yz"])
            ms(T.Y1[:, S:S + 8], 0.0, ["Yz"])
            ms(T.uw[:, 0:16], 0.0, ["uwz"])
            ts(T.smi[:, 1:2], T.smi[:, 0:1], 15, None, ALU.bitwise_and, None, ["smi0"], ["smi1"])
            ts(T.ia[:, 64:128], T.mpi[:], 15, None, ALU.bitwise_and, None, ["mpi"], ["ia1"])
            ts(T.ia[:, 0:64], T.mpi[:], 4, None, ALU.arith_shift_right, None, ["mpi"], ["ia0"])
            cp(T.sm[:, 30:31], T.smi[:, 1:2], ["smi1"], ["pm"])
        else:
            ts(T.t1[:], T.ia[:, 64:128], 64.0, None, ALU.mult, None, ["ia1"], ["t1"])
            ts(T.bi[:], T.bi[:], T.sm[:, 30:31], None, ALU.add, None, ["bi", "pm"], ["bi"])
            tt(T.t2[:], T.t1[:], T.ia[:, 0:64], ALU.add, ["t1", "ia0"], ["t2"])
            ms(T.c101[:], 101.0, ["c101"])
            cp(T.ml[:], T.t2[:], ["t2"], ["ml"])
            ts(T.HE[:, 0:1], T.sm[:, 30:31], 0.0, 136.0 * S - 101.0, ALU.is_equal, ALU.mult, ["pm"], ["HE0"])

    for t in range(NB):
        last = t == NB - 1
        p, o = t - 1, t - 2
        if t > 0:
            close_y(0)
            close_y(1)
            cut_v(0)
            close_x(0)
            open_x(1)
            cut_v(1)
            close_x(1)
            scatter_f(t)
            if t > 1:
                e_w(p)
            else:
                e_scatter(p)
            rate(t, 0)
            rate(t, 1)
            mirror(0)
            down_a(0)
            mirror(1)
            if not last:
                send_a(t)
                vote_lists(t, -1)
            ends()
            levels(0)
            w_mm(0)
            if t > 1:
                z(o, 0, 1)
            e_digits(t, 0)
            if t > 1:
                e_s()
            e_digits(t, 1)
            h_scan(0)
            e_digits(t, 2)
            down_a(1)
            da(0)
            levels(1)
            da(1)
            i_mm(0)
            if t > 1:
                z(o, 1, 1)
            i_cp(0)
            w_mm(1)
            slope(0)
            slope(1)
            durations(t)
            delta(0)
            if t > 1:
                z(o, 2, 1)
            h_scan(1)
            i_mm(1)
            if t > 1:
                e_c()
            else:
                e_w(p)
        else:
            da(0)
            da(1)
            w_mm(0)
            slope(0)
            h_scan(0)
            i_mm(0)
            w_mm(1)
            slope(1)
            i_cp(0)
            late_s()
            delta(0)
            vote_lists(t, -1)
            late_v(0)
            h_scan(1)
            i_mm(1)
            late_v(1)
        if 0 < t < NB - 1:
            vote_lists(t, 0)
        i_cp(1)
        delta(1)
        if t > 2:
            out_mm(t - 3, 0, 4)
        y_scan(t, 0)
        delta(2)
        if t == 0:
            for step in range(3):
                e_digits(t, step)
            vote_lists(t, 0)
        elif t == 1:
            e_s()
            e_c()
        else:
            z(o, 3, 1)
        if 0 < t < NB - 1:
            vote_lists(t, 1)
        y_scan(t, 1)
        delta(3)
        if t > 0:
            e_v(p, 0)
            e_v(p, 1)
        if not last:
            if t == 0:
                vote_lists(t, 1)
            vote_lists(t, 2)
            dead_list(t, 0)
        if t > 1:
            z(o, 4)
        if t == 0:
            durations(t)
        else:
            e_source()
        y_scan(t, 2)
        if not last:
            vote_lists(t, 3)
        if t > 1:
            z(o, 6)
            tanh(o, 0)
            tanh(o, 4)
            tanh(o, 2)
        y_scan(t, 3)
        if not last:
            votes(t)
            if t == 0:
                ms(T.winF[:, 0:S], 1.0, wk)
                act(T.ob[:, 128:B], T.zb[:, 128:B], ACT.Identity, ["zb", "ob0"], ["ob"], bias=1.0)
                remote(plan(T, topo)["first"][rank, 1, 2][0], T.winF[:, 0:B], T.ob[:], "oa", "ml", ["ob"])
            dead_v()
            open_y(0)
            open_y(1)
            open_x(0)
            if t == 0:
                e_source()
                gains()
            if t > 1:
                tanh(o, 6)
                fold(o, 0)
                fold(o, 2)
            if t > 0:
                e_scatter(t, min(t - 1, 1), 2)
    e_v(p, 2)
    fold(o, 0)
    tanh(o, 6)
    out_mm(o, 2)
    out_mm(o, 6)
    z(p, 0)
    z(p, 4)
    e_scatter(t)
    e_w(t)
    tanh(p, 0)
    tanh(p, 4)
    fold(p, 0)
    z(p, 2)
    e_s()
    e_c()
    tanh(p, 2)
    e_v(t, 0)
    e_v(t, 1)
    out_mm(o, 0)
    z(p, 6)
    e_v(t, 2)
    tanh(p, 6)
    fold(p, 2)
    scale(p, 0)
    scale(p, 1)
    for c in range(4):
        summed[c] += 1
    for c in range(4):
        for j in (c, c + 4):
            z(t, j, 1)
            tanh(t, j, 1)
            out_mm(t, j, 1)
        if c == 2:
            scale(p, 2)
    scale(p, 3)
    for c in range(4):
        store(c, p)
    for s in dcount:
        wait("G", (s, dcount[s]))
    for q in cnt:
        wait("G", ("c" + q, cnt[q]))
